import numpy as np
import ml_dtypes


def mxq(x, axis, fmt="e4m3"):
    dtype, down = {"e4m3": (ml_dtypes.float8_e4m3fn, 7), "e5m2": (ml_dtypes.float8_e5m2, 14)}[fmt]
    v = np.moveaxis(np.asarray(x, np.float32).astype(ml_dtypes.bfloat16).astype(np.float64), axis, -1)
    blocks = v.reshape(v.shape[:-1] + (-1, 32))
    amax = np.abs(blocks).max(-1, keepdims=True)
    byte = np.maximum(np.where(amax > 0, np.frexp(amax)[1] - 1 + 127, 0) - down, 1)
    scale = np.exp2(byte - 127.0)
    codes = (blocks / scale).astype(np.float32).astype(dtype).astype(np.float64)
    return np.moveaxis((codes * scale).reshape(v.shape), -1, axis)


WIDE = False


def mx_kscale(k):
    if not WIDE:
        return np.ones(k)
    levels = np.array([18, -18])
    if k % 512:
        return np.exp2(np.random.permutation(np.resize(levels, k // 32))).repeat(32)
    a = np.empty((k // 512, 16))
    for p in range(k // 512):
        a[p, :8] = np.random.permutation(np.resize(levels, 8))
        for g in range(8):
            far = levels[np.abs(levels - a[p, g]) >= 10]
            a[p, g + 8] = far[np.random.randint(len(far))]
    return np.exp2(a.ravel()).repeat(32)


def f64(x):
    return np.asarray(x).astype(np.float64)


def striped(idx):
    return np.tile(np.asarray(idx).reshape(-1, 16).T, (8, 1)).astype(np.uint16)


def unstriped(offs):
    return offs[:16].T.reshape(-1).astype(np.int64)


def sig(x):
    return 1.0 / (1.0 + np.exp(-x))


def setup_inputs():
    n = np.random.standard_normal
    uni = np.random.uniform
    order = np.random.permutation(2048)
    neg = order[:512]
    pos = order[512:1024]
    f_d = mx_kscale(512)
    f_r = mx_kscale(512)
    return {
        "x": (0.5 * n((512, 512)) * f_r[:, None] * f_d[None, :]).astype(np.float32),
        "wT": (n((512, 2048)) / np.sqrt(512) / f_d[:, None]).astype(np.float32),
        "us": (uni(0.75, 1.3, (512, 1)) / f_r[:, None]).astype(np.float32),
        "ts": np.tile(uni(0.75, 1.3, 2048), (128, 1)).astype(np.float32),
        "wt": (uni(0.75, 1.3, (512, 1))).astype(np.float32),
        "offs": striped(neg),
        "poffs": striped(pos),
    }


def reference(x, wT, us, ts, wt, offs, poffs):
    neg = unstriped(offs)
    pos = unstriped(poffs)
    wT_i = f64(wT)[:, neg]
    wT_r = f64(wT)[:, pos]
    ts_i = f64(ts)[:1][:, neg]
    ts_r = f64(ts)[:1][:, pos]
    tpc = ts_r.T
    wpr = wT_r.T
    s0 = (f64(x) * wpr).sum(-1, keepdims=True)
    sp = f64(us) * tpc * s0
    a = mxq(f64(x), 1, "e4m3") @ mxq(wT_i, 0, "e4m3")
    z = f64(us) * ts_i * a
    g = f64(wt) * f64(us) * ts_i * sig(z)
    gp = f64(wt) * f64(us) * tpc * (sig(sp) - 1.0)
    dn = mxq(f64(x), 0, "e4m3").T @ mxq(g, 0, "e5m2")
    g1 = np.zeros((512, 2048))
    g1[:, neg] = dn
    dp = gp * f64(x)
    dpT = dp.T
    g2 = np.zeros((512, 2048))
    g2[:, pos] = dpT
    out = g1 + g2
    return out

@@ -1,0 +1,196 @@
+from contextlib import ExitStack
+
+import concourse.mybir as mybir
+from concourse.masks import make_identity
+
+F32 = mybir.dt.float32
+BF16 = mybir.dt.bfloat16
+U32 = mybir.dt.uint32
+U16 = mybir.dt.uint16
+U8 = mybir.dt.uint8
+E4M3X4 = mybir.dt.float8_e4m3fn_x4
+E5M2X4 = mybir.dt.float8_e5m2_x4
+MULT = mybir.AluOpType.mult
+COPY = mybir.ActivationFunctionType.Copy
+SIGMOID = mybir.ActivationFunctionType.Sigmoid
+
+P = 128
+PACK = 4
+D = 512
+R = 512
+SLOTS = 512
+T = 2048
+
+FLOPS = 2 * R * D * SLOTS + 2 * D * R * SLOTS
+
+
+def tile_attend_gspos_ns_w_kernel(tc, x, wT, us, ts, wt, offs, poffs, out):
+    nc = tc.nc
+    with ExitStack() as ctx:
+        lists = ctx.enter_context(tc.tile_pool(name="lists", bufs=1))
+        sb = ctx.enter_context(tc.tile_pool(name="sb", bufs=1))
+        psum = ctx.enter_context(tc.psum_pool(name="psum", bufs=1))
+
+        def bank(n, name):
+            return psum.tile([P, PACK, P], F32, name=name, tag="bank%d" % n)
+
+        def quantize(name, grouped, fmt):
+            codes = sb.tile([P, 512], U32, name=name + "_codes", align_bytes=64)
+            scales = sb.tile([P, 512], U8, name=name + "_scales", align_bytes=64)
+            nc.vector.quantize_mx(out=codes[:].bitcast(fmt), scales=scales[:], in_=grouped[:])
+            return codes, scales
+
+        neg = lists.tile([P, SLOTS // 16], U16, name="neg")
+        pos = lists.tile([P, R // 16], U16, name="pos")
+        nc.sync.dma_start(pos[:], poffs)
+        nc.sync.dma_start(neg[:], offs)
+
+        ts_row = sb.tile([P, T], F32, name="ts_row")
+        nc.vector.memset(ts_row[:], 0.0)
+        us_col = sb.tile([P, PACK], F32, name="us_col")
+        wt_col = sb.tile([P, PACK], F32, name="wt_col")
+        nc.scalar.dma_start(out=us_col[:], in_=us.rearrange("(s j) o -> s (j o)", j=PACK))
+        nc.scalar.dma_start(out=wt_col[:], in_=wt.rearrange("(s j) o -> s (j o)", j=PACK))
+
+        w_planes = wT.rearrange("(p t) c -> t p c", t=PACK)
+        w = [sb.tile([P, T], F32, name="w%d" % t) for t in range(PACK)]
+        x_sb = sb.tile([P, PACK, D], F32, name="x_sb")
+        nc.sync.dma_start(out=x_sb[:], in_=x.rearrange("(s j) d -> s j d", j=PACK))
+        nc.sync.dma_start(out=ts_row[0:1, :], in_=ts[0:1, :])
+        for t in range(PACK):
+            nc.sync.dma_start(out=w[t][:], in_=w_planes[t])
+
+        ident = sb.tile([P, P], F32, name="ident")
+        make_identity(nc, ident[:])
+        window = [sb.tile([P, T], F32, name="window%d" % t) for t in range(PACK - 1)]
+        for tile in window:
+            nc.vector.memset(tile[:], 0.0)
+        window.append(window[0])
+
+        xT = sb.tile([P, PACK, R], F32, name="xT")
+        for t in range(PACK):
+            turned_x = bank(4 + t, "turned_x%d" % t)
+            for j in range(PACK):
+                nc.tensor.transpose(turned_x[:, j, :], x_sb[:, j, t:D:PACK], ident[:])
+            nc.scalar.copy(xT[:, t, :].rearrange("p (s j) -> p s j", j=PACK), turned_x[:].rearrange("p j s -> p s j"))
+
+        x_d = sb.tile([P, R * PACK], BF16, name="x_d", align_bytes=64)
+        x_d_view = x_d[:].rearrange("p (j s t) -> p s j t", j=PACK, t=PACK)
+        xT_view = xT[:].rearrange("p t (s j) -> p s j t", j=PACK)
+        for h in range(PACK):
+            part = slice(h * 32, (h + 1) * 32)
+            nc.scalar.copy(x_d_view[:, part], xT_view[:, part])
+
+        ts_pos_row = sb.tile([P, R], F32, name="ts_pos_row")
+        ts_neg_row = sb.tile([P, SLOTS], F32, name="ts_neg_row")
+        nc.vector.tensor_copy(ts_pos_row[:], ts_row[:].indirect(pos[:]))
+        nc.vector.tensor_copy(ts_neg_row[:], ts_row[:].indirect(neg[:]))
+        turned_pos = bank(7, "turned_pos")
+        turned_neg = bank(6, "turned_neg")
+        for j in range(PACK):
+            nc.tensor.transpose(turned_pos[:, j, :], ts_pos_row[:, j:R:PACK], ident[:])
+        for b in range(PACK):
+            nc.tensor.transpose(turned_neg[:, b, :], ts_neg_row[:, b * P:(b + 1) * P], ident[:])
+        ts_pos = sb.tile([P, PACK], F32, name="ts_pos")
+        ts_neg = sb.tile([P, PACK], F32, name="ts_neg")
+        nc.scalar.copy(ts_pos[:], turned_pos[:, :, 0])
+        nc.scalar.copy(ts_neg[:], turned_neg[:, :, 0])
+        ts_spread = bank(5, "ts_spread")
+        for b in range(PACK):
+            nc.tensor.transpose(ts_spread[:, b, :], ts_neg[:, b:b + 1].to_broadcast([P, P]), ident[:])
+        wu = sb.tile([P, PACK], F32, name="wu")
+        us_ts = sb.tile([P, PACK], F32, name="us_ts")
+        wu_ts = sb.tile([P, PACK], F32, name="wu_ts")
+        nc.gpsimd.tensor_tensor(wu[:], wt_col[:], us_col[:], MULT)
+        nc.gpsimd.tensor_tensor(us_ts[:], us_col[:], ts_pos[:], MULT)
+        nc.gpsimd.tensor_tensor(wu_ts[:], wu[:], ts_pos[:], MULT)
+        factor = sb.tile([P, P, PACK, PACK], F32, name="factor")
+        for j in range(PACK):
+            nc.scalar.activation(factor[:, :, j, :], ts_spread[:].rearrange("p b (c i) -> p (b c) i", i=PACK), COPY,
+                                 scale=wu[:, j:j + 1])
+
+        w_pos = sb.tile([P, PACK, R], F32, name="w_pos")
+        w_neg = sb.tile([P, PACK, SLOTS], BF16, name="w_neg", tag="first")
+        w_pos_rows = [bank(j, "w_pos_rows%d" % j) for j in range(PACK)]
+        for t in range(PACK):
+            nc.vector.tensor_copy(w_pos[:, t, :], w[t][:].indirect(pos[:]))
+            nc.vector.tensor_copy(w_neg[:, t, :], w[t][:].indirect(neg[:]))
+            for j in range(PACK):
+                nc.tensor.transpose(w_pos_rows[j][:, t, :], w_pos[:, t, j:R:PACK], ident[:])
+
+        sp = sb.tile([P, PACK], F32, name="sp")
+        sig_p = sb.tile([P, PACK], F32, name="sig_p")
+        gp_col = sb.tile([P, PACK], F32, name="gp_col")
+        products = sb.tile([P, P, PACK], F32, name="products")
+        gp_spread = bank(7, "gp_spread")
+        for j in range(PACK):
+            nc.vector.scalar_tensor_tensor(
+                out=products[:], in0=w_pos_rows[j][:].rearrange("p t m -> p m t"), scalar=us_ts[:, j:j + 1],
+                in1=x_sb[:, j, :].rearrange("p (m t) -> p m t", t=PACK), op0=MULT, op1=MULT, accum_out=sp[:, j:j + 1])
+            nc.scalar.activation(sig_p[:, j:j + 1], sp[:, j:j + 1], SIGMOID, scale=-1.0)
+            nc.scalar.activation(gp_col[:, j:j + 1], sig_p[:, j:j + 1], COPY, scale=wu_ts[:, j:j + 1])
+            nc.tensor.transpose(gp_spread[:, j, :], gp_col[:, j:j + 1].to_broadcast([P, P]), ident[:])
+
+        w_d = sb.tile([P, SLOTS * PACK], BF16, name="w_d", align_bytes=64)
+        w_d_view = w_d[:].rearrange("p (c i t) -> p c t i", i=PACK, t=PACK)
+        w_neg_view = w_neg[:].rearrange("p t (c i) -> p c t i", i=PACK)
+        for h in range(PACK):
+            part = slice(h * 32, (h + 1) * 32)
+            nc.scalar.copy(w_d_view[:, part], w_neg_view[:, part])
+        gp_row = sb.tile([P, R], F32, name="gp_row", tag="first")
+        nc.scalar.activation(gp_row[:].rearrange("p (s j) -> p s j", j=PACK), gp_spread[:].rearrange("p j s -> p s j"),
+                             COPY, scale=-1.0)
+        x_d_codes, x_d_scales = quantize("x_d", x_d, E4M3X4)
+        w_d_codes, w_d_scales = quantize("w_d", w_d, E4M3X4)
+
+        def scatter_positives(t, factor_row):
+            nc.vector.tensor_tensor(window[t][:].indirect(pos[:]), xT[:, t, :], factor_row[:], MULT)
+
+        for t in range(2):
+            scatter_positives(t, gp_row)
+
+        scaled = sb.tile([P, PACK, R], F32, name="scaled")
+        for b in range(PACK):
+            scores = bank(b, "scores%d" % b)
+            cols = slice(b * P, (b + 1) * P)
+            nc.tensor.matmul_mx(out=scores[:].rearrange("p j s -> p (j s)"),
+                                lhsT=w_d_codes[:, cols].bitcast(E4M3X4), lhsT_scale=w_d_scales[:, cols],
+                                rhs=x_d_codes[:].bitcast(E4M3X4), rhs_scale=x_d_scales[:], start=True, stop=True)
+            nc.scalar.activation(scaled[:, b, :], scores[:].rearrange("p j s -> p (j s)"), COPY, scale=ts_neg[:, b:b + 1])
+        sig = sb.tile([P, P, PACK, PACK], F32, name="sig", tag="last")
+        for j in range(PACK):
+            rows = bank((4, 5, 6, 0)[j], "score_rows%d" % j)
+            for b in range(PACK):
+                nc.tensor.transpose(rows[:, b, :], scaled[:, b, j * P:(j + 1) * P], ident[:])
+            nc.scalar.activation(sig[:, :, j, :], rows[:].rearrange("p b (c i) -> p (b c) i", i=PACK), SIGMOID,
+                                 scale=us_col[:, j:j + 1])
+
+        x_r = sb.tile([P, D * PACK], BF16, name="x_r", align_bytes=64)
+        x_r_view = x_r[:].rearrange("p (t m j) -> p m t j", t=PACK, j=PACK)
+        x_view = x_sb[:].rearrange("p j (m t) -> p m t j", t=PACK)
+        for h in range(PACK):
+            part = slice(h * 32, (h + 1) * 32)
+            nc.scalar.copy(x_r_view[:, part], x_view[:, part])
+        x_r_codes, x_r_scales = quantize("x_r", x_r, E4M3X4)
+
+        g = sb.tile([P, SLOTS * PACK], BF16, name="g", align_bytes=64)
+        nc.vector.tensor_tensor(g[:].rearrange("p (c i j) -> p c j i", i=PACK, j=PACK), sig[:], factor[:], MULT)
+        g_codes, g_scales = quantize("g", g, E5M2X4)
+        gp_row_last = sb.tile([P, R], F32, name="gp_row_last", tag="last")
+        nc.scalar.activation(gp_row_last[:].rearrange("p (s j) -> p s j", j=PACK), gp_spread[:].rearrange("p j s -> p s j"),
+                             COPY, scale=-1.0)
+        scatter_positives(2, gp_row_last)
+
+        dn = sb.tile([P, PACK, SLOTS], F32, name="dn")
+        out_planes = out.rearrange("(p t) c -> t p c", t=PACK)
+        for t in range(PACK):
+            sums = bank(1 + t, "sums%d" % t)
+            cols = slice(t * P, (t + 1) * P)
+            nc.tensor.matmul_mx(out=sums[:].rearrange("p j s -> p (j s)"),
+                                lhsT=x_r_codes[:, cols].bitcast(E4M3X4), lhsT_scale=x_r_scales[:, cols],
+                                rhs=g_codes[:].bitcast(E5M2X4), rhs_scale=g_scales[:], start=True, stop=True)
+            nc.scalar.copy(dn[:, t, :], sums[:].rearrange("p j s -> p (j s)"))
+            if t == PACK - 1:
+                scatter_positives(t, gp_row)
+            nc.vector.tensor_copy(window[t][:].indirect(neg[:]), dn[:, t, :])
+            nc.sync.dma_start(out=out_planes[t], in_=window[t][:])

@@ -34,9 +34,9 @@ def tile_attend_gspos_ns_w_kernel(tc, x, wT, us, ts, wt, offs, poffs, out):
         def bank(n, name):
             return psum.tile([P, PACK, P], F32, name=name, tag="bank%d" % n)
 
-        def quantize(name, grouped, fmt):
+        def quantize(name, grouped, fmt, scales_tag):
             codes = sb.tile([P, 512], U32, name=name + "_codes", align_bytes=64)
-            scales = sb.tile([P, 512], U8, name=name + "_scales", align_bytes=64)
+            scales = sb.tile([P, 512], U8, name=name + "_scales", tag=scales_tag, align_bytes=64)
             nc.vector.quantize_mx(out=codes[:].bitcast(fmt), scales=scales[:], in_=grouped[:])
             return codes, scales
 
@@ -119,16 +119,17 @@ def tile_attend_gspos_ns_w_kernel(tc, x, wT, us, ts, wt, offs, poffs, out):
                 nc.tensor.transpose(w_pos_rows[j][:, t, :], w_pos[:, t, j:R:PACK], ident[:])
 
         sp = sb.tile([P, PACK], F32, name="sp")
-        sig_p = sb.tile([P, PACK], F32, name="sig_p")
+        sig_p = sb.tile([P, PACK], F32, name="sig_p", tag="sig_p", align_bytes=64)
         gp_col = sb.tile([P, PACK], F32, name="gp_col")
-        products = sb.tile([P, P, PACK], F32, name="products")
+        products = sb.tile([P, P, PACK], F32, name="products", tag="products", align_bytes=64)
         gp_spread = bank(7, "gp_spread")
         for j in range(PACK):
             nc.vector.scalar_tensor_tensor(
                 out=products[:], in0=w_pos_rows[j][:].rearrange("p t m -> p m t"), scalar=us_ts[:, j:j + 1],
                 in1=x_sb[:, j, :].rearrange("p (m t) -> p m t", t=PACK), op0=MULT, op1=MULT, accum_out=sp[:, j:j + 1])
-            nc.scalar.activation(sig_p[:, j:j + 1], sp[:, j:j + 1], SIGMOID, scale=-1.0)
-            nc.scalar.activation(gp_col[:, j:j + 1], sig_p[:, j:j + 1], COPY, scale=wu_ts[:, j:j + 1])
+        nc.scalar.activation(sig_p[:], sp[:], SIGMOID, scale=-1.0)
+        nc.vector.tensor_tensor(gp_col[:], sig_p[:], wu_ts[:], MULT)
+        for j in range(PACK):
             nc.tensor.transpose(gp_spread[:, j, :], gp_col[:, j:j + 1].to_broadcast([P, P]), ident[:])
 
         w_d = sb.tile([P, SLOTS * PACK], BF16, name="w_d", align_bytes=64)
@@ -140,16 +141,19 @@ def tile_attend_gspos_ns_w_kernel(tc, x, wT, us, ts, wt, offs, poffs, out):
         gp_row = sb.tile([P, R], F32, name="gp_row", tag="first")
         nc.scalar.activation(gp_row[:].rearrange("p (s j) -> p s j", j=PACK), gp_spread[:].rearrange("p j s -> p s j"),
                              COPY, scale=-1.0)
-        x_d_codes, x_d_scales = quantize("x_d", x_d, E4M3X4)
-        w_d_codes, w_d_scales = quantize("w_d", w_d, E4M3X4)
+        x_d_codes, x_d_scales = quantize("x_d", x_d, E4M3X4, "products")
+        w_d_codes, w_d_scales = quantize("w_d", w_d, E4M3X4, "sig_p")
 
-        def scatter_positives(t, factor_row):
-            nc.vector.tensor_tensor(window[t][:].indirect(pos[:]), xT[:, t, :], factor_row[:], MULT)
+        def scatter_positives(t, rows, factor_row):
+            entries = pos[:, rows.start // 16:rows.stop // 16]
+            nc.vector.tensor_tensor(window[t][:].indirect(entries), xT[:, t, rows], factor_row, MULT)
 
+        all_rows, first_half, second_half = slice(0, R), slice(0, R // 2), slice(R // 2, R)
         for t in range(2):
-            scatter_positives(t, gp_row)
+            scatter_positives(t, all_rows, gp_row[:])
+        scatter_positives(2, first_half, gp_row[:, first_half])
 
-        scaled = sb.tile([P, PACK, R], F32, name="scaled")
+        scaled = sb.tile([P, PACK, R], F32, name="scaled", tag="scaled", align_bytes=64)
         for b in range(PACK):
             scores = bank(b, "scores%d" % b)
             cols = slice(b * P, (b + 1) * P)
@@ -171,15 +175,14 @@ def tile_attend_gspos_ns_w_kernel(tc, x, wT, us, ts, wt, offs, poffs, out):
         for h in range(PACK):
             part = slice(h * 32, (h + 1) * 32)
             nc.scalar.copy(x_r_view[:, part], x_view[:, part])
-        x_r_codes, x_r_scales = quantize("x_r", x_r, E4M3X4)
+        x_r_codes, x_r_scales = quantize("x_r", x_r, E4M3X4, "scaled")
 
         g = sb.tile([P, SLOTS * PACK], BF16, name="g", align_bytes=64)
         nc.vector.tensor_tensor(g[:].rearrange("p (c i j) -> p c j i", i=PACK, j=PACK), sig[:], factor[:], MULT)
-        g_codes, g_scales = quantize("g", g, E5M2X4)
-        gp_row_last = sb.tile([P, R], F32, name="gp_row_last", tag="last")
-        nc.scalar.activation(gp_row_last[:].rearrange("p (s j) -> p s j", j=PACK), gp_spread[:].rearrange("p j s -> p s j"),
-                             COPY, scale=-1.0)
-        scatter_positives(2, gp_row_last)
+        g_codes, g_scales = quantize("g", g, E5M2X4, "g_scales")
+        gp_row_last = sb.tile([P, R // 2], F32, name="gp_row_last", tag="last")
+        nc.scalar.copy(gp_row_last[:], gp_row[:, second_half])
+        scatter_positives(2, second_half, gp_row_last[:])
 
         dn = sb.tile([P, PACK, SLOTS], F32, name="dn")
         out_planes = out.rearrange("(p t) c -> t p c", t=PACK)
@@ -191,6 +194,6 @@ def tile_attend_gspos_ns_w_kernel(tc, x, wT, us, ts, wt, offs, poffs, out):
                                 rhs=g_codes[:].bitcast(E5M2X4), rhs_scale=g_scales[:], start=True, stop=True)
             nc.scalar.copy(dn[:, t, :], sums[:].rearrange("p j s -> p (j s)"))
             if t == PACK - 1:
-                scatter_positives(t, gp_row)
+                scatter_positives(t, all_rows, gp_row[:])
             nc.vector.tensor_copy(window[t][:].indirect(neg[:]), dn[:, t, :])
             nc.sync.dma_start(out=out_planes[t], in_=window[t][:])

@@ -46,7 +46,7 @@ def tile_attend_gspos_ns_w_kernel(tc, x, wT, us, ts, wt, offs, poffs, out):
         nc.sync.dma_start(neg[:], offs)
 
         ts_row = sb.tile([P, T], F32, name="ts_row")
-        nc.vector.memset(ts_row[:], 0.0)
+        nc.gpsimd.memset(ts_row[:], 0.0)
         us_col = sb.tile([P, PACK], F32, name="us_col")
         wt_col = sb.tile([P, PACK], F32, name="wt_col")
         nc.scalar.dma_start(out=us_col[:], in_=us.rearrange("(s j) o -> s (j o)", j=PACK))
@@ -62,10 +62,10 @@ def tile_attend_gspos_ns_w_kernel(tc, x, wT, us, ts, wt, offs, poffs, out):
 
         ident = sb.tile([P, P], F32, name="ident")
         make_identity(nc, ident[:])
-        window = [sb.tile([P, T], F32, name="window%d" % t) for t in range(PACK - 1)]
-        for tile in window:
-            nc.vector.memset(tile[:], 0.0)
-        window.append(window[0])
+        window = [sb.tile([P, T], F32, name="window%d" % t) for t in range(PACK)]
+        for t in range(PACK):
+            engine = nc.vector if t < 2 else nc.gpsimd
+            engine.memset(window[t][:], 0.0)
 
         xT = sb.tile([P, PACK, R], F32, name="xT")
         for t in range(PACK):
@@ -95,19 +95,12 @@ def tile_attend_gspos_ns_w_kernel(tc, x, wT, us, ts, wt, offs, poffs, out):
         ts_neg = sb.tile([P, PACK], F32, name="ts_neg")
         nc.scalar.copy(ts_pos[:], turned_pos[:, :, 0])
         nc.scalar.copy(ts_neg[:], turned_neg[:, :, 0])
-        ts_spread = bank(5, "ts_spread")
-        for b in range(PACK):
-            nc.tensor.transpose(ts_spread[:, b, :], ts_neg[:, b:b + 1].to_broadcast([P, P]), ident[:])
         wu = sb.tile([P, PACK], F32, name="wu")
         us_ts = sb.tile([P, PACK], F32, name="us_ts")
         wu_ts = sb.tile([P, PACK], F32, name="wu_ts")
         nc.gpsimd.tensor_tensor(wu[:], wt_col[:], us_col[:], MULT)
         nc.gpsimd.tensor_tensor(us_ts[:], us_col[:], ts_pos[:], MULT)
         nc.gpsimd.tensor_tensor(wu_ts[:], wu[:], ts_pos[:], MULT)
-        factor = sb.tile([P, P, PACK, PACK], F32, name="factor")
-        for j in range(PACK):
-            nc.scalar.activation(factor[:, :, j, :], ts_spread[:].rearrange("p b (c i) -> p (b c) i", i=PACK), COPY,
-                                 scale=wu[:, j:j + 1])
 
         w_pos = sb.tile([P, PACK, R], F32, name="w_pos")
         w_neg = sb.tile([P, PACK, SLOTS], BF16, name="w_neg", tag="first")
@@ -149,9 +142,9 @@ def tile_attend_gspos_ns_w_kernel(tc, x, wT, us, ts, wt, offs, poffs, out):
             nc.vector.tensor_tensor(window[t][:].indirect(entries), xT[:, t, rows], factor_row, MULT)
 
         all_rows, first_half, second_half = slice(0, R), slice(0, R // 2), slice(R // 2, R)
-        for t in range(2):
+        for t in range(PACK - 1):
             scatter_positives(t, all_rows, gp_row[:])
-        scatter_positives(2, first_half, gp_row[:, first_half])
+        scatter_positives(PACK - 1, first_half, gp_row[:, first_half])
 
         scaled = sb.tile([P, PACK, R], F32, name="scaled", tag="scaled", align_bytes=64)
         for b in range(PACK):
@@ -161,13 +154,31 @@ def tile_attend_gspos_ns_w_kernel(tc, x, wT, us, ts, wt, offs, poffs, out):
                                 lhsT=w_d_codes[:, cols].bitcast(E4M3X4), lhsT_scale=w_d_scales[:, cols],
                                 rhs=x_d_codes[:].bitcast(E4M3X4), rhs_scale=x_d_scales[:], start=True, stop=True)
             nc.scalar.activation(scaled[:, b, :], scores[:].rearrange("p j s -> p (j s)"), COPY, scale=ts_neg[:, b:b + 1])
-        sig = sb.tile([P, P, PACK, PACK], F32, name="sig", tag="last")
+        sig = sb.tile([P, PACK, SLOTS], F32, name="sig")
+        weighted = sb.tile([P, PACK, SLOTS], F32, name="weighted")
         for j in range(PACK):
-            rows = bank((4, 5, 6, 0)[j], "score_rows%d" % j)
+            rows = bank(4 + j, "score_rows%d" % j)
             for b in range(PACK):
                 nc.tensor.transpose(rows[:, b, :], scaled[:, b, j * P:(j + 1) * P], ident[:])
-            nc.scalar.activation(sig[:, :, j, :], rows[:].rearrange("p b (c i) -> p (b c) i", i=PACK), SIGMOID,
-                                 scale=us_col[:, j:j + 1])
+            nc.scalar.activation(sig[:, j, :], rows[:].rearrange("p b i -> p (b i)"), SIGMOID, scale=us_col[:, j:j + 1])
+            nc.scalar.activation(weighted[:, j, :], sig[:, j, :], COPY, scale=wu[:, j:j + 1])
+        slot_rows = [bank(b, "slot_rows%d" % b) for b in range(PACK)]
+        for j in range(PACK):
+            for b in range(PACK):
+                nc.tensor.transpose(slot_rows[b][:, j, :], weighted[:, j, b * P:(b + 1) * P], ident[:])
+        g_slots = sb.tile([P, PACK, R], BF16, name="g_slots", tag="last")
+        g = sb.tile([P, SLOTS * PACK], BF16, name="g", align_bytes=64)
+        g_words = g[:].bitcast(F32).rearrange("p (b i u) -> p b i u", b=PACK, u=2)
+        for k in range(2):
+            pairs = bank(4 + k, "pairs%d" % k)
+            for bb in range(2):
+                b = 2 * k + bb
+                nc.scalar.activation(g_slots[:, b, :].rearrange("p (u s e) -> p u s e", u=2, e=2),
+                                     slot_rows[b][:].rearrange("p (u e) s -> p u s e", u=2), COPY, scale=ts_neg[:, b:b + 1])
+                words = g_slots[:, b, :].bitcast(F32)
+                for u in range(2):
+                    nc.tensor.transpose(pairs[:, 2 * bb + u, :], words[:, u * P:(u + 1) * P], ident[:])
+            nc.scalar.copy(g_words[:, 2 * k:2 * k + 2], pairs[:].rearrange("p (b u) i -> p b i u", u=2))
 
         x_r = sb.tile([P, D * PACK], BF16, name="x_r", align_bytes=64)
         x_r_view = x_r[:].rearrange("p (t m j) -> p m t j", t=PACK, j=PACK)
@@ -177,23 +188,19 @@ def tile_attend_gspos_ns_w_kernel(tc, x, wT, us, ts, wt, offs, poffs, out):
             nc.scalar.copy(x_r_view[:, part], x_view[:, part])
         x_r_codes, x_r_scales = quantize("x_r", x_r, E4M3X4, "scaled")
 
-        g = sb.tile([P, SLOTS * PACK], BF16, name="g", align_bytes=64)
-        nc.vector.tensor_tensor(g[:].rearrange("p (c i j) -> p c j i", i=PACK, j=PACK), sig[:], factor[:], MULT)
         g_codes, g_scales = quantize("g", g, E5M2X4, "g_scales")
         gp_row_last = sb.tile([P, R // 2], F32, name="gp_row_last", tag="last")
         nc.scalar.copy(gp_row_last[:], gp_row[:, second_half])
-        scatter_positives(2, second_half, gp_row_last[:])
+        scatter_positives(PACK - 1, second_half, gp_row_last[:])
 
         dn = sb.tile([P, PACK, SLOTS], F32, name="dn")
         out_planes = out.rearrange("(p t) c -> t p c", t=PACK)
         for t in range(PACK):
-            sums = bank(1 + t, "sums%d" % t)
+            sums = bank((6 + t) % 8, "sums%d" % t)
             cols = slice(t * P, (t + 1) * P)
             nc.tensor.matmul_mx(out=sums[:].rearrange("p j s -> p (j s)"),
                                 lhsT=x_r_codes[:, cols].bitcast(E4M3X4), lhsT_scale=x_r_scales[:, cols],
                                 rhs=g_codes[:].bitcast(E5M2X4), rhs_scale=g_scales[:], start=True, stop=True)
             nc.scalar.copy(dn[:, t, :], sums[:].rearrange("p j s -> p (j s)"))
-            if t == PACK - 1:
-                scatter_positives(t, all_rows, gp_row[:])
             nc.vector.tensor_copy(window[t][:].indirect(neg[:]), dn[:, t, :])
             nc.sync.dma_start(out=out_planes[t], in_=window[t][:])

@@ -45,8 +45,8 @@ def tile_attend_gspos_ns_w_kernel(tc, x, wT, us, ts, wt, offs, poffs, out):
         nc.sync.dma_start(pos[:], poffs)
         nc.sync.dma_start(neg[:], offs)
 
-        ts_row = sb.tile([P, T], F32, name="ts_row")
-        nc.gpsimd.memset(ts_row[:], 0.0)
+        ts_row = sb.tile([P, T], F32, name="ts_row", tag="ts_row")
+        nc.vector.memset(ts_row[:], 0.0)
         us_col = sb.tile([P, PACK], F32, name="us_col")
         wt_col = sb.tile([P, PACK], F32, name="wt_col")
         nc.scalar.dma_start(out=us_col[:], in_=us.rearrange("(s j) o -> s (j o)", j=PACK))
@@ -62,31 +62,29 @@ def tile_attend_gspos_ns_w_kernel(tc, x, wT, us, ts, wt, offs, poffs, out):
 
         ident = sb.tile([P, P], F32, name="ident")
         make_identity(nc, ident[:])
-        window = [sb.tile([P, T], F32, name="window%d" % t) for t in range(PACK)]
-        for t in range(PACK):
-            engine = nc.vector if t < 2 else nc.gpsimd
-            engine.memset(window[t][:], 0.0)
+        window = [sb.tile([P, T], F32, name="window%d" % t) for t in range(PACK - 1)]
+        for tile in window:
+            nc.vector.memset(tile[:], 0.0)
 
+        x_dealt = sb.tile([P, PACK, PACK, P], F32, name="x_dealt")
+        for j in range(PACK):
+            nc.scalar.copy(x_dealt[:, j].rearrange("p t (c i) -> p c t i", i=PACK),
+                           x_sb[:, j, :].rearrange("p (c i t) -> p c t i", i=PACK, t=PACK))
         xT = sb.tile([P, PACK, R], F32, name="xT")
         for t in range(PACK):
             turned_x = bank(4 + t, "turned_x%d" % t)
             for j in range(PACK):
-                nc.tensor.transpose(turned_x[:, j, :], x_sb[:, j, t:D:PACK], ident[:])
+                nc.tensor.transpose(turned_x[:, j, :], x_dealt[:, j, t, :], ident[:])
             nc.scalar.copy(xT[:, t, :].rearrange("p (s j) -> p s j", j=PACK), turned_x[:].rearrange("p j s -> p s j"))
-
-        x_d = sb.tile([P, R * PACK], BF16, name="x_d", align_bytes=64)
-        x_d_view = x_d[:].rearrange("p (j s t) -> p s j t", j=PACK, t=PACK)
-        xT_view = xT[:].rearrange("p t (s j) -> p s j t", j=PACK)
-        for h in range(PACK):
-            part = slice(h * 32, (h + 1) * 32)
-            nc.scalar.copy(x_d_view[:, part], xT_view[:, part])
 
         ts_pos_row = sb.tile([P, R], F32, name="ts_pos_row")
         ts_neg_row = sb.tile([P, SLOTS], F32, name="ts_neg_row")
         nc.vector.tensor_copy(ts_pos_row[:], ts_row[:].indirect(pos[:]))
         nc.vector.tensor_copy(ts_neg_row[:], ts_row[:].indirect(neg[:]))
-        turned_pos = bank(7, "turned_pos")
-        turned_neg = bank(6, "turned_neg")
+        window.append(sb.tile([P, T], F32, name="window_last", tag="ts_row"))
+        nc.gpsimd.memset(window[PACK - 1][:], 0.0)
+        turned_pos = bank(0, "turned_pos")
+        turned_neg = bank(1, "turned_neg")
         for j in range(PACK):
             nc.tensor.transpose(turned_pos[:, j, :], ts_pos_row[:, j:R:PACK], ident[:])
         for b in range(PACK):
@@ -102,28 +100,36 @@ def tile_attend_gspos_ns_w_kernel(tc, x, wT, us, ts, wt, offs, poffs, out):
         nc.gpsimd.tensor_tensor(us_ts[:], us_col[:], ts_pos[:], MULT)
         nc.gpsimd.tensor_tensor(wu_ts[:], wu[:], ts_pos[:], MULT)
 
+        x_d = sb.tile([P, R * PACK], BF16, name="x_d", align_bytes=64)
+        x_d_view = x_d[:].rearrange("p (j s t) -> p s j t", j=PACK, t=PACK)
+        xT_view = xT[:].rearrange("p t (s j) -> p s j t", j=PACK)
+        for h in range(PACK):
+            part = slice(h * 32, (h + 1) * 32)
+            nc.scalar.copy(x_d_view[:, part], xT_view[:, part])
+
         w_pos = sb.tile([P, PACK, R], F32, name="w_pos")
         w_neg = sb.tile([P, PACK, SLOTS], BF16, name="w_neg", tag="first")
+        w_pos_dealt = sb.tile([P, PACK, PACK, P], F32, name="w_pos_dealt")
         w_pos_rows = [bank(j, "w_pos_rows%d" % j) for j in range(PACK)]
         for t in range(PACK):
             nc.vector.tensor_copy(w_pos[:, t, :], w[t][:].indirect(pos[:]))
             nc.vector.tensor_copy(w_neg[:, t, :], w[t][:].indirect(neg[:]))
+            nc.scalar.copy(w_pos_dealt[:, t].rearrange("p j (c i) -> p c j i", i=PACK),
+                           w_pos[:, t, :].rearrange("p (c i j) -> p c j i", i=PACK, j=PACK))
             for j in range(PACK):
-                nc.tensor.transpose(w_pos_rows[j][:, t, :], w_pos[:, t, j:R:PACK], ident[:])
+                nc.tensor.transpose(w_pos_rows[j][:, t, :], w_pos_dealt[:, t, j, :], ident[:])
 
-        sp = sb.tile([P, PACK], F32, name="sp")
-        sig_p = sb.tile([P, PACK], F32, name="sig_p", tag="sig_p", align_bytes=64)
-        gp_col = sb.tile([P, PACK], F32, name="gp_col")
-        products = sb.tile([P, P, PACK], F32, name="products", tag="products", align_bytes=64)
-        gp_spread = bank(7, "gp_spread")
+        sp = sb.tile([P, PACK], F32, name="sp", tag="sp", align_bytes=64)
+        sig_p = sb.tile([P, PACK], F32, name="sig_p")
+        products = sb.tile([P, PACK, PACK, P], F32, name="products", tag="products", align_bytes=64)
+        sig_spread = bank(7, "sig_spread")
         for j in range(PACK):
             nc.vector.scalar_tensor_tensor(
-                out=products[:], in0=w_pos_rows[j][:].rearrange("p t m -> p m t"), scalar=us_ts[:, j:j + 1],
-                in1=x_sb[:, j, :].rearrange("p (m t) -> p m t", t=PACK), op0=MULT, op1=MULT, accum_out=sp[:, j:j + 1])
+                out=products[:, j], in0=w_pos_rows[j][:], scalar=us_ts[:, j:j + 1],
+                in1=x_dealt[:, j], op0=MULT, op1=MULT, accum_out=sp[:, j:j + 1])
         nc.scalar.activation(sig_p[:], sp[:], SIGMOID, scale=-1.0)
-        nc.vector.tensor_tensor(gp_col[:], sig_p[:], wu_ts[:], MULT)
         for j in range(PACK):
-            nc.tensor.transpose(gp_spread[:, j, :], gp_col[:, j:j + 1].to_broadcast([P, P]), ident[:])
+            nc.tensor.transpose(sig_spread[:, j, :], sig_p[:, j:j + 1].to_broadcast([P, P]), ident[:])
 
         w_d = sb.tile([P, SLOTS * PACK], BF16, name="w_d", align_bytes=64)
         w_d_view = w_d[:].rearrange("p (c i t) -> p c t i", i=PACK, t=PACK)
@@ -131,11 +137,18 @@ def tile_attend_gspos_ns_w_kernel(tc, x, wT, us, ts, wt, offs, poffs, out):
         for h in range(PACK):
             part = slice(h * 32, (h + 1) * 32)
             nc.scalar.copy(w_d_view[:, part], w_neg_view[:, part])
-        gp_row = sb.tile([P, R], F32, name="gp_row", tag="first")
-        nc.scalar.activation(gp_row[:].rearrange("p (s j) -> p s j", j=PACK), gp_spread[:].rearrange("p j s -> p s j"),
-                             COPY, scale=-1.0)
+        factor_spread = bank(6, "factor_spread")
+        for j in range(PACK):
+            nc.tensor.transpose(factor_spread[:, j, :], wu_ts[:, j:j + 1].to_broadcast([P, P]), ident[:])
+        factor_row = sb.tile([P, P, PACK], F32, name="factor_row")
+        nc.scalar.copy(factor_row[:], factor_spread[:].rearrange("p j s -> p s j"))
         x_d_codes, x_d_scales = quantize("x_d", x_d, E4M3X4, "products")
-        w_d_codes, w_d_scales = quantize("w_d", w_d, E4M3X4, "sig_p")
+        w_d_codes, w_d_scales = quantize("w_d", w_d, E4M3X4, "sp")
+
+        gp_row = sb.tile([P, R], F32, name="gp_row", tag="first")
+        nc.vector.scalar_tensor_tensor(
+            out=gp_row[:].rearrange("p (s j) -> p s j", j=PACK), in0=sig_spread[:].rearrange("p j s -> p s j"), scalar=-1.0,
+            in1=factor_row[:], op0=MULT, op1=MULT)
 
         def scatter_positives(t, rows, factor_row):
             entries = pos[:, rows.start // 16:rows.stop // 16]
@@ -180,13 +193,10 @@ def tile_attend_gspos_ns_w_kernel(tc, x, wT, us, ts, wt, offs, poffs, out):
                     nc.tensor.transpose(pairs[:, 2 * bb + u, :], words[:, u * P:(u + 1) * P], ident[:])
             nc.scalar.copy(g_words[:, 2 * k:2 * k + 2], pairs[:].rearrange("p (b u) i -> p b i u", u=2))
 
-        x_r = sb.tile([P, D * PACK], BF16, name="x_r", align_bytes=64)
-        x_r_view = x_r[:].rearrange("p (t m j) -> p m t j", t=PACK, j=PACK)
-        x_view = x_sb[:].rearrange("p j (m t) -> p m t j", t=PACK)
-        for h in range(PACK):
-            part = slice(h * 32, (h + 1) * 32)
-            nc.scalar.copy(x_r_view[:, part], x_view[:, part])
-        x_r_codes, x_r_scales = quantize("x_r", x_r, E4M3X4, "scaled")
+        x_r = sb.tile([P, D * PACK], BF16, name="x_r", tag="scaled", align_bytes=64)
+        nc.vector.tensor_copy(x_r[:].rearrange("p (c i j) -> p c j i", i=PACK, j=PACK),
+                              x_dealt[:].rearrange("p j t (c i) -> p (t c) j i", i=PACK))
+        x_r_codes, x_r_scales = quantize("x_r", x_r, E4M3X4, "x_r_scales")
 
         g_codes, g_scales = quantize("g", g, E5M2X4, "g_scales")
         gp_row_last = sb.tile([P, R // 2], F32, name="gp_row_last", tag="last")

@@ -5,6 +5,7 @@ from concourse.masks import make_identity
 
 F32 = mybir.dt.float32
 BF16 = mybir.dt.bfloat16
+I32 = mybir.dt.int32
 U32 = mybir.dt.uint32
 U16 = mybir.dt.uint16
 U8 = mybir.dt.uint8
@@ -46,14 +47,14 @@ def tile_attend_gspos_ns_w_kernel(tc, x, wT, us, ts, wt, offs, poffs, out):
         nc.sync.dma_start(neg[:], offs)
 
         ts_row = sb.tile([P, T], F32, name="ts_row", tag="ts_row")
-        nc.vector.memset(ts_row[:], 0.0)
+        nc.vector.memset(ts_row[:].bitcast(I32), 0)
         us_col = sb.tile([P, PACK], F32, name="us_col")
         wt_col = sb.tile([P, PACK], F32, name="wt_col")
         nc.scalar.dma_start(out=us_col[:], in_=us.rearrange("(s j) o -> s (j o)", j=PACK))
         nc.scalar.dma_start(out=wt_col[:], in_=wt.rearrange("(s j) o -> s (j o)", j=PACK))
 
         w_planes = wT.rearrange("(p t) c -> t p c", t=PACK)
-        w = [sb.tile([P, T], F32, name="w%d" % t) for t in range(PACK)]
+        w = [sb.tile([P, T], F32, name="w%d" % t, tag="w%d" % t) for t in range(PACK)]
         x_sb = sb.tile([P, PACK, D], F32, name="x_sb")
         nc.sync.dma_start(out=x_sb[:], in_=x.rearrange("(s j) d -> s j d", j=PACK))
         nc.sync.dma_start(out=ts_row[0:1, :], in_=ts[0:1, :])
@@ -62,9 +63,8 @@ def tile_attend_gspos_ns_w_kernel(tc, x, wT, us, ts, wt, offs, poffs, out):
 
         ident = sb.tile([P, P], F32, name="ident")
         make_identity(nc, ident[:])
-        window = [sb.tile([P, T], F32, name="window%d" % t) for t in range(PACK - 1)]
-        for tile in window:
-            nc.vector.memset(tile[:], 0.0)
+        window = [sb.tile([P, T], F32, name="window0")]
+        nc.vector.memset(window[0][:].bitcast(I32), 0)
 
         x_dealt = sb.tile([P, PACK, PACK, P], F32, name="x_dealt")
         for j in range(PACK):
@@ -81,8 +81,8 @@ def tile_attend_gspos_ns_w_kernel(tc, x, wT, us, ts, wt, offs, poffs, out):
         ts_neg_row = sb.tile([P, SLOTS], F32, name="ts_neg_row")
         nc.vector.tensor_copy(ts_pos_row[:], ts_row[:].indirect(pos[:]))
         nc.vector.tensor_copy(ts_neg_row[:], ts_row[:].indirect(neg[:]))
-        window.append(sb.tile([P, T], F32, name="window_last", tag="ts_row"))
-        nc.gpsimd.memset(window[PACK - 1][:], 0.0)
+        window.append(sb.tile([P, T], F32, name="window1", tag="ts_row"))
+        nc.gpsimd.memset(window[1][:].bitcast(I32), 0)
         turned_pos = bank(0, "turned_pos")
         turned_neg = bank(1, "turned_neg")
         for j in range(PACK):
@@ -114,6 +114,9 @@ def tile_attend_gspos_ns_w_kernel(tc, x, wT, us, ts, wt, offs, poffs, out):
         for t in range(PACK):
             nc.vector.tensor_copy(w_pos[:, t, :], w[t][:].indirect(pos[:]))
             nc.vector.tensor_copy(w_neg[:, t, :], w[t][:].indirect(neg[:]))
+            if t < 2:
+                window.append(sb.tile([P, T], F32, name="window%d" % (2 + t), tag="w%d" % t))
+                nc.gpsimd.memset(window[2 + t][:].bitcast(I32), 0)
             nc.scalar.copy(w_pos_dealt[:, t].rearrange("p j (c i) -> p c j i", i=PACK),
                            w_pos[:, t, :].rearrange("p (c i j) -> p c j i", i=PACK, j=PACK))
             for j in range(PACK):

@@ -12,6 +12,7 @@ U8 = mybir.dt.uint8
 E4M3X4 = mybir.dt.float8_e4m3fn_x4
 E5M2X4 = mybir.dt.float8_e5m2_x4
 MULT = mybir.AluOpType.mult
+ADD = mybir.AluOpType.add
 COPY = mybir.ActivationFunctionType.Copy
 SIGMOID = mybir.ActivationFunctionType.Sigmoid
 
@@ -21,6 +22,7 @@ D = 512
 R = 512
 SLOTS = 512
 T = 2048
+HALF = SLOTS // 2
 
 FLOPS = 2 * R * D * SLOTS + 2 * D * R * SLOTS
 
@@ -35,41 +37,48 @@ def tile_attend_gspos_ns_w_kernel(tc, x, wT, us, ts, wt, offs, poffs, out):
         def bank(n, name):
             return psum.tile([P, PACK, P], F32, name=name, tag="bank%d" % n)
 
-        def quantize(name, grouped, fmt, scales_tag):
-            codes = sb.tile([P, 512], U32, name=name + "_codes", align_bytes=64)
-            scales = sb.tile([P, 512], U8, name=name + "_scales", tag=scales_tag, align_bytes=64)
+        def flat(tile):
+            return tile[:].rearrange("p a b -> p (a b)")
+
+        def quantize(name, grouped, fmt, codes_tag=""):
+            codes = sb.tile([P, 512], U32, name=name + "_codes", tag=codes_tag, align_bytes=64)
+            scales = sb.tile([P, 512], U8, name=name + "_scales", align_bytes=64)
             nc.vector.quantize_mx(out=codes[:].bitcast(fmt), scales=scales[:], in_=grouped[:])
             return codes, scales
 
         neg = lists.tile([P, SLOTS // 16], U16, name="neg")
         pos = lists.tile([P, R // 16], U16, name="pos")
+        x_rows = x.rearrange("(s j) d -> s j d", j=PACK)
+        x_sb = [sb.tile([P, 2, D], F32, name="x_sb%d" % h) for h in range(2)]
+        for h in range(2):
+            nc.sync.dma_start(out=x_sb[h][:], in_=x_rows[:, 2 * h:2 * h + 2, :])
         nc.sync.dma_start(pos[:], poffs)
         nc.sync.dma_start(neg[:], offs)
 
-        ts_row = sb.tile([P, T], F32, name="ts_row", tag="ts_row")
-        nc.vector.memset(ts_row[:].bitcast(I32), 0)
-        us_col = sb.tile([P, PACK], F32, name="us_col")
-        wt_col = sb.tile([P, PACK], F32, name="wt_col")
-        nc.scalar.dma_start(out=us_col[:], in_=us.rearrange("(s j) o -> s (j o)", j=PACK))
-        nc.scalar.dma_start(out=wt_col[:], in_=wt.rearrange("(s j) o -> s (j o)", j=PACK))
-
-        w_planes = wT.rearrange("(p t) c -> t p c", t=PACK)
-        w = [sb.tile([P, T], F32, name="w%d" % t, tag="w%d" % t) for t in range(PACK)]
-        x_sb = sb.tile([P, PACK, D], F32, name="x_sb")
-        nc.sync.dma_start(out=x_sb[:], in_=x.rearrange("(s j) d -> s j d", j=PACK))
-        nc.sync.dma_start(out=ts_row[0:1, :], in_=ts[0:1, :])
-        for t in range(PACK):
-            nc.sync.dma_start(out=w[t][:], in_=w_planes[t])
-
+        ts_row = sb.tile([P, T], F32, name="ts_row")
+        nc.gpsimd.memset(ts_row[:].bitcast(I32), 0)
         ident = sb.tile([P, P], F32, name="ident")
         make_identity(nc, ident[:])
-        window = [sb.tile([P, T], F32, name="window0")]
-        nc.vector.memset(window[0][:].bitcast(I32), 0)
+        uw_rows = sb.tile([P, P], F32, name="uw_rows")
+        nc.gpsimd.memset(uw_rows[:].bitcast(I32), 0)
+
+        nc.sync.dma_start(out=ts_row[0:1, :], in_=ts[0:1, :])
+        w_planes = wT.rearrange("(p t) c -> t p c", t=PACK)
+        w = [sb.tile([P, T], F32, name="w%d" % t, tag="w%d" % t, align_bytes=64) for t in range(PACK)]
+        nc.sync.dma_start(out=w[0][:], in_=w_planes[0])
+        us_col = sb.tile([P, PACK], F32, name="us_col")
+        wt_col = sb.tile([P, PACK], F32, name="wt_col")
+        nc.sync.dma_start(out=uw_rows[0:PACK, :], in_=us.rearrange("(b s) o -> b (s o)", b=PACK))
+        nc.sync.dma_start(out=uw_rows[PACK:2 * PACK, :], in_=wt.rearrange("(b s) o -> b (s o)", b=PACK))
+        nc.sync.dma_start(out=us_col[:], in_=us.rearrange("(s j) o -> s (j o)", j=PACK))
+        nc.sync.dma_start(out=wt_col[:], in_=wt.rearrange("(s j) o -> s (j o)", j=PACK))
+        for t in range(1, PACK):
+            nc.sync.dma_start(out=w[t][:], in_=w_planes[t])
 
         x_dealt = sb.tile([P, PACK, PACK, P], F32, name="x_dealt")
         for j in range(PACK):
             nc.scalar.copy(x_dealt[:, j].rearrange("p t (c i) -> p c t i", i=PACK),
-                           x_sb[:, j, :].rearrange("p (c i t) -> p c t i", i=PACK, t=PACK))
+                           x_sb[j // 2][:, j % 2, :].rearrange("p (c i t) -> p c t i", i=PACK, t=PACK))
         xT = sb.tile([P, PACK, R], F32, name="xT")
         for t in range(PACK):
             turned_x = bank(4 + t, "turned_x%d" % t)
@@ -81,24 +90,30 @@ def tile_attend_gspos_ns_w_kernel(tc, x, wT, us, ts, wt, offs, poffs, out):
         ts_neg_row = sb.tile([P, SLOTS], F32, name="ts_neg_row")
         nc.vector.tensor_copy(ts_pos_row[:], ts_row[:].indirect(pos[:]))
         nc.vector.tensor_copy(ts_neg_row[:], ts_row[:].indirect(neg[:]))
-        window.append(sb.tile([P, T], F32, name="window1", tag="ts_row"))
-        nc.gpsimd.memset(window[1][:].bitcast(I32), 0)
-        turned_pos = bank(0, "turned_pos")
-        turned_neg = bank(1, "turned_neg")
-        for j in range(PACK):
-            nc.tensor.transpose(turned_pos[:, j, :], ts_pos_row[:, j:R:PACK], ident[:])
+        turned_pos = bank(6, "turned_pos")
+        turned_neg = bank(7, "turned_neg")
+        for b in range(PACK):
+            nc.tensor.transpose(turned_pos[:, b, :], ts_pos_row[:, b * P:(b + 1) * P], ident[:])
         for b in range(PACK):
             nc.tensor.transpose(turned_neg[:, b, :], ts_neg_row[:, b * P:(b + 1) * P], ident[:])
-        ts_pos = sb.tile([P, PACK], F32, name="ts_pos")
         ts_neg = sb.tile([P, PACK], F32, name="ts_neg")
-        nc.scalar.copy(ts_pos[:], turned_pos[:, :, 0])
         nc.scalar.copy(ts_neg[:], turned_neg[:, :, 0])
+        turned_uw = bank(5, "turned_uw")
+        nc.tensor.transpose(turned_uw[:, 0, :], uw_rows[:], ident[:])
+        minus_uw = sb.tile([P, 2 * PACK], F32, name="minus_uw")
+        nc.scalar.activation(minus_uw[:], turned_uw[:, 0, 0:2 * PACK], COPY, scale=-1.0)
+
         wu = sb.tile([P, PACK], F32, name="wu")
-        us_ts = sb.tile([P, PACK], F32, name="us_ts")
+        minus_us_ts = sb.tile([P, PACK], F32, name="minus_us_ts")
         wu_ts = sb.tile([P, PACK], F32, name="wu_ts")
         nc.gpsimd.tensor_tensor(wu[:], wt_col[:], us_col[:], MULT)
-        nc.gpsimd.tensor_tensor(us_ts[:], us_col[:], ts_pos[:], MULT)
-        nc.gpsimd.tensor_tensor(wu_ts[:], wu[:], ts_pos[:], MULT)
+        for b in range(PACK):
+            nc.scalar.activation(minus_us_ts[:, b:b + 1], turned_pos[:, b, 0:1], COPY, scale=minus_uw[:, b:b + 1])
+        for b in range(PACK):
+            nc.scalar.activation(wu_ts[:, b:b + 1], minus_us_ts[:, b:b + 1], COPY, scale=minus_uw[:, PACK + b:PACK + b + 1])
+        window = [sb.tile([P, T], F32, name="window%d" % t) for t in range(PACK)]
+        for t in range(PACK):
+            nc.gpsimd.memset(window[t][:].bitcast(I32), 0)
 
         x_d = sb.tile([P, R * PACK], BF16, name="x_d", align_bytes=64)
         x_d_view = x_d[:].rearrange("p (j s t) -> p s j t", j=PACK, t=PACK)
@@ -106,102 +121,103 @@ def tile_attend_gspos_ns_w_kernel(tc, x, wT, us, ts, wt, offs, poffs, out):
         for h in range(PACK):
             part = slice(h * 32, (h + 1) * 32)
             nc.scalar.copy(x_d_view[:, part], xT_view[:, part])
+        factor_spread = bank(3, "factor_spread")
+        for b in range(PACK):
+            nc.tensor.transpose(factor_spread[:, b, :], wu_ts[:, b:b + 1].to_broadcast([P, P]), ident[:])
+        factor_row = sb.tile([P, R], F32, name="factor_row")
+        nc.scalar.copy(factor_row[:], flat(factor_spread))
 
-        w_pos = sb.tile([P, PACK, R], F32, name="w_pos")
-        w_neg = sb.tile([P, PACK, SLOTS], BF16, name="w_neg", tag="first")
-        w_pos_dealt = sb.tile([P, PACK, PACK, P], F32, name="w_pos_dealt")
-        w_pos_rows = [bank(j, "w_pos_rows%d" % j) for j in range(PACK)]
+        x_r = sb.tile([P, D * PACK], BF16, name="x_r", align_bytes=64)
+        x_r_view = x_r[:].rearrange("p (t c i j) -> p t c j i", t=PACK, i=PACK, j=PACK)
         for t in range(PACK):
-            nc.vector.tensor_copy(w_pos[:, t, :], w[t][:].indirect(pos[:]))
+            nc.scalar.copy(x_r_view[:, t], x_dealt[:, :, t, :].rearrange("p j (c i) -> p c j i", i=PACK))
+
+        products = sb.tile([P, PACK, R], F32, name="products")
+        w_neg = sb.tile([P, PACK, SLOTS], BF16, name="w_neg")
+        dots = bank(2, "dots")
+        for t in range(PACK):
             nc.vector.tensor_copy(w_neg[:, t, :], w[t][:].indirect(neg[:]))
-            if t < 2:
-                window.append(sb.tile([P, T], F32, name="window%d" % (2 + t), tag="w%d" % t))
-                nc.gpsimd.memset(window[2 + t][:].bitcast(I32), 0)
-            nc.scalar.copy(w_pos_dealt[:, t].rearrange("p j (c i) -> p c j i", i=PACK),
-                           w_pos[:, t, :].rearrange("p (c i j) -> p c j i", i=PACK, j=PACK))
-            for j in range(PACK):
-                nc.tensor.transpose(w_pos_rows[j][:, t, :], w_pos_dealt[:, t, j, :], ident[:])
+            nc.vector.tensor_tensor(products[:, t, :], w[t][:].indirect(pos[:]), xT[:, t, :], MULT)
+            for b in range(PACK):
+                nc.tensor.matmul(dots[:, b, :], lhsT=products[:, t, b * P:(b + 1) * P], rhs=ident[:], is_transpose=True,
+                                 start=(t == 0 and b == 0), stop=(t == PACK - 1 and b == PACK - 1))
 
-        sp = sb.tile([P, PACK], F32, name="sp", tag="sp", align_bytes=64)
-        sig_p = sb.tile([P, PACK], F32, name="sig_p")
-        products = sb.tile([P, PACK, PACK, P], F32, name="products", tag="products", align_bytes=64)
-        sig_spread = bank(7, "sig_spread")
-        for j in range(PACK):
-            nc.vector.scalar_tensor_tensor(
-                out=products[:, j], in0=w_pos_rows[j][:], scalar=us_ts[:, j:j + 1],
-                in1=x_dealt[:, j], op0=MULT, op1=MULT, accum_out=sp[:, j:j + 1])
-        nc.scalar.activation(sig_p[:], sp[:], SIGMOID, scale=-1.0)
-        for j in range(PACK):
-            nc.tensor.transpose(sig_spread[:, j, :], sig_p[:, j:j + 1].to_broadcast([P, P]), ident[:])
-
-        w_d = sb.tile([P, SLOTS * PACK], BF16, name="w_d", align_bytes=64)
+        w_d = sb.tile([P, SLOTS * PACK], BF16, name="w_d", tag="w_d", align_bytes=64)
         w_d_view = w_d[:].rearrange("p (c i t) -> p c t i", i=PACK, t=PACK)
         w_neg_view = w_neg[:].rearrange("p t (c i) -> p c t i", i=PACK)
-        for h in range(PACK):
-            part = slice(h * 32, (h + 1) * 32)
+        for b in range(PACK):
+            part = slice(b * 32, (b + 1) * 32)
             nc.scalar.copy(w_d_view[:, part], w_neg_view[:, part])
-        factor_spread = bank(6, "factor_spread")
-        for j in range(PACK):
-            nc.tensor.transpose(factor_spread[:, j, :], wu_ts[:, j:j + 1].to_broadcast([P, P]), ident[:])
-        factor_row = sb.tile([P, P, PACK], F32, name="factor_row")
-        nc.scalar.copy(factor_row[:], factor_spread[:].rearrange("p j s -> p s j"))
-        x_d_codes, x_d_scales = quantize("x_d", x_d, E4M3X4, "products")
-        w_d_codes, w_d_scales = quantize("w_d", w_d, E4M3X4, "sp")
+        x_d_codes, x_d_scales = quantize("x_d", x_d, E4M3X4, "w3")
+        w_d_codes = sb.tile([P, SLOTS], U32, name="w_d_codes", align_bytes=64)
+        w_d_scales = sb.tile([P, SLOTS], U8, name="w_d_scales", align_bytes=64)
 
-        gp_row = sb.tile([P, R], F32, name="gp_row", tag="first")
-        nc.vector.scalar_tensor_tensor(
-            out=gp_row[:].rearrange("p (s j) -> p s j", j=PACK), in0=sig_spread[:].rearrange("p j s -> p s j"), scalar=-1.0,
-            in1=factor_row[:], op0=MULT, op1=MULT)
+        def quantize_w_d(h):
+            words = slice(h * HALF, (h + 1) * HALF)
+            nc.vector.quantize_mx(out=w_d_codes[:, words].bitcast(E4M3X4), scales=w_d_scales[:, words],
+                                  in_=w_d[:, h * HALF * PACK:(h + 1) * HALF * PACK])
 
-        def scatter_positives(t, rows, factor_row):
+        quantize_w_d(0)
+        s0 = sb.tile([P, PACK], F32, name="s0")
+        nc.vector.tensor_reduce(out=s0[:], in_=dots[:], axis=mybir.AxisListType.X, op=ADD)
+        quantize_w_d(1)
+        x_r_codes, x_r_scales = quantize("x_r", x_r, E4M3X4)
+        sig_p = sb.tile([P, PACK], F32, name="sig_p")
+        sig_spread = bank(3, "sig_spread")
+        for b in range(PACK):
+            nc.scalar.activation(sig_p[:, b:b + 1], s0[:, b:b + 1], SIGMOID, scale=minus_us_ts[:, b:b + 1])
+        for b in range(PACK):
+            nc.tensor.transpose(sig_spread[:, b, :], sig_p[:, b:b + 1].to_broadcast([P, P]), ident[:])
+        gp_row = sb.tile([P, R], F32, name="gp_row", tag="w_d", align_bytes=64)
+        nc.vector.scalar_tensor_tensor(out=gp_row[:], in0=flat(sig_spread), scalar=-1.0, in1=factor_row[:], op0=MULT, op1=MULT)
+
+        def scatter_positives(t, rows, factors):
             entries = pos[:, rows.start // 16:rows.stop // 16]
-            nc.vector.tensor_tensor(window[t][:].indirect(entries), xT[:, t, rows], factor_row, MULT)
+            nc.vector.tensor_tensor(window[t][:].indirect(entries), xT[:, t, rows], factors, MULT)
 
         all_rows, first_half, second_half = slice(0, R), slice(0, R // 2), slice(R // 2, R)
         for t in range(PACK - 1):
             scatter_positives(t, all_rows, gp_row[:])
         scatter_positives(PACK - 1, first_half, gp_row[:, first_half])
 
-        scaled = sb.tile([P, PACK, R], F32, name="scaled", tag="scaled", align_bytes=64)
-        for b in range(PACK):
-            scores = bank(b, "scores%d" % b)
-            cols = slice(b * P, (b + 1) * P)
-            nc.tensor.matmul_mx(out=scores[:].rearrange("p j s -> p (j s)"),
-                                lhsT=w_d_codes[:, cols].bitcast(E4M3X4), lhsT_scale=w_d_scales[:, cols],
-                                rhs=x_d_codes[:].bitcast(E4M3X4), rhs_scale=x_d_scales[:], start=True, stop=True)
-            nc.scalar.activation(scaled[:, b, :], scores[:].rearrange("p j s -> p (j s)"), COPY, scale=ts_neg[:, b:b + 1])
-        sig = sb.tile([P, PACK, SLOTS], F32, name="sig")
-        weighted = sb.tile([P, PACK, SLOTS], F32, name="weighted")
-        for j in range(PACK):
-            rows = bank(4 + j, "score_rows%d" % j)
-            for b in range(PACK):
-                nc.tensor.transpose(rows[:, b, :], scaled[:, b, j * P:(j + 1) * P], ident[:])
-            nc.scalar.activation(sig[:, j, :], rows[:].rearrange("p b i -> p (b i)"), SIGMOID, scale=us_col[:, j:j + 1])
-            nc.scalar.activation(weighted[:, j, :], sig[:, j, :], COPY, scale=wu[:, j:j + 1])
-        slot_rows = [bank(b, "slot_rows%d" % b) for b in range(PACK)]
-        for j in range(PACK):
-            for b in range(PACK):
-                nc.tensor.transpose(slot_rows[b][:, j, :], weighted[:, j, b * P:(b + 1) * P], ident[:])
+        scaled = sb.tile([P, PACK, R], F32, name="scaled")
+        sig = sb.tile([P, 2, PACK, HALF], F32, name="sig")
+        weighted = sb.tile([P, 2, PACK, HALF], F32, name="weighted")
         g_slots = sb.tile([P, PACK, R], BF16, name="g_slots", tag="last")
         g = sb.tile([P, SLOTS * PACK], BF16, name="g", align_bytes=64)
         g_words = g[:].bitcast(F32).rearrange("p (b i u) -> p b i u", b=PACK, u=2)
-        for k in range(2):
-            pairs = bank(4 + k, "pairs%d" % k)
+        for h in range(2):
+            blocks = (2 * h, 2 * h + 1)
+            rows = [bank(2 * h + k, "score_rows%d_%d" % (h, k)) for k in range(2)]
+            for b in blocks:
+                scores = bank(4 + b, "scores%d" % b)
+                cols = slice(b * P, (b + 1) * P)
+                nc.tensor.matmul_mx(out=flat(scores),
+                                    lhsT=w_d_codes[:, cols].bitcast(E4M3X4), lhsT_scale=w_d_scales[:, cols],
+                                    rhs=x_d_codes[:].bitcast(E4M3X4), rhs_scale=x_d_scales[:], start=True, stop=True)
+                nc.scalar.activation(scaled[:, b, :], flat(scores), COPY, scale=ts_neg[:, b:b + 1])
+            for b in blocks:
+                for j in range(PACK):
+                    nc.tensor.transpose(rows[j // 2][:, 2 * (j % 2) + b % 2, :], scaled[:, b, j * P:(j + 1) * P], ident[:])
+            slot_rows = [bank(4 + b, "slot_rows%d" % b) for b in blocks]
+            for j in range(PACK):
+                nc.scalar.activation(sig[:, h, j, :], flat(rows[j // 2])[:, (j % 2) * HALF:(j % 2 + 1) * HALF], SIGMOID,
+                                     scale=us_col[:, j:j + 1])
+            for j in range(PACK):
+                nc.scalar.activation(weighted[:, h, j, :], sig[:, h, j, :], COPY, scale=wu[:, j:j + 1])
+                for bb in range(2):
+                    nc.tensor.transpose(slot_rows[bb][:, j, :], weighted[:, h, j, bb * P:(bb + 1) * P], ident[:])
+            pairs = bank(2 * h, "pairs%d" % h)
             for bb in range(2):
-                b = 2 * k + bb
+                b = blocks[bb]
                 nc.scalar.activation(g_slots[:, b, :].rearrange("p (u s e) -> p u s e", u=2, e=2),
-                                     slot_rows[b][:].rearrange("p (u e) s -> p u s e", u=2), COPY, scale=ts_neg[:, b:b + 1])
+                                     slot_rows[bb][:].rearrange("p (u e) s -> p u s e", u=2), COPY, scale=ts_neg[:, b:b + 1])
                 words = g_slots[:, b, :].bitcast(F32)
                 for u in range(2):
                     nc.tensor.transpose(pairs[:, 2 * bb + u, :], words[:, u * P:(u + 1) * P], ident[:])
-            nc.scalar.copy(g_words[:, 2 * k:2 * k + 2], pairs[:].rearrange("p (b u) i -> p b i u", u=2))
+            nc.scalar.copy(g_words[:, 2 * h:2 * h + 2], pairs[:].rearrange("p (b u) i -> p b i u", u=2))
 
-        x_r = sb.tile([P, D * PACK], BF16, name="x_r", tag="scaled", align_bytes=64)
-        nc.vector.tensor_copy(x_r[:].rearrange("p (c i j) -> p c j i", i=PACK, j=PACK),
-                              x_dealt[:].rearrange("p j t (c i) -> p (t c) j i", i=PACK))
-        x_r_codes, x_r_scales = quantize("x_r", x_r, E4M3X4, "x_r_scales")
-
-        g_codes, g_scales = quantize("g", g, E5M2X4, "g_scales")
+        g_codes, g_scales = quantize("g", g, E5M2X4)
         gp_row_last = sb.tile([P, R // 2], F32, name="gp_row_last", tag="last")
         nc.scalar.copy(gp_row_last[:], gp_row[:, second_half])
         scatter_positives(PACK - 1, second_half, gp_row_last[:])
@@ -209,11 +225,11 @@ def tile_attend_gspos_ns_w_kernel(tc, x, wT, us, ts, wt, offs, poffs, out):
         dn = sb.tile([P, PACK, SLOTS], F32, name="dn")
         out_planes = out.rearrange("(p t) c -> t p c", t=PACK)
         for t in range(PACK):
-            sums = bank((6 + t) % 8, "sums%d" % t)
+            sums = bank(4 + t, "sums%d" % t)
             cols = slice(t * P, (t + 1) * P)
-            nc.tensor.matmul_mx(out=sums[:].rearrange("p j s -> p (j s)"),
+            nc.tensor.matmul_mx(out=flat(sums),
                                 lhsT=x_r_codes[:, cols].bitcast(E4M3X4), lhsT_scale=x_r_scales[:, cols],
                                 rhs=g_codes[:].bitcast(E5M2X4), rhs_scale=g_scales[:], start=True, stop=True)
-            nc.scalar.copy(dn[:, t, :], sums[:].rearrange("p j s -> p (j s)"))
+            nc.scalar.copy(dn[:, t, :], flat(sums))
             nc.vector.tensor_copy(window[t][:].indirect(neg[:]), dn[:, t, :])
             nc.sync.dma_start(out=out_planes[t], in_=window[t][:])

@@ -32,6 +32,7 @@ def tile_attend_gspos_ns_w_kernel(tc, x, wT, us, ts, wt, offs, poffs, out):
     with ExitStack() as ctx:
         lists = ctx.enter_context(tc.tile_pool(name="lists", bufs=1))
         sb = ctx.enter_context(tc.tile_pool(name="sb", bufs=1))
+        shared = ctx.enter_context(tc.tile_pool(name="shared", bufs=1))
         psum = ctx.enter_context(tc.psum_pool(name="psum", bufs=1))
 
         def bank(n, name):
@@ -56,7 +57,9 @@ def tile_attend_gspos_ns_w_kernel(tc, x, wT, us, ts, wt, offs, poffs, out):
         nc.sync.dma_start(neg[:], offs)
 
         ts_row = sb.tile([P, T], F32, name="ts_row")
-        nc.gpsimd.memset(ts_row[:].bitcast(I32), 0)
+        nc.vector.memset(ts_row[:].bitcast(I32), 0)
+        window = [sb.tile([P, T], F32, name="window%d" % t) for t in range(PACK)]
+        nc.vector.memset(window[0][:].bitcast(I32), 0)
         ident = sb.tile([P, P], F32, name="ident")
         make_identity(nc, ident[:])
         uw_rows = sb.tile([P, P], F32, name="uw_rows")
@@ -104,15 +107,14 @@ def tile_attend_gspos_ns_w_kernel(tc, x, wT, us, ts, wt, offs, poffs, out):
         nc.scalar.activation(minus_uw[:], turned_uw[:, 0, 0:2 * PACK], COPY, scale=-1.0)
 
         wu = sb.tile([P, PACK], F32, name="wu")
-        minus_us_ts = sb.tile([P, PACK], F32, name="minus_us_ts")
+        minus_us_ts = sb.tile([P, PACK], F32, name="minus_us_ts", tag="scaled")
         wu_ts = sb.tile([P, PACK], F32, name="wu_ts")
         nc.gpsimd.tensor_tensor(wu[:], wt_col[:], us_col[:], MULT)
         for b in range(PACK):
             nc.scalar.activation(minus_us_ts[:, b:b + 1], turned_pos[:, b, 0:1], COPY, scale=minus_uw[:, b:b + 1])
         for b in range(PACK):
             nc.scalar.activation(wu_ts[:, b:b + 1], minus_us_ts[:, b:b + 1], COPY, scale=minus_uw[:, PACK + b:PACK + b + 1])
-        window = [sb.tile([P, T], F32, name="window%d" % t) for t in range(PACK)]
-        for t in range(PACK):
+        for t in range(1, PACK):
             nc.gpsimd.memset(window[t][:].bitcast(I32), 0)
 
         x_d = sb.tile([P, R * PACK], BF16, name="x_d", align_bytes=64)
@@ -150,24 +152,27 @@ def tile_attend_gspos_ns_w_kernel(tc, x, wT, us, ts, wt, offs, poffs, out):
             nc.scalar.copy(w_d_view[:, part], w_neg_view[:, part])
         x_d_codes, x_d_scales = quantize("x_d", x_d, E4M3X4, "w3")
         w_d_codes = sb.tile([P, SLOTS], U32, name="w_d_codes", align_bytes=64)
-        w_d_scales = sb.tile([P, SLOTS], U8, name="w_d_scales", align_bytes=64)
+        w_d_scales = []
 
-        def quantize_w_d(h):
+        def quantize_w_d(h, scales):
             words = slice(h * HALF, (h + 1) * HALF)
-            nc.vector.quantize_mx(out=w_d_codes[:, words].bitcast(E4M3X4), scales=w_d_scales[:, words],
+            w_d_scales.append(scales)
+            nc.vector.quantize_mx(out=w_d_codes[:, words].bitcast(E4M3X4), scales=scales[:],
                                   in_=w_d[:, h * HALF * PACK:(h + 1) * HALF * PACK])
 
-        quantize_w_d(0)
-        s0 = sb.tile([P, PACK], F32, name="s0")
-        nc.vector.tensor_reduce(out=s0[:], in_=dots[:], axis=mybir.AxisListType.X, op=ADD)
-        quantize_w_d(1)
-        x_r_codes, x_r_scales = quantize("x_r", x_r, E4M3X4)
+        quantize_w_d(0, sb.tile([P, HALF], U8, name="w_d_scales0", align_bytes=64))
+        s0 = shared.tile([P, 32], F32, name="s0", offset=192, align_bytes=64)
+        nc.vector.tensor_reduce(out=s0[:, 0:PACK], in_=dots[:], axis=mybir.AxisListType.X, op=ADD)
         sig_p = sb.tile([P, PACK], F32, name="sig_p")
         sig_spread = bank(3, "sig_spread")
         for b in range(PACK):
             nc.scalar.activation(sig_p[:, b:b + 1], s0[:, b:b + 1], SIGMOID, scale=minus_us_ts[:, b:b + 1])
         for b in range(PACK):
             nc.tensor.transpose(sig_spread[:, b, :], sig_p[:, b:b + 1].to_broadcast([P, P]), ident[:])
+        quantize_w_d(1, shared.tile([P, HALF], U8, name="w_d_scales1", offset=0, align_bytes=64))
+        x_r_codes = sb.tile([P, D], U32, name="x_r_codes", align_bytes=64)
+        x_r_scales = shared.tile([P, D], U8, name="x_r_scales", offset=256, align_bytes=64)
+        nc.vector.quantize_mx(out=x_r_codes[:].bitcast(E4M3X4), scales=x_r_scales[:], in_=x_r[:])
         gp_row = sb.tile([P, R], F32, name="gp_row", tag="w_d", align_bytes=64)
         nc.vector.scalar_tensor_tensor(out=gp_row[:], in0=flat(sig_spread), scalar=-1.0, in1=factor_row[:], op0=MULT, op1=MULT)
 
@@ -180,7 +185,7 @@ def tile_attend_gspos_ns_w_kernel(tc, x, wT, us, ts, wt, offs, poffs, out):
             scatter_positives(t, all_rows, gp_row[:])
         scatter_positives(PACK - 1, first_half, gp_row[:, first_half])
 
-        scaled = sb.tile([P, PACK, R], F32, name="scaled")
+        scaled = sb.tile([P, PACK, R], F32, name="scaled", tag="scaled")
         sig = sb.tile([P, 2, PACK, HALF], F32, name="sig")
         weighted = sb.tile([P, 2, PACK, HALF], F32, name="weighted")
         g_slots = sb.tile([P, PACK, R], BF16, name="g_slots", tag="last")
@@ -193,7 +198,7 @@ def tile_attend_gspos_ns_w_kernel(tc, x, wT, us, ts, wt, offs, poffs, out):
                 scores = bank(4 + b, "scores%d" % b)
                 cols = slice(b * P, (b + 1) * P)
                 nc.tensor.matmul_mx(out=flat(scores),
-                                    lhsT=w_d_codes[:, cols].bitcast(E4M3X4), lhsT_scale=w_d_scales[:, cols],
+                                    lhsT=w_d_codes[:, cols].bitcast(E4M3X4), lhsT_scale=w_d_scales[h][:, (b % 2) * P:(b % 2 + 1) * P],
                                     rhs=x_d_codes[:].bitcast(E4M3X4), rhs_scale=x_d_scales[:], start=True, stop=True)
                 nc.scalar.activation(scaled[:, b, :], flat(scores), COPY, scale=ts_neg[:, b:b + 1])
             for b in blocks:

@@ -22,6 +22,7 @@ D = 512
 R = 512
 SLOTS = 512
 T = 2048
+WINDOW_BYTES = 4 * T
 HALF = SLOTS // 2
 
 FLOPS = 2 * R * D * SLOTS + 2 * D * R * SLOTS
@@ -33,6 +34,7 @@ def tile_attend_gspos_ns_w_kernel(tc, x, wT, us, ts, wt, offs, poffs, out):
         lists = ctx.enter_context(tc.tile_pool(name="lists", bufs=1))
         sb = ctx.enter_context(tc.tile_pool(name="sb", bufs=1))
         shared = ctx.enter_context(tc.tile_pool(name="shared", bufs=1))
+        late = ctx.enter_context(tc.tile_pool(name="late", bufs=1))
         psum = ctx.enter_context(tc.psum_pool(name="psum", bufs=1))
 
         def bank(n, name):
@@ -58,7 +60,7 @@ def tile_attend_gspos_ns_w_kernel(tc, x, wT, us, ts, wt, offs, poffs, out):
 
         ts_row = sb.tile([P, T], F32, name="ts_row")
         nc.vector.memset(ts_row[:].bitcast(I32), 0)
-        window = [sb.tile([P, T], F32, name="window%d" % t) for t in range(PACK)]
+        window = [sb.tile([P, T], F32, name="window0")]
         nc.vector.memset(window[0][:].bitcast(I32), 0)
         ident = sb.tile([P, P], F32, name="ident")
         make_identity(nc, ident[:])
@@ -114,8 +116,6 @@ def tile_attend_gspos_ns_w_kernel(tc, x, wT, us, ts, wt, offs, poffs, out):
             nc.scalar.activation(minus_us_ts[:, b:b + 1], turned_pos[:, b, 0:1], COPY, scale=minus_uw[:, b:b + 1])
         for b in range(PACK):
             nc.scalar.activation(wu_ts[:, b:b + 1], minus_us_ts[:, b:b + 1], COPY, scale=minus_uw[:, PACK + b:PACK + b + 1])
-        for t in range(1, PACK):
-            nc.gpsimd.memset(window[t][:].bitcast(I32), 0)
 
         x_d = sb.tile([P, R * PACK], BF16, name="x_d", align_bytes=64)
         x_d_view = x_d[:].rearrange("p (j s t) -> p s j t", j=PACK, t=PACK)
@@ -126,10 +126,10 @@ def tile_attend_gspos_ns_w_kernel(tc, x, wT, us, ts, wt, offs, poffs, out):
         factor_spread = bank(3, "factor_spread")
         for b in range(PACK):
             nc.tensor.transpose(factor_spread[:, b, :], wu_ts[:, b:b + 1].to_broadcast([P, P]), ident[:])
-        factor_row = sb.tile([P, R], F32, name="factor_row")
+        factor_row = late.tile([P, R], F32, name="factor_row", offset=2 * WINDOW_BYTES - 1024)
         nc.scalar.copy(factor_row[:], flat(factor_spread))
 
-        x_r = sb.tile([P, D * PACK], BF16, name="x_r", align_bytes=64)
+        x_r = late.tile([P, D * PACK], BF16, name="x_r", offset=0, align_bytes=64)
         x_r_view = x_r[:].rearrange("p (t c i j) -> p t c j i", t=PACK, i=PACK, j=PACK)
         for t in range(PACK):
             nc.scalar.copy(x_r_view[:, t], x_dealt[:, :, t, :].rearrange("p j (c i) -> p c j i", i=PACK))
@@ -175,6 +175,9 @@ def tile_attend_gspos_ns_w_kernel(tc, x, wT, us, ts, wt, offs, poffs, out):
         nc.vector.quantize_mx(out=x_r_codes[:].bitcast(E4M3X4), scales=x_r_scales[:], in_=x_r[:])
         gp_row = sb.tile([P, R], F32, name="gp_row", tag="w_d", align_bytes=64)
         nc.vector.scalar_tensor_tensor(out=gp_row[:], in0=flat(sig_spread), scalar=-1.0, in1=factor_row[:], op0=MULT, op1=MULT)
+        for t in range(1, PACK):
+            window.append(late.tile([P, T], F32, name="window%d" % t, offset=(t - 1) * WINDOW_BYTES))
+            nc.gpsimd.memset(window[t][:].bitcast(I32), 0)
 
         def scatter_positives(t, rows, factors):
             entries = pos[:, rows.start // 16:rows.stop // 16]

@@ -59,22 +59,24 @@ def tile_attend_gspos_ns_w_kernel(tc, x, wT, us, ts, wt, offs, poffs, out):
         nc.sync.dma_start(neg[:], offs)
 
         ts_row = sb.tile([P, T], F32, name="ts_row")
-        nc.vector.memset(ts_row[:].bitcast(I32), 0)
+        nc.vector.memset(ts_row[0:P - 1, :].bitcast(I32), 0)
         window = [sb.tile([P, T], F32, name="window0")]
         nc.vector.memset(window[0][:].bitcast(I32), 0)
         ident = sb.tile([P, P], F32, name="ident")
         make_identity(nc, ident[:])
+        table_warm_up = sb.tile([P, 1], F32, name="table_warm_up")
+        nc.scalar.activation(table_warm_up[:], ident[:, 0:1], SIGMOID)
         uw_rows = sb.tile([P, P], F32, name="uw_rows")
-        nc.gpsimd.memset(uw_rows[:].bitcast(I32), 0)
+        nc.gpsimd.memset(uw_rows[0:P - 2 * PACK, :].bitcast(I32), 0)
 
-        nc.sync.dma_start(out=ts_row[0:1, :], in_=ts[0:1, :])
+        nc.sync.dma_start(out=ts_row[P - 1:P, :], in_=ts[0:1, :])
         w_planes = wT.rearrange("(p t) c -> t p c", t=PACK)
         w = [sb.tile([P, T], F32, name="w%d" % t, tag="w%d" % t, align_bytes=64) for t in range(PACK)]
         nc.sync.dma_start(out=w[0][:], in_=w_planes[0])
         us_col = sb.tile([P, PACK], F32, name="us_col")
         wt_col = sb.tile([P, PACK], F32, name="wt_col")
-        nc.sync.dma_start(out=uw_rows[0:PACK, :], in_=us.rearrange("(b s) o -> b (s o)", b=PACK))
-        nc.sync.dma_start(out=uw_rows[PACK:2 * PACK, :], in_=wt.rearrange("(b s) o -> b (s o)", b=PACK))
+        nc.sync.dma_start(out=uw_rows[P - 2 * PACK:P - PACK, :], in_=us.rearrange("(b s) o -> b (s o)", b=PACK))
+        nc.sync.dma_start(out=uw_rows[P - PACK:P, :], in_=wt.rearrange("(b s) o -> b (s o)", b=PACK))
         nc.sync.dma_start(out=us_col[:], in_=us.rearrange("(s j) o -> s (j o)", j=PACK))
         nc.sync.dma_start(out=wt_col[:], in_=wt.rearrange("(s j) o -> s (j o)", j=PACK))
         for t in range(1, PACK):
@@ -92,7 +94,7 @@ def tile_attend_gspos_ns_w_kernel(tc, x, wT, us, ts, wt, offs, poffs, out):
             nc.scalar.copy(xT[:, t, :].rearrange("p (s j) -> p s j", j=PACK), turned_x[:].rearrange("p j s -> p s j"))
 
         ts_pos_row = sb.tile([P, R], F32, name="ts_pos_row")
-        ts_neg_row = sb.tile([P, SLOTS], F32, name="ts_neg_row")
+        ts_neg_row = sb.tile([P, SLOTS], F32, name="ts_neg_row", tag="x_r", align_bytes=64)
         nc.vector.tensor_copy(ts_pos_row[:], ts_row[:].indirect(pos[:]))
         nc.vector.tensor_copy(ts_neg_row[:], ts_row[:].indirect(neg[:]))
         turned_pos = bank(6, "turned_pos")
@@ -102,20 +104,22 @@ def tile_attend_gspos_ns_w_kernel(tc, x, wT, us, ts, wt, offs, poffs, out):
         for b in range(PACK):
             nc.tensor.transpose(turned_neg[:, b, :], ts_neg_row[:, b * P:(b + 1) * P], ident[:])
         ts_neg = sb.tile([P, PACK], F32, name="ts_neg")
-        nc.scalar.copy(ts_neg[:], turned_neg[:, :, 0])
+        nc.scalar.copy(ts_neg[:], turned_neg[:, :, P - 1])
         turned_uw = bank(5, "turned_uw")
         nc.tensor.transpose(turned_uw[:, 0, :], uw_rows[:], ident[:])
-        minus_uw = sb.tile([P, 2 * PACK], F32, name="minus_uw")
-        nc.scalar.activation(minus_uw[:], turned_uw[:, 0, 0:2 * PACK], COPY, scale=-1.0)
+        minus_us = sb.tile([P, PACK], F32, name="minus_us")
+        wt_list = sb.tile([P, PACK], F32, name="wt_list")
+        nc.scalar.activation(minus_us[:], turned_uw[:, 0, P - 2 * PACK:P - PACK], COPY, scale=-1.0)
+        nc.scalar.copy(wt_list[:], turned_uw[:, 0, P - PACK:P])
 
         wu = sb.tile([P, PACK], F32, name="wu")
-        minus_us_ts = sb.tile([P, PACK], F32, name="minus_us_ts", tag="scaled")
-        wu_ts = sb.tile([P, PACK], F32, name="wu_ts")
+        minus_us_ts = sb.tile([P, PACK], F32, name="minus_us_ts")
+        minus_wu_ts = sb.tile([P, PACK], F32, name="minus_wu_ts")
         nc.gpsimd.tensor_tensor(wu[:], wt_col[:], us_col[:], MULT)
         for b in range(PACK):
-            nc.scalar.activation(minus_us_ts[:, b:b + 1], turned_pos[:, b, 0:1], COPY, scale=minus_uw[:, b:b + 1])
+            nc.scalar.activation(minus_us_ts[:, b:b + 1], turned_pos[:, b, P - 1:P], COPY, scale=minus_us[:, b:b + 1])
         for b in range(PACK):
-            nc.scalar.activation(wu_ts[:, b:b + 1], minus_us_ts[:, b:b + 1], COPY, scale=minus_uw[:, PACK + b:PACK + b + 1])
+            nc.scalar.activation(minus_wu_ts[:, b:b + 1], minus_us_ts[:, b:b + 1], COPY, scale=wt_list[:, b:b + 1])
 
         x_d = sb.tile([P, R * PACK], BF16, name="x_d", align_bytes=64)
         x_d_view = x_d[:].rearrange("p (j s t) -> p s j t", j=PACK, t=PACK)
@@ -123,60 +127,67 @@ def tile_attend_gspos_ns_w_kernel(tc, x, wT, us, ts, wt, offs, poffs, out):
         for h in range(PACK):
             part = slice(h * 32, (h + 1) * 32)
             nc.scalar.copy(x_d_view[:, part], xT_view[:, part])
-        factor_spread = bank(3, "factor_spread")
-        for b in range(PACK):
-            nc.tensor.transpose(factor_spread[:, b, :], wu_ts[:, b:b + 1].to_broadcast([P, P]), ident[:])
-        factor_row = late.tile([P, R], F32, name="factor_row", offset=2 * WINDOW_BYTES - 1024)
-        nc.scalar.copy(factor_row[:], flat(factor_spread))
 
-        x_r = late.tile([P, D * PACK], BF16, name="x_r", offset=0, align_bytes=64)
+        x_r = sb.tile([P, D * PACK], BF16, name="x_r", tag="x_r", align_bytes=64)
         x_r_view = x_r[:].rearrange("p (t c i j) -> p t c j i", t=PACK, i=PACK, j=PACK)
         for t in range(PACK):
             nc.scalar.copy(x_r_view[:, t], x_dealt[:, :, t, :].rearrange("p j (c i) -> p c j i", i=PACK))
 
-        products = sb.tile([P, PACK, R], F32, name="products")
-        w_neg = sb.tile([P, PACK, SLOTS], BF16, name="w_neg")
+        products = shared.tile([P, PACK, R], F32, name="products", offset=8192, align_bytes=64)
+        w_neg = sb.tile([P, 2, PACK, HALF], BF16, name="w_neg")
         dots = bank(2, "dots")
         for t in range(PACK):
-            nc.vector.tensor_copy(w_neg[:, t, :], w[t][:].indirect(neg[:]))
+            if t < PACK - 1:
+                nc.vector.tensor_copy(w_neg[:, :, t, :], w[t][:].indirect(neg[:]))
             nc.vector.tensor_tensor(products[:, t, :], w[t][:].indirect(pos[:]), xT[:, t, :], MULT)
             for b in range(PACK):
                 nc.tensor.matmul(dots[:, b, :], lhsT=products[:, t, b * P:(b + 1) * P], rhs=ident[:], is_transpose=True,
                                  start=(t == 0 and b == 0), stop=(t == PACK - 1 and b == PACK - 1))
 
-        w_d = sb.tile([P, SLOTS * PACK], BF16, name="w_d", tag="w_d", align_bytes=64)
-        w_d_view = w_d[:].rearrange("p (c i t) -> p c t i", i=PACK, t=PACK)
-        w_neg_view = w_neg[:].rearrange("p t (c i) -> p c t i", i=PACK)
-        for b in range(PACK):
-            part = slice(b * 32, (b + 1) * 32)
-            nc.scalar.copy(w_d_view[:, part], w_neg_view[:, part])
-        x_d_codes, x_d_scales = quantize("x_d", x_d, E4M3X4, "w3")
+        for h in range(2):
+            nc.vector.tensor_copy(w_neg[:, h, PACK - 1, :],
+                                  w[PACK - 1][:].indirect(neg[:, h * HALF // 16:(h + 1) * HALF // 16]))
+
         w_d_codes = sb.tile([P, SLOTS], U32, name="w_d_codes", align_bytes=64)
         w_d_scales = []
 
-        def quantize_w_d(h, scales):
-            words = slice(h * HALF, (h + 1) * HALF)
-            w_d_scales.append(scales)
-            nc.vector.quantize_mx(out=w_d_codes[:, words].bitcast(E4M3X4), scales=scales[:],
-                                  in_=w_d[:, h * HALF * PACK:(h + 1) * HALF * PACK])
+        def interleave_w(h, grouped):
+            nc.scalar.copy(grouped[:].rearrange("p (c i t) -> p c t i", i=PACK, t=PACK),
+                           w_neg[:, h].rearrange("p t (c i) -> p c t i", i=PACK))
 
-        quantize_w_d(0, sb.tile([P, HALF], U8, name="w_d_scales0", align_bytes=64))
-        s0 = shared.tile([P, 32], F32, name="s0", offset=192, align_bytes=64)
+        def quantize_w_d(h, grouped, scales):
+            w_d_scales.append(scales)
+            nc.vector.quantize_mx(out=w_d_codes[:, h * HALF:(h + 1) * HALF].bitcast(E4M3X4), scales=scales[:], in_=grouped[:])
+
+        w_d0 = sb.tile([P, HALF * PACK], BF16, name="w_d0", align_bytes=64)
+        interleave_w(0, w_d0)
+
+        s0 = late.tile([P, 32], F32, name="s0", offset=WINDOW_BYTES - 64, align_bytes=64)
         nc.vector.tensor_reduce(out=s0[:, 0:PACK], in_=dots[:], axis=mybir.AxisListType.X, op=ADD)
+        quantize_w_d(0, w_d0, shared.tile([P, HALF], U8, name="w_d_scales0", offset=8192, align_bytes=64))
+        x_r_codes = sb.tile([P, D], U32, name="x_r_codes", align_bytes=64)
+        x_r_scales = shared.tile([P, D], U8, name="x_r_scales", offset=8192 + 512, align_bytes=64)
+        nc.vector.quantize_mx(out=x_r_codes[:].bitcast(E4M3X4), scales=x_r_scales[:], in_=x_r[:])
         sig_p = sb.tile([P, PACK], F32, name="sig_p")
         sig_spread = bank(3, "sig_spread")
         for b in range(PACK):
             nc.scalar.activation(sig_p[:, b:b + 1], s0[:, b:b + 1], SIGMOID, scale=minus_us_ts[:, b:b + 1])
+        gp = sb.tile([P, PACK], F32, name="gp")
         for b in range(PACK):
-            nc.tensor.transpose(sig_spread[:, b, :], sig_p[:, b:b + 1].to_broadcast([P, P]), ident[:])
-        quantize_w_d(1, shared.tile([P, HALF], U8, name="w_d_scales1", offset=0, align_bytes=64))
-        x_r_codes = sb.tile([P, D], U32, name="x_r_codes", align_bytes=64)
-        x_r_scales = shared.tile([P, D], U8, name="x_r_scales", offset=256, align_bytes=64)
-        nc.vector.quantize_mx(out=x_r_codes[:].bitcast(E4M3X4), scales=x_r_scales[:], in_=x_r[:])
-        gp_row = sb.tile([P, R], F32, name="gp_row", tag="w_d", align_bytes=64)
-        nc.vector.scalar_tensor_tensor(out=gp_row[:], in0=flat(sig_spread), scalar=-1.0, in1=factor_row[:], op0=MULT, op1=MULT)
-        for t in range(1, PACK):
-            window.append(late.tile([P, T], F32, name="window%d" % t, offset=(t - 1) * WINDOW_BYTES))
+            nc.scalar.activation(gp[:, b:b + 1], sig_p[:, b:b + 1], COPY, scale=minus_wu_ts[:, b:b + 1])
+        w_d1_bytes = late.tile([P, HALF * PACK + 64], BF16, name="w_d1", offset=WINDOW_BYTES, align_bytes=64)
+        w_d1 = w_d1_bytes[:, 32:32 + HALF * PACK]
+        interleave_w(1, w_d1)
+        for b in range(PACK):
+            nc.tensor.transpose(sig_spread[:, b, :], gp[:, b:b + 1].to_broadcast([P, P]), ident[:])
+        x_d_codes = sb.tile([P, R], U32, name="x_d_codes", align_bytes=64)
+        x_d_scales = late.tile([P, R], U8, name="x_d_scales", offset=WINDOW_BYTES - 512, align_bytes=64)
+        nc.vector.quantize_mx(out=x_d_codes[:].bitcast(E4M3X4), scales=x_d_scales[:], in_=x_d[:])
+        quantize_w_d(1, w_d1, sb.tile([P, HALF], U8, name="w_d_scales1", tag="x_r", align_bytes=64))
+        gp_row = late.tile([P, R], F32, name="gp_row", offset=WINDOW_BYTES + 64, align_bytes=64)
+        nc.vector.tensor_copy(gp_row[:], flat(sig_spread))
+        for t, offset in ((1, WINDOW_BYTES + 64 + 4 * R), (2, 64)):
+            window.append(late.tile([P, T], F32, name="window%d" % t, offset=offset))
             nc.gpsimd.memset(window[t][:].bitcast(I32), 0)
 
         def scatter_positives(t, rows, factors):
@@ -186,7 +197,6 @@ def tile_attend_gspos_ns_w_kernel(tc, x, wT, us, ts, wt, offs, poffs, out):
         all_rows, first_half, second_half = slice(0, R), slice(0, R // 2), slice(R // 2, R)
         for t in range(PACK - 1):
             scatter_positives(t, all_rows, gp_row[:])
-        scatter_positives(PACK - 1, first_half, gp_row[:, first_half])
 
         scaled = sb.tile([P, PACK, R], F32, name="scaled", tag="scaled")
         sig = sb.tile([P, 2, PACK, HALF], F32, name="sig")
@@ -194,36 +204,38 @@ def tile_attend_gspos_ns_w_kernel(tc, x, wT, us, ts, wt, offs, poffs, out):
         g_slots = sb.tile([P, PACK, R], BF16, name="g_slots", tag="last")
         g = sb.tile([P, SLOTS * PACK], BF16, name="g", align_bytes=64)
         g_words = g[:].bitcast(F32).rearrange("p (b i u) -> p b i u", b=PACK, u=2)
-        for h in range(2):
-            blocks = (2 * h, 2 * h + 1)
-            rows = [bank(2 * h + k, "score_rows%d_%d" % (h, k)) for k in range(2)]
-            for b in blocks:
-                scores = bank(4 + b, "scores%d" % b)
-                cols = slice(b * P, (b + 1) * P)
-                nc.tensor.matmul_mx(out=flat(scores),
-                                    lhsT=w_d_codes[:, cols].bitcast(E4M3X4), lhsT_scale=w_d_scales[h][:, (b % 2) * P:(b % 2 + 1) * P],
-                                    rhs=x_d_codes[:].bitcast(E4M3X4), rhs_scale=x_d_scales[:], start=True, stop=True)
-                nc.scalar.activation(scaled[:, b, :], flat(scores), COPY, scale=ts_neg[:, b:b + 1])
-            for b in blocks:
-                for j in range(PACK):
-                    nc.tensor.transpose(rows[j // 2][:, 2 * (j % 2) + b % 2, :], scaled[:, b, j * P:(j + 1) * P], ident[:])
-            slot_rows = [bank(4 + b, "slot_rows%d" % b) for b in blocks]
+        rows = [[bank(2 * h + k, "score_rows%d_%d" % (h, k)) for k in range(2)] for h in range(2)]
+        for b in range(PACK):
+            h = b // 2
+            scores = bank(4 + b, "scores%d" % b)
+            cols = slice(b * P, (b + 1) * P)
+            nc.tensor.matmul_mx(out=flat(scores),
+                                lhsT=w_d_codes[:, cols].bitcast(E4M3X4), lhsT_scale=w_d_scales[h][:, (b % 2) * P:(b % 2 + 1) * P],
+                                rhs=x_d_codes[:].bitcast(E4M3X4), rhs_scale=x_d_scales[:], start=True, stop=True)
+            nc.scalar.activation(scaled[:, b, :], flat(scores), COPY, scale=ts_neg[:, b:b + 1])
             for j in range(PACK):
-                nc.scalar.activation(sig[:, h, j, :], flat(rows[j // 2])[:, (j % 2) * HALF:(j % 2 + 1) * HALF], SIGMOID,
+                nc.tensor.transpose(rows[h][j // 2][:, 2 * (j % 2) + b % 2, :], scaled[:, b, j * P:(j + 1) * P], ident[:])
+        window.append(sb.tile([P, T], F32, name="window3", tag="scaled"))
+        nc.gpsimd.memset(window[PACK - 1][:].bitcast(I32), 0)
+        scatter_positives(PACK - 1, first_half, gp_row[:, first_half])
+        slot_rows = [bank(4 + b, "slot_rows%d" % b) for b in range(PACK)]
+        for h in range(2):
+            for j in range(PACK):
+                nc.scalar.activation(sig[:, h, j, :], flat(rows[h][j // 2])[:, (j % 2) * HALF:(j % 2 + 1) * HALF], SIGMOID,
                                      scale=us_col[:, j:j + 1])
             for j in range(PACK):
                 nc.scalar.activation(weighted[:, h, j, :], sig[:, h, j, :], COPY, scale=wu[:, j:j + 1])
                 for bb in range(2):
-                    nc.tensor.transpose(slot_rows[bb][:, j, :], weighted[:, h, j, bb * P:(bb + 1) * P], ident[:])
-            pairs = bank(2 * h, "pairs%d" % h)
-            for bb in range(2):
-                b = blocks[bb]
-                nc.scalar.activation(g_slots[:, b, :].rearrange("p (u s e) -> p u s e", u=2, e=2),
-                                     slot_rows[bb][:].rearrange("p (u e) s -> p u s e", u=2), COPY, scale=ts_neg[:, b:b + 1])
-                words = g_slots[:, b, :].bitcast(F32)
-                for u in range(2):
-                    nc.tensor.transpose(pairs[:, 2 * bb + u, :], words[:, u * P:(u + 1) * P], ident[:])
-            nc.scalar.copy(g_words[:, 2 * h:2 * h + 2], pairs[:].rearrange("p (b u) i -> p b i u", u=2))
+                    nc.tensor.transpose(slot_rows[2 * h + bb][:, j, :], weighted[:, h, j, bb * P:(bb + 1) * P], ident[:])
+        pairs = [bank(2 * h, "pairs%d" % h) for h in range(2)]
+        for b in range(PACK):
+            nc.scalar.activation(g_slots[:, b, :].rearrange("p (u s e) -> p u s e", u=2, e=2),
+                                 slot_rows[b][:].rearrange("p (u e) s -> p u s e", u=2), COPY, scale=ts_neg[:, b:b + 1])
+            words = g_slots[:, b, :].bitcast(F32)
+            for u in range(2):
+                nc.tensor.transpose(pairs[b // 2][:, 2 * (b % 2) + u, :], words[:, u * P:(u + 1) * P], ident[:])
+        for h in range(2):
+            nc.scalar.copy(g_words[:, 2 * h:2 * h + 2], pairs[h][:].rearrange("p (b u) i -> p b i u", u=2))
 
         g_codes, g_scales = quantize("g", g, E5M2X4)
         gp_row_last = sb.tile([P, R // 2], F32, name="gp_row_last", tag="last")

@@ -173,10 +173,8 @@ def tile_attend_gspos_ns_w_kernel(tc, x, wT, us, ts, wt, offs, poffs, out):
         for b in range(PACK):
             nc.scalar.activation(sig_p[:, b:b + 1], s0[:, b:b + 1], SIGMOID, scale=minus_us_ts[:, b:b + 1])
         gp = sb.tile([P, PACK], F32, name="gp")
-        for b in range(PACK):
-            nc.scalar.activation(gp[:, b:b + 1], sig_p[:, b:b + 1], COPY, scale=minus_wu_ts[:, b:b + 1])
-        w_d1_bytes = late.tile([P, HALF * PACK + 64], BF16, name="w_d1", offset=WINDOW_BYTES, align_bytes=64)
-        w_d1 = w_d1_bytes[:, 32:32 + HALF * PACK]
+        nc.vector.tensor_tensor(gp[:], sig_p[:], minus_wu_ts[:], MULT)
+        w_d1 = late.tile([P, HALF * PACK], BF16, name="w_d1", offset=WINDOW_BYTES, align_bytes=64)
         interleave_w(1, w_d1)
         for b in range(PACK):
             nc.tensor.transpose(sig_spread[:, b, :], gp[:, b:b + 1].to_broadcast([P, P]), ident[:])
@@ -184,9 +182,9 @@ def tile_attend_gspos_ns_w_kernel(tc, x, wT, us, ts, wt, offs, poffs, out):
         x_d_scales = late.tile([P, R], U8, name="x_d_scales", offset=WINDOW_BYTES - 512, align_bytes=64)
         nc.vector.quantize_mx(out=x_d_codes[:].bitcast(E4M3X4), scales=x_d_scales[:], in_=x_d[:])
         quantize_w_d(1, w_d1, sb.tile([P, HALF], U8, name="w_d_scales1", tag="x_r", align_bytes=64))
-        gp_row = late.tile([P, R], F32, name="gp_row", offset=WINDOW_BYTES + 64, align_bytes=64)
-        nc.vector.tensor_copy(gp_row[:], flat(sig_spread))
-        for t, offset in ((1, WINDOW_BYTES + 64 + 4 * R), (2, 64)):
+        gp_row = sb.tile([P, R], F32, name="gp_row")
+        nc.scalar.copy(gp_row[:], flat(sig_spread))
+        for t, offset in ((1, WINDOW_BYTES + 64), (2, 64)):
             window.append(late.tile([P, T], F32, name="window%d" % t, offset=offset))
             nc.gpsimd.memset(window[t][:].bitcast(I32), 0)
 

@@ -1,7 +1,6 @@
 from contextlib import ExitStack
 
 import concourse.mybir as mybir
-from concourse.masks import make_identity
 
 F32 = mybir.dt.float32
 BF16 = mybir.dt.bfloat16
@@ -12,7 +11,6 @@ U8 = mybir.dt.uint8
 E4M3X4 = mybir.dt.float8_e4m3fn_x4
 E5M2X4 = mybir.dt.float8_e5m2_x4
 MULT = mybir.AluOpType.mult
-ADD = mybir.AluOpType.add
 COPY = mybir.ActivationFunctionType.Copy
 SIGMOID = mybir.ActivationFunctionType.Sigmoid
 
@@ -22,7 +20,6 @@ D = 512
 R = 512
 SLOTS = 512
 T = 2048
-WINDOW_BYTES = 4 * T
 HALF = SLOTS // 2
 
 FLOPS = 2 * R * D * SLOTS + 2 * D * R * SLOTS
@@ -33,8 +30,6 @@ def tile_attend_gspos_ns_w_kernel(tc, x, wT, us, ts, wt, offs, poffs, out):
     with ExitStack() as ctx:
         lists = ctx.enter_context(tc.tile_pool(name="lists", bufs=1))
         sb = ctx.enter_context(tc.tile_pool(name="sb", bufs=1))
-        shared = ctx.enter_context(tc.tile_pool(name="shared", bufs=1))
-        late = ctx.enter_context(tc.tile_pool(name="late", bufs=1))
         psum = ctx.enter_context(tc.psum_pool(name="psum", bufs=1))
 
         def bank(n, name):
@@ -43,83 +38,65 @@ def tile_attend_gspos_ns_w_kernel(tc, x, wT, us, ts, wt, offs, poffs, out):
         def flat(tile):
             return tile[:].rearrange("p a b -> p (a b)")
 
-        def quantize(name, grouped, fmt, codes_tag=""):
-            codes = sb.tile([P, 512], U32, name=name + "_codes", tag=codes_tag, align_bytes=64)
-            scales = sb.tile([P, 512], U8, name=name + "_scales", align_bytes=64)
+        def quantize(name, grouped, fmt, words, scales_tag=""):
+            codes = sb.tile([P, words], U32, name=name + "_codes", align_bytes=64)
+            scales = sb.tile([P, words], U8, name=name + "_scales", tag=scales_tag, align_bytes=64)
             nc.vector.quantize_mx(out=codes[:].bitcast(fmt), scales=scales[:], in_=grouped[:])
             return codes, scales
 
         neg = lists.tile([P, SLOTS // 16], U16, name="neg")
         pos = lists.tile([P, R // 16], U16, name="pos")
-        x_rows = x.rearrange("(s j) d -> s j d", j=PACK)
-        x_sb = [sb.tile([P, 2, D], F32, name="x_sb%d" % h) for h in range(2)]
-        for h in range(2):
-            nc.sync.dma_start(out=x_sb[h][:], in_=x_rows[:, 2 * h:2 * h + 2, :])
         nc.sync.dma_start(pos[:], poffs)
         nc.sync.dma_start(neg[:], offs)
-
         ts_row = sb.tile([P, T], F32, name="ts_row")
+        nc.sync.dma_start(out=ts_row[P - 1:P, :], in_=ts[0:1, :])
+        x_sb = sb.tile([P, PACK, D], F32, name="x_sb")
+        nc.sync.dma_start(out=x_sb[:], in_=x.rearrange("(s j) d -> s j d", j=PACK))
+
         nc.vector.memset(ts_row[0:P - 1, :].bitcast(I32), 0)
-        window = [sb.tile([P, T], F32, name="window0")]
-        nc.vector.memset(window[0][:].bitcast(I32), 0)
+        uw_rows = sb.tile([P, P], F32, name="uw_rows")
+        nc.vector.memset(uw_rows[0:P - 2 * PACK, :].bitcast(I32), 0)
+        ones = sb.tile([P, P], F32, name="ones", tag="first")
+        nc.vector.memset(ones[:], 1.0)
         ident = sb.tile([P, P], F32, name="ident")
-        make_identity(nc, ident[:])
+        nc.gpsimd.affine_select(out=ident[:], in_=ones[:], compare_op=mybir.AluOpType.is_equal, fill=0.0, base=0,
+                                pattern=[[-1, P]], channel_multiplier=1)
         table_warm_up = sb.tile([P, 1], F32, name="table_warm_up")
         nc.scalar.activation(table_warm_up[:], ident[:, 0:1], SIGMOID)
-        uw_rows = sb.tile([P, P], F32, name="uw_rows")
-        nc.gpsimd.memset(uw_rows[0:P - 2 * PACK, :].bitcast(I32), 0)
+        window = [sb.tile([P, T], F32, name="window0", tag="first")]
+        nc.gpsimd.memset(window[0][:].bitcast(I32), 0)
 
-        nc.sync.dma_start(out=ts_row[P - 1:P, :], in_=ts[0:1, :])
         w_planes = wT.rearrange("(p t) c -> t p c", t=PACK)
         w = [sb.tile([P, T], F32, name="w%d" % t, tag="w%d" % t, align_bytes=64) for t in range(PACK)]
         nc.sync.dma_start(out=w[0][:], in_=w_planes[0])
-        us_col = sb.tile([P, PACK], F32, name="us_col")
-        wt_col = sb.tile([P, PACK], F32, name="wt_col")
         nc.sync.dma_start(out=uw_rows[P - 2 * PACK:P - PACK, :], in_=us.rearrange("(b s) o -> b (s o)", b=PACK))
         nc.sync.dma_start(out=uw_rows[P - PACK:P, :], in_=wt.rearrange("(b s) o -> b (s o)", b=PACK))
-        nc.sync.dma_start(out=us_col[:], in_=us.rearrange("(s j) o -> s (j o)", j=PACK))
-        nc.sync.dma_start(out=wt_col[:], in_=wt.rearrange("(s j) o -> s (j o)", j=PACK))
         for t in range(1, PACK):
             nc.sync.dma_start(out=w[t][:], in_=w_planes[t])
+        us_col = sb.tile([P, PACK], F32, name="us_col")
+        wt_col = sb.tile([P, PACK], F32, name="wt_col")
+        nc.sync.dma_start(out=us_col[:], in_=us.rearrange("(s j) o -> s (j o)", j=PACK))
+        nc.sync.dma_start(out=wt_col[:], in_=wt.rearrange("(s j) o -> s (j o)", j=PACK))
 
-        x_dealt = sb.tile([P, PACK, PACK, P], F32, name="x_dealt")
-        for j in range(PACK):
-            nc.scalar.copy(x_dealt[:, j].rearrange("p t (c i) -> p c t i", i=PACK),
-                           x_sb[j // 2][:, j % 2, :].rearrange("p (c i t) -> p c t i", i=PACK, t=PACK))
+        ts_pos_row = sb.tile([P, R], F32, name="ts_pos_row")
+        ts_neg_row = sb.tile([P, SLOTS], F32, name="ts_neg_row")
+        nc.vector.tensor_copy(ts_pos_row[:], ts_row[:].indirect(pos[:]))
+        nc.vector.tensor_copy(ts_neg_row[:], ts_row[:].indirect(neg[:]))
+
+        x_r = sb.tile([P, D * PACK], BF16, name="x_r", tag="x_r", align_bytes=64)
+        nc.vector.tensor_copy(x_r[:].rearrange("p (t m j) -> p m j t", t=PACK, j=PACK),
+                              x_sb[:].rearrange("p j (m t) -> p m j t", t=PACK))
+        x_r_codes, x_r_scales = quantize("x_r", x_r, E4M3X4, D)
+        window.append(sb.tile([P, T], F32, name="window1", tag="x_r", align_bytes=64))
+        nc.gpsimd.memset(window[1][:].bitcast(I32), 0)
+
+        x_planes = x_sb[:].rearrange("p j (m t) -> p j t m", t=PACK)
         xT = sb.tile([P, PACK, R], F32, name="xT")
         for t in range(PACK):
             turned_x = bank(4 + t, "turned_x%d" % t)
             for j in range(PACK):
-                nc.tensor.transpose(turned_x[:, j, :], x_dealt[:, j, t, :], ident[:])
+                nc.tensor.transpose(turned_x[:, j, :], x_planes[:, j, t, :], ident[:])
             nc.scalar.copy(xT[:, t, :].rearrange("p (s j) -> p s j", j=PACK), turned_x[:].rearrange("p j s -> p s j"))
-
-        ts_pos_row = sb.tile([P, R], F32, name="ts_pos_row")
-        ts_neg_row = sb.tile([P, SLOTS], F32, name="ts_neg_row", tag="x_r", align_bytes=64)
-        nc.vector.tensor_copy(ts_pos_row[:], ts_row[:].indirect(pos[:]))
-        nc.vector.tensor_copy(ts_neg_row[:], ts_row[:].indirect(neg[:]))
-        turned_pos = bank(6, "turned_pos")
-        turned_neg = bank(7, "turned_neg")
-        for b in range(PACK):
-            nc.tensor.transpose(turned_pos[:, b, :], ts_pos_row[:, b * P:(b + 1) * P], ident[:])
-        for b in range(PACK):
-            nc.tensor.transpose(turned_neg[:, b, :], ts_neg_row[:, b * P:(b + 1) * P], ident[:])
-        ts_neg = sb.tile([P, PACK], F32, name="ts_neg")
-        nc.scalar.copy(ts_neg[:], turned_neg[:, :, P - 1])
-        turned_uw = bank(5, "turned_uw")
-        nc.tensor.transpose(turned_uw[:, 0, :], uw_rows[:], ident[:])
-        minus_us = sb.tile([P, PACK], F32, name="minus_us")
-        wt_list = sb.tile([P, PACK], F32, name="wt_list")
-        nc.scalar.activation(minus_us[:], turned_uw[:, 0, P - 2 * PACK:P - PACK], COPY, scale=-1.0)
-        nc.scalar.copy(wt_list[:], turned_uw[:, 0, P - PACK:P])
-
-        wu = sb.tile([P, PACK], F32, name="wu")
-        minus_us_ts = sb.tile([P, PACK], F32, name="minus_us_ts")
-        minus_wu_ts = sb.tile([P, PACK], F32, name="minus_wu_ts")
-        nc.gpsimd.tensor_tensor(wu[:], wt_col[:], us_col[:], MULT)
-        for b in range(PACK):
-            nc.scalar.activation(minus_us_ts[:, b:b + 1], turned_pos[:, b, P - 1:P], COPY, scale=minus_us[:, b:b + 1])
-        for b in range(PACK):
-            nc.scalar.activation(minus_wu_ts[:, b:b + 1], minus_us_ts[:, b:b + 1], COPY, scale=wt_list[:, b:b + 1])
 
         x_d = sb.tile([P, R * PACK], BF16, name="x_d", align_bytes=64)
         x_d_view = x_d[:].rearrange("p (j s t) -> p s j t", j=PACK, t=PACK)
@@ -128,126 +105,173 @@ def tile_attend_gspos_ns_w_kernel(tc, x, wT, us, ts, wt, offs, poffs, out):
             part = slice(h * 32, (h + 1) * 32)
             nc.scalar.copy(x_d_view[:, part], xT_view[:, part])
 
-        x_r = sb.tile([P, D * PACK], BF16, name="x_r", tag="x_r", align_bytes=64)
-        x_r_view = x_r[:].rearrange("p (t c i j) -> p t c j i", t=PACK, i=PACK, j=PACK)
-        for t in range(PACK):
-            nc.scalar.copy(x_r_view[:, t], x_dealt[:, :, t, :].rearrange("p j (c i) -> p c j i", i=PACK))
+        turned_pos = bank(0, "turned_pos")
+        turned_neg = bank(7, "turned_neg")
+        for b in range(PACK):
+            nc.tensor.transpose(turned_pos[:, b, :], ts_pos_row[:, b * P:(b + 1) * P], ident[:])
+        for b in range(PACK):
+            nc.tensor.transpose(turned_neg[:, b, :], ts_neg_row[:, b * P:(b + 1) * P], ident[:])
+        turned_uw = bank(1, "turned_uw")
+        nc.tensor.transpose(turned_uw[:, 0, :], uw_rows[:], ident[:])
+        minus_us = sb.tile([P, PACK], F32, name="minus_us")
+        wt_list = sb.tile([P, PACK], F32, name="wt_list")
+        nc.scalar.activation(minus_us[:], turned_uw[:, 0, P - 2 * PACK:P - PACK], COPY, scale=-1.0)
+        nc.scalar.copy(wt_list[:], turned_uw[:, 0, P - PACK:P])
+        minus_us_ts = sb.tile([P, PACK], F32, name="minus_us_ts")
+        minus_wu_ts = sb.tile([P, PACK], F32, name="minus_wu_ts")
+        for b in range(PACK):
+            nc.scalar.activation(minus_us_ts[:, b:b + 1], turned_pos[:, b, P - 1:P], COPY, scale=minus_us[:, b:b + 1])
+        for b in range(PACK):
+            nc.scalar.activation(minus_wu_ts[:, b:b + 1], minus_us_ts[:, b:b + 1], COPY, scale=wt_list[:, b:b + 1])
+        ts_neg = sb.tile([P, PACK], F32, name="ts_neg")
+        nc.scalar.copy(ts_neg[:], turned_neg[:, :, P - 1])
+        wu = sb.tile([P, PACK], F32, name="wu")
+        nc.gpsimd.tensor_tensor(wu[:], wt_col[:], us_col[:], MULT)
 
-        products = shared.tile([P, PACK, R], F32, name="products", offset=8192, align_bytes=64)
-        w_neg = sb.tile([P, 2, PACK, HALF], BF16, name="w_neg")
-        dots = bank(2, "dots")
-        for t in range(PACK):
-            if t < PACK - 1:
-                nc.vector.tensor_copy(w_neg[:, :, t, :], w[t][:].indirect(neg[:]))
+        products = sb.tile([P, PACK, R], F32, name="products")
+        w_neg = sb.tile([P, PACK, SLOTS], BF16, name="w_neg")
+        w_d = sb.tile([P, SLOTS * PACK], BF16, name="w_d", tag="w_d", align_bytes=64)
+        first_half, second_half, all_rows = slice(0, HALF), slice(HALF, R), slice(0, R)
+
+        def interleave_pair(u, slots):
+            planes = slice(2 * u, 2 * u + 2)
+            words = w_d[:, PACK * slots.start:PACK * slots.stop]
+            nc.scalar.copy(words.rearrange("p (c i t) -> p c t i", i=PACK, t=PACK)[:, :, planes, :],
+                           w_neg[:, planes, slots].rearrange("p t (c i) -> p c t i", i=PACK))
+
+        dots = [bank(h, "dots%d" % h) for h in range(2)]
+
+        def add_products(t, b):
+            nc.tensor.matmul(dots[b // 2][:, b % 2, :], lhsT=products[:, t, b * P:(b + 1) * P], rhs=ident[:], is_transpose=True,
+                             start=(t == 0 and b % 2 == 0), stop=(t == PACK - 1 and b % 2 == 1))
+
+        for t in range(PACK - 1):
             nc.vector.tensor_tensor(products[:, t, :], w[t][:].indirect(pos[:]), xT[:, t, :], MULT)
+            nc.vector.tensor_copy(w_neg[:, t, :], w[t][:].indirect(neg[:]))
+            if t == 1:
+                interleave_pair(0, all_rows)
             for b in range(PACK):
-                nc.tensor.matmul(dots[:, b, :], lhsT=products[:, t, b * P:(b + 1) * P], rhs=ident[:], is_transpose=True,
-                                 start=(t == 0 and b == 0), stop=(t == PACK - 1 and b == PACK - 1))
-
+                add_products(t, b)
+        last = PACK - 1
         for h in range(2):
-            nc.vector.tensor_copy(w_neg[:, h, PACK - 1, :],
-                                  w[PACK - 1][:].indirect(neg[:, h * HALF // 16:(h + 1) * HALF // 16]))
+            part = slice(h * HALF, (h + 1) * HALF)
+            nc.vector.tensor_tensor(products[:, last, part], w[last][:].indirect(pos[:, h * HALF // 16:(h + 1) * HALF // 16]),
+                                    xT[:, last, part], MULT)
+            for k in range(2):
+                add_products(last, 2 * h + k)
+            nc.vector.tensor_copy(w_neg[:, last, part], w[last][:].indirect(neg[:, h * HALF // 16:(h + 1) * HALF // 16]))
 
-        w_d_codes = sb.tile([P, SLOTS], U32, name="w_d_codes", align_bytes=64)
-        w_d_scales = []
+        x_d_codes, x_d_scales = quantize("x_d", x_d, E4M3X4, R, scales_tag="w3")
 
-        def interleave_w(h, grouped):
-            nc.scalar.copy(grouped[:].rearrange("p (c i t) -> p c t i", i=PACK, t=PACK),
-                           w_neg[:, h].rearrange("p t (c i) -> p c t i", i=PACK))
+        terms = sb.tile([P, PACK, P], F32, name="terms")
+        spread = [bank(4 + h, "spread%d" % h) for h in range(2)]
 
-        def quantize_w_d(h, grouped, scales):
-            w_d_scales.append(scales)
-            nc.vector.quantize_mx(out=w_d_codes[:, h * HALF:(h + 1) * HALF].bitcast(E4M3X4), scales=scales[:], in_=grouped[:])
-
-        w_d0 = sb.tile([P, HALF * PACK], BF16, name="w_d0", align_bytes=64)
-        interleave_w(0, w_d0)
-
-        s0 = late.tile([P, 32], F32, name="s0", offset=WINDOW_BYTES - 64, align_bytes=64)
-        nc.vector.tensor_reduce(out=s0[:, 0:PACK], in_=dots[:], axis=mybir.AxisListType.X, op=ADD)
-        quantize_w_d(0, w_d0, shared.tile([P, HALF], U8, name="w_d_scales0", offset=8192, align_bytes=64))
-        x_r_codes = sb.tile([P, D], U32, name="x_r_codes", align_bytes=64)
-        x_r_scales = shared.tile([P, D], U8, name="x_r_scales", offset=8192 + 512, align_bytes=64)
-        nc.vector.quantize_mx(out=x_r_codes[:].bitcast(E4M3X4), scales=x_r_scales[:], in_=x_r[:])
-        sig_p = sb.tile([P, PACK], F32, name="sig_p")
-        sig_spread = bank(3, "sig_spread")
-        for b in range(PACK):
-            nc.scalar.activation(sig_p[:, b:b + 1], s0[:, b:b + 1], SIGMOID, scale=minus_us_ts[:, b:b + 1])
-        gp = sb.tile([P, PACK], F32, name="gp")
-        nc.vector.tensor_tensor(gp[:], sig_p[:], minus_wu_ts[:], MULT)
-        w_d1 = late.tile([P, HALF * PACK], BF16, name="w_d1", offset=WINDOW_BYTES, align_bytes=64)
-        interleave_w(1, w_d1)
-        for b in range(PACK):
-            nc.tensor.transpose(sig_spread[:, b, :], gp[:, b:b + 1].to_broadcast([P, P]), ident[:])
-        x_d_codes = sb.tile([P, R], U32, name="x_d_codes", align_bytes=64)
-        x_d_scales = late.tile([P, R], U8, name="x_d_scales", offset=WINDOW_BYTES - 512, align_bytes=64)
-        nc.vector.quantize_mx(out=x_d_codes[:].bitcast(E4M3X4), scales=x_d_scales[:], in_=x_d[:])
-        quantize_w_d(1, w_d1, sb.tile([P, HALF], U8, name="w_d_scales1", tag="x_r", align_bytes=64))
-        gp_row = sb.tile([P, R], F32, name="gp_row")
-        nc.scalar.copy(gp_row[:], flat(sig_spread))
-        for t, offset in ((1, WINDOW_BYTES + 64), (2, 64)):
-            window.append(late.tile([P, T], F32, name="window%d" % t, offset=offset))
-            nc.gpsimd.memset(window[t][:].bitcast(I32), 0)
+        def spread_factor(h):
+            minus_sp = sb.tile([P, 2], F32, name="minus_sp%d" % h, tag="minus_sp")
+            sig_p = w_d[:].bitcast(F32)[:, 2 * h * HALF + 1:2 * h * HALF + 4:2]
+            gp = sb.tile([P, 2], F32, name="gp%d" % h)
+            for k in range(2):
+                b = 2 * h + k
+                nc.scalar.activation(terms[:, b, :], dots[h][:, k, :], COPY, scale=minus_us_ts[:, b:b + 1], accum_out=minus_sp[:, k:k + 1])
+            nc.scalar.activation(sig_p, minus_sp[:], SIGMOID)
+            for k in range(2):
+                b = 2 * h + k
+                nc.scalar.activation(gp[:, k:k + 1], sig_p[:, k:k + 1], COPY, scale=minus_wu_ts[:, b:b + 1])
+                nc.tensor.transpose(spread[h][:, k, :], gp[:, k:k + 1].to_broadcast([P, P]), ident[:])
 
         def scatter_positives(t, rows, factors):
             entries = pos[:, rows.start // 16:rows.stop // 16]
             nc.vector.tensor_tensor(window[t][:].indirect(entries), xT[:, t, rows], factors, MULT)
 
-        all_rows, first_half, second_half = slice(0, R), slice(0, R // 2), slice(R // 2, R)
-        for t in range(PACK - 1):
-            scatter_positives(t, all_rows, gp_row[:])
+        gp_row = sb.tile([P, R], F32, name="gp_row")
+        w_d_codes = sb.tile([P, SLOTS], U32, name="w_d_codes", align_bytes=64)
+        w_d_scales = sb.tile([P, SLOTS], U8, name="w_d_scales", align_bytes=64)
+        for h, part in enumerate((first_half, second_half)):
+            spread_factor(h)
+            interleave_pair(1, part)
+            nc.vector.quantize_mx(out=w_d_codes[:, part].bitcast(E4M3X4), scales=w_d_scales[:, part],
+                                  in_=w_d[:, PACK * part.start:PACK * part.stop])
+            nc.scalar.copy(gp_row[:, part], flat(spread[h])[:, 0:HALF])
+            for t in range(2):
+                scatter_positives(t, part, gp_row[:, part])
+        window.append(sb.tile([P, T], F32, name="window2", tag="w_d", align_bytes=64))
+        nc.gpsimd.memset(window[2][:].bitcast(I32), 0)
+        scatter_positives(2, all_rows, gp_row[:])
 
-        scaled = sb.tile([P, PACK, R], F32, name="scaled", tag="scaled")
-        sig = sb.tile([P, 2, PACK, HALF], F32, name="sig")
-        weighted = sb.tile([P, 2, PACK, HALF], F32, name="weighted")
-        g_slots = sb.tile([P, PACK, R], BF16, name="g_slots", tag="last")
-        g = sb.tile([P, SLOTS * PACK], BF16, name="g", align_bytes=64)
-        g_words = g[:].bitcast(F32).rearrange("p (b i u) -> p b i u", b=PACK, u=2)
-        rows = [[bank(2 * h + k, "score_rows%d_%d" % (h, k)) for k in range(2)] for h in range(2)]
-        for b in range(PACK):
-            h = b // 2
-            scores = bank(4 + b, "scores%d" % b)
-            cols = slice(b * P, (b + 1) * P)
-            nc.tensor.matmul_mx(out=flat(scores),
-                                lhsT=w_d_codes[:, cols].bitcast(E4M3X4), lhsT_scale=w_d_scales[h][:, (b % 2) * P:(b % 2 + 1) * P],
-                                rhs=x_d_codes[:].bitcast(E4M3X4), rhs_scale=x_d_scales[:], start=True, stop=True)
-            nc.scalar.activation(scaled[:, b, :], flat(scores), COPY, scale=ts_neg[:, b:b + 1])
+        g_codes = sb.tile([P, SLOTS], U32, name="g_codes", align_bytes=64)
+        g_scales = sb.tile([P, SLOTS], U8, name="g_scales", align_bytes=64)
+        nc.vector.memset(g_codes[:, second_half].bitcast(I32), 0)
+        nc.vector.memset(g_scales[:, second_half].bitcast(I32), 0)
+
+        def weigh(h):
+            scaled = sb.tile([P, 2, R], F32, name="scaled%d" % h, tag="scaled%d" % h)
+            sig = sb.tile([P, PACK, HALF], F32, name="sig%d" % h)
+            weighted = sb.tile([P, PACK, HALF], F32, name="weighted%d" % h)
+            rows = [bank(2 * h + k, "score_rows%d_%d" % (h, k)) for k in range(2)]
+            for k in range(2):
+                b = 2 * h + k
+                scores = bank((6, 0)[h] + k, "scores%d" % b)
+                cols = slice(b * P, (b + 1) * P)
+                nc.tensor.matmul_mx(out=flat(scores),
+                                    lhsT=w_d_codes[:, cols].bitcast(E4M3X4), lhsT_scale=w_d_scales[:, cols],
+                                    rhs=x_d_codes[:].bitcast(E4M3X4), rhs_scale=x_d_scales[:], start=True, stop=True)
+                nc.scalar.activation(scaled[:, k, :], flat(scores), COPY, scale=ts_neg[:, b:b + 1])
+                for j in range(PACK):
+                    nc.tensor.transpose(rows[j // 2][:, 2 * (j % 2) + k, :], scaled[:, k, j * P:(j + 1) * P], ident[:])
+            slot_rows = [bank(4 + 2 * h + k, "slot_rows%d_%d" % (h, k)) for k in range(2)]
             for j in range(PACK):
-                nc.tensor.transpose(rows[h][j // 2][:, 2 * (j % 2) + b % 2, :], scaled[:, b, j * P:(j + 1) * P], ident[:])
-        window.append(sb.tile([P, T], F32, name="window3", tag="scaled"))
-        nc.gpsimd.memset(window[PACK - 1][:].bitcast(I32), 0)
-        scatter_positives(PACK - 1, first_half, gp_row[:, first_half])
-        slot_rows = [bank(4 + b, "slot_rows%d" % b) for b in range(PACK)]
-        for h in range(2):
-            for j in range(PACK):
-                nc.scalar.activation(sig[:, h, j, :], flat(rows[h][j // 2])[:, (j % 2) * HALF:(j % 2 + 1) * HALF], SIGMOID,
+                nc.scalar.activation(sig[:, j, :], flat(rows[j // 2])[:, (j % 2) * HALF:(j % 2 + 1) * HALF], SIGMOID,
                                      scale=us_col[:, j:j + 1])
-            for j in range(PACK):
-                nc.scalar.activation(weighted[:, h, j, :], sig[:, h, j, :], COPY, scale=wu[:, j:j + 1])
-                for bb in range(2):
-                    nc.tensor.transpose(slot_rows[2 * h + bb][:, j, :], weighted[:, h, j, bb * P:(bb + 1) * P], ident[:])
-        pairs = [bank(2 * h, "pairs%d" % h) for h in range(2)]
-        for b in range(PACK):
-            nc.scalar.activation(g_slots[:, b, :].rearrange("p (u s e) -> p u s e", u=2, e=2),
-                                 slot_rows[b][:].rearrange("p (u e) s -> p u s e", u=2), COPY, scale=ts_neg[:, b:b + 1])
-            words = g_slots[:, b, :].bitcast(F32)
-            for u in range(2):
-                nc.tensor.transpose(pairs[b // 2][:, 2 * (b % 2) + u, :], words[:, u * P:(u + 1) * P], ident[:])
-        for h in range(2):
-            nc.scalar.copy(g_words[:, 2 * h:2 * h + 2], pairs[h][:].rearrange("p (b u) i -> p b i u", u=2))
+                nc.scalar.activation(weighted[:, j, :], sig[:, j, :], COPY, scale=wu[:, j:j + 1])
+                for k in range(2):
+                    nc.tensor.transpose(slot_rows[k][:, j, :], weighted[:, j, k * P:(k + 1) * P], ident[:])
+            return slot_rows
 
-        g_codes, g_scales = quantize("g", g, E5M2X4)
-        gp_row_last = sb.tile([P, R // 2], F32, name="gp_row_last", tag="last")
-        nc.scalar.copy(gp_row_last[:], gp_row[:, second_half])
-        scatter_positives(PACK - 1, second_half, gp_row_last[:])
+        def round_g(h, slot_rows):
+            g_slots = sb.tile([P, 2, R], BF16, name="g_slots%d" % h, tag="g_slots%d" % h)
+            g = sb.tile([P, HALF * PACK], BF16, name="g%d" % h, align_bytes=64)
+            pairs = bank((6, 0)[h], "pairs%d" % h)
+            for k in range(2):
+                nc.scalar.activation(g_slots[:, k, :].rearrange("p (u s e) -> p u s e", u=2, e=2),
+                                     slot_rows[k][:].rearrange("p (u e) s -> p u s e", u=2), COPY,
+                                     scale=ts_neg[:, 2 * h + k:2 * h + k + 1])
+                words = g_slots[:, k, :].bitcast(F32)
+                for u in range(2):
+                    nc.tensor.transpose(pairs[:, 2 * k + u, :], words[:, u * P:(u + 1) * P], ident[:])
+            nc.scalar.copy(g[:].bitcast(F32).rearrange("p (k i u) -> p k i u", k=2, u=2),
+                           pairs[:].rearrange("p (k u) i -> p k i u", u=2))
+            return g
 
-        dn = sb.tile([P, PACK, SLOTS], F32, name="dn")
-        out_planes = out.rearrange("(p t) c -> t p c", t=PACK)
-        for t in range(PACK):
-            sums = bank(4 + t, "sums%d" % t)
+        def quantize_g(g, slots):
+            nc.vector.quantize_mx(out=g_codes[:, slots].bitcast(E5M2X4), scales=g_scales[:, slots], in_=g[:])
+
+        def product(t, n, name):
+            sums = bank(n, name)
             cols = slice(t * P, (t + 1) * P)
             nc.tensor.matmul_mx(out=flat(sums),
                                 lhsT=x_r_codes[:, cols].bitcast(E4M3X4), lhsT_scale=x_r_scales[:, cols],
                                 rhs=g_codes[:].bitcast(E5M2X4), rhs_scale=g_scales[:], start=True, stop=True)
-            nc.scalar.copy(dn[:, t, :], flat(sums))
-            nc.vector.tensor_copy(window[t][:].indirect(neg[:]), dn[:, t, :])
+            return flat(sums)
+
+        def scatter_negatives(t, sums, slots, name, tag=""):
+            dn = sb.tile([P, slots.stop - slots.start], F32, name=name, tag=tag)
+            nc.scalar.copy(dn[:], sums[:, slots])
+            nc.vector.tensor_copy(window[t][:].indirect(neg[:, slots.start // 16:slots.stop // 16]), dn[:])
+
+        quantize_g(round_g(0, weigh(0)), first_half)
+        window.append(sb.tile([P, T], F32, name="window3", tag="scaled0"))
+        nc.gpsimd.memset(window[last][:].bitcast(I32), 0)
+        gp_last = sb.tile([P, R], F32, name="gp_last", tag="g_slots0")
+        nc.scalar.copy(gp_last[:], gp_row[:])
+        scatter_positives(last, all_rows, gp_last[:])
+        slot_rows = weigh(1)
+        scatter_negatives(0, product(0, 3, "early0"), first_half, "dn0_first")
+        g_second = round_g(1, slot_rows)
+        early = product(1, 7, "early1")
+        quantize_g(g_second, second_half)
+        scatter_negatives(1, early, first_half, "dn1_first", tag="g_slots1")
+        out_planes = out.rearrange("(p t) c -> t p c", t=PACK)
+        for t in range(PACK):
+            sums = product(t, (2, 4, 5, 6)[t], "sums%d" % t)
+            scatter_negatives(t, sums, second_half if t < 2 else all_rows, "dn%d" % t)
             nc.sync.dma_start(out=out_planes[t], in_=window[t][:])

@@ -30,6 +30,7 @@ def tile_attend_gspos_ns_w_kernel(tc, x, wT, us, ts, wt, offs, poffs, out):
     with ExitStack() as ctx:
         lists = ctx.enter_context(tc.tile_pool(name="lists", bufs=1))
         sb = ctx.enter_context(tc.tile_pool(name="sb", bufs=1))
+        late = ctx.enter_context(tc.tile_pool(name="late", bufs=1))
         psum = ctx.enter_context(tc.psum_pool(name="psum", bufs=1))
 
         def bank(n, name):
@@ -98,7 +99,7 @@ def tile_attend_gspos_ns_w_kernel(tc, x, wT, us, ts, wt, offs, poffs, out):
                 nc.tensor.transpose(turned_x[:, j, :], x_planes[:, j, t, :], ident[:])
             nc.scalar.copy(xT[:, t, :].rearrange("p (s j) -> p s j", j=PACK), turned_x[:].rearrange("p j s -> p s j"))
 
-        x_d = sb.tile([P, R * PACK], BF16, name="x_d", align_bytes=64)
+        x_d = sb.tile([P, R * PACK], BF16, name="x_d", tag="x_d", align_bytes=64)
         x_d_view = x_d[:].rearrange("p (j s t) -> p s j t", j=PACK, t=PACK)
         xT_view = xT[:].rearrange("p t (s j) -> p s j t", j=PACK)
         for h in range(PACK):
@@ -128,47 +129,60 @@ def tile_attend_gspos_ns_w_kernel(tc, x, wT, us, ts, wt, offs, poffs, out):
         wu = sb.tile([P, PACK], F32, name="wu")
         nc.gpsimd.tensor_tensor(wu[:], wt_col[:], us_col[:], MULT)
 
-        products = sb.tile([P, PACK, R], F32, name="products")
-        w_neg = sb.tile([P, PACK, SLOTS], BF16, name="w_neg")
-        w_d = sb.tile([P, SLOTS * PACK], BF16, name="w_d", tag="w_d", align_bytes=64)
+        last = PACK - 1
         first_half, second_half, all_rows = slice(0, HALF), slice(HALF, R), slice(0, R)
-
-        def interleave_pair(u, slots):
-            planes = slice(2 * u, 2 * u + 2)
-            words = w_d[:, PACK * slots.start:PACK * slots.stop]
-            nc.scalar.copy(words.rearrange("p (c i t) -> p c t i", i=PACK, t=PACK)[:, :, planes, :],
-                           w_neg[:, planes, slots].rearrange("p t (c i) -> p c t i", i=PACK))
-
+        halves = (first_half, second_half)
+        w_d = [sb.tile([P, HALF * PACK], BF16, name="w_d0", align_bytes=64),
+               late.tile([P, HALF * PACK], BF16, name="w_d1", offset=4 * T - PACK * HALF, align_bytes=64)]
+        low_planes = sb.tile([P, 2, SLOTS], BF16, name="low_planes")
         dots = [bank(h, "dots%d" % h) for h in range(2)]
 
-        def add_products(t, b):
-            nc.tensor.matmul(dots[b // 2][:, b % 2, :], lhsT=products[:, t, b * P:(b + 1) * P], rhs=ident[:], is_transpose=True,
-                             start=(t == 0 and b % 2 == 0), stop=(t == PACK - 1 and b % 2 == 1))
+        def entries(listed, part):
+            return listed[:, part.start // 16:part.stop // 16]
 
-        for t in range(PACK - 1):
-            nc.vector.tensor_tensor(products[:, t, :], w[t][:].indirect(pos[:]), xT[:, t, :], MULT)
-            nc.vector.tensor_copy(w_neg[:, t, :], w[t][:].indirect(neg[:]))
-            if t == 1:
-                interleave_pair(0, all_rows)
-            for b in range(PACK):
-                add_products(t, b)
-        last = PACK - 1
+        def interleave_pair(u, h, planes):
+            nc.scalar.copy(w_d[h][:].rearrange("p (c i t) -> p c t i", i=PACK, t=PACK)[:, :, 2 * u:2 * u + 2, :],
+                           planes.rearrange("p t (c i) -> p c t i", i=PACK))
+
+        def gather_positives(t, rows):
+            name = "products%d_%d" % (t, rows.start)
+            products = sb.tile([P, rows.stop - rows.start], F32, name=name, tag=name, align_bytes=64)
+            nc.vector.tensor_tensor(products[:], w[t][:].indirect(entries(pos, rows)), xT[:, t, rows], MULT)
+            for k, b in enumerate(range(rows.start // P, rows.stop // P)):
+                nc.tensor.matmul(dots[b // 2][:, b % 2, :], lhsT=products[:, k * P:(k + 1) * P], rhs=ident[:], is_transpose=True,
+                                 start=(t == 0 and b % 2 == 0), stop=(t == last and b % 2 == 1))
+
+        def gather_high_planes(h, planes, tile):
+            for t in planes:
+                nc.vector.tensor_copy(tile[:, t - 2, :], w[t][:].indirect(entries(neg, halves[h])))
+
+        for t in range(2):
+            gather_positives(t, all_rows)
+            nc.vector.tensor_copy(low_planes[:, t, :], w[t][:].indirect(neg[:]))
         for h in range(2):
-            part = slice(h * HALF, (h + 1) * HALF)
-            nc.vector.tensor_tensor(products[:, last, part], w[last][:].indirect(pos[:, h * HALF // 16:(h + 1) * HALF // 16]),
-                                    xT[:, last, part], MULT)
-            for k in range(2):
-                add_products(last, 2 * h + k)
-            nc.vector.tensor_copy(w_neg[:, last, part], w[last][:].indirect(neg[:, h * HALF // 16:(h + 1) * HALF // 16]))
+            interleave_pair(0, h, low_planes[:, :, halves[h]])
+        high_first = sb.tile([P, 2, HALF], BF16, name="high_first")
+        gather_positives(2, all_rows)
+        gather_high_planes(0, (2,), high_first)
+        for h in range(2):
+            gather_positives(last, halves[h])
+        gather_high_planes(0, (last,), high_first)
+        x_d_codes, x_d_scales = quantize("x_d", x_d, E4M3X4, R, scales_tag="products3_256")
 
-        x_d_codes, x_d_scales = quantize("x_d", x_d, E4M3X4, R, scales_tag="w3")
+        w_d_codes = sb.tile([P, SLOTS], U32, name="w_d_codes", align_bytes=64)
+        w_d_scales = sb.tile([P, SLOTS], U8, name="w_d_scales", align_bytes=64)
+
+        def quantize_w_d(h, high_planes):
+            interleave_pair(1, h, high_planes[:])
+            nc.vector.quantize_mx(out=w_d_codes[:, halves[h]].bitcast(E4M3X4), scales=w_d_scales[:, halves[h]], in_=w_d[h][:])
 
         terms = sb.tile([P, PACK, P], F32, name="terms")
         spread = [bank(4 + h, "spread%d" % h) for h in range(2)]
+        gp_row = sb.tile([P, R], F32, name="gp_row")
 
         def spread_factor(h):
-            minus_sp = sb.tile([P, 2], F32, name="minus_sp%d" % h, tag="minus_sp")
-            sig_p = w_d[:].bitcast(F32)[:, 2 * h * HALF + 1:2 * h * HALF + 4:2]
+            sig_p = w_d[h][:].bitcast(F32)[:, 1:4:2]
+            minus_sp = sb.tile([P, 2], F32, name="minus_sp%d" % h)
             gp = sb.tile([P, 2], F32, name="gp%d" % h)
             for k in range(2):
                 b = 2 * h + k
@@ -180,33 +194,15 @@ def tile_attend_gspos_ns_w_kernel(tc, x, wT, us, ts, wt, offs, poffs, out):
                 nc.tensor.transpose(spread[h][:, k, :], gp[:, k:k + 1].to_broadcast([P, P]), ident[:])
 
         def scatter_positives(t, rows, factors):
-            entries = pos[:, rows.start // 16:rows.stop // 16]
-            nc.vector.tensor_tensor(window[t][:].indirect(entries), xT[:, t, rows], factors, MULT)
+            nc.vector.tensor_tensor(window[t][:].indirect(entries(pos, rows)), xT[:, t, rows], factors, MULT)
 
-        gp_row = sb.tile([P, R], F32, name="gp_row")
-        w_d_codes = sb.tile([P, SLOTS], U32, name="w_d_codes", align_bytes=64)
-        w_d_scales = sb.tile([P, SLOTS], U8, name="w_d_scales", align_bytes=64)
-        for h, part in enumerate((first_half, second_half)):
-            spread_factor(h)
-            interleave_pair(1, part)
-            nc.vector.quantize_mx(out=w_d_codes[:, part].bitcast(E4M3X4), scales=w_d_scales[:, part],
-                                  in_=w_d[:, PACK * part.start:PACK * part.stop])
-            nc.scalar.copy(gp_row[:, part], flat(spread[h])[:, 0:HALF])
+        def scatter_low_planes(h):
+            nc.scalar.copy(gp_row[:, halves[h]], flat(spread[h])[:, 0:HALF])
             for t in range(2):
-                scatter_positives(t, part, gp_row[:, part])
-        window.append(sb.tile([P, T], F32, name="window2", tag="w_d", align_bytes=64))
-        nc.gpsimd.memset(window[2][:].bitcast(I32), 0)
-        scatter_positives(2, all_rows, gp_row[:])
+                scatter_positives(t, halves[h], gp_row[:, halves[h]])
 
-        g_codes = sb.tile([P, SLOTS], U32, name="g_codes", align_bytes=64)
-        g_scales = sb.tile([P, SLOTS], U8, name="g_scales", align_bytes=64)
-        nc.vector.memset(g_codes[:, second_half].bitcast(I32), 0)
-        nc.vector.memset(g_scales[:, second_half].bitcast(I32), 0)
-
-        def weigh(h):
-            scaled = sb.tile([P, 2, R], F32, name="scaled%d" % h, tag="scaled%d" % h)
-            sig = sb.tile([P, PACK, HALF], F32, name="sig%d" % h)
-            weighted = sb.tile([P, PACK, HALF], F32, name="weighted%d" % h)
+        def scale_scores(h):
+            scaled = sb.tile([P, 2, R], F32, name="scaled%d" % h)
             rows = [bank(2 * h + k, "score_rows%d_%d" % (h, k)) for k in range(2)]
             for k in range(2):
                 b = 2 * h + k
@@ -218,6 +214,30 @@ def tile_attend_gspos_ns_w_kernel(tc, x, wT, us, ts, wt, offs, poffs, out):
                 nc.scalar.activation(scaled[:, k, :], flat(scores), COPY, scale=ts_neg[:, b:b + 1])
                 for j in range(PACK):
                     nc.tensor.transpose(rows[j // 2][:, 2 * (j % 2) + k, :], scaled[:, k, j * P:(j + 1) * P], ident[:])
+            return rows
+
+        spread_factor(0)
+        quantize_w_d(0, high_first)
+        high_second = sb.tile([P, 2, HALF], BF16, name="high_second", tag="x_d", align_bytes=64)
+        gather_high_planes(1, (2, 3), high_second)
+        scatter_low_planes(0)
+        rows_first = scale_scores(0)
+        spread_factor(1)
+        quantize_w_d(1, high_second)
+        scatter_low_planes(1)
+        for t in (2, last):
+            window.append(late.tile([P, T], F32, name="window%d" % t, offset=4 * T * (t - 2), align_bytes=64))
+            nc.gpsimd.memset(window[t][:].bitcast(I32), 0)
+        scatter_positives(2, all_rows, gp_row[:])
+
+        g_codes = sb.tile([P, SLOTS], U32, name="g_codes", align_bytes=64)
+        g_scales = sb.tile([P, SLOTS], U8, name="g_scales", align_bytes=64)
+        nc.vector.memset(g_codes[:, second_half].bitcast(I32), 0)
+        nc.vector.memset(g_scales[:, second_half].bitcast(I32), 0)
+
+        def weigh(h, rows):
+            sig = sb.tile([P, PACK, HALF], F32, name="sig%d" % h)
+            weighted = sb.tile([P, PACK, HALF], F32, name="weighted%d" % h, tag="weighted%d" % h)
             slot_rows = [bank(4 + 2 * h + k, "slot_rows%d_%d" % (h, k)) for k in range(2)]
             for j in range(PACK):
                 nc.scalar.activation(sig[:, j, :], flat(rows[j // 2])[:, (j % 2) * HALF:(j % 2 + 1) * HALF], SIGMOID,
@@ -256,15 +276,13 @@ def tile_attend_gspos_ns_w_kernel(tc, x, wT, us, ts, wt, offs, poffs, out):
         def scatter_negatives(t, sums, slots, name, tag=""):
             dn = sb.tile([P, slots.stop - slots.start], F32, name=name, tag=tag)
             nc.scalar.copy(dn[:], sums[:, slots])
-            nc.vector.tensor_copy(window[t][:].indirect(neg[:, slots.start // 16:slots.stop // 16]), dn[:])
+            nc.vector.tensor_copy(window[t][:].indirect(entries(neg, slots)), dn[:])
 
-        quantize_g(round_g(0, weigh(0)), first_half)
-        window.append(sb.tile([P, T], F32, name="window3", tag="scaled0"))
-        nc.gpsimd.memset(window[last][:].bitcast(I32), 0)
-        gp_last = sb.tile([P, R], F32, name="gp_last", tag="g_slots0")
-        nc.scalar.copy(gp_last[:], gp_row[:])
+        quantize_g(round_g(0, weigh(0, rows_first)), first_half)
+        gp_last = sb.tile([P, R], F32, name="gp_last", tag="weighted0")
+        nc.sync.dma_start(out=gp_last[:], in_=gp_row[:])
         scatter_positives(last, all_rows, gp_last[:])
-        slot_rows = weigh(1)
+        slot_rows = weigh(1, scale_scores(1))
         scatter_negatives(0, product(0, 3, "early0"), first_half, "dn0_first")
         g_second = round_g(1, slot_rows)
         early = product(1, 7, "early1")

@@ -51,12 +51,14 @@ def tile_attend_gspos_ns_w_kernel(tc, x, wT, us, ts, wt, offs, poffs, out):
         nc.sync.dma_start(neg[:], offs)
         ts_row = sb.tile([P, T], F32, name="ts_row")
         nc.sync.dma_start(out=ts_row[P - 1:P, :], in_=ts[0:1, :])
-        x_sb = sb.tile([P, PACK, D], F32, name="x_sb")
-        nc.sync.dma_start(out=x_sb[:], in_=x.rearrange("(s j) d -> s j d", j=PACK))
+        x_sb = sb.tile([P, PACK * D], F32, name="x_sb")
+        x_rows = x.rearrange("(s j) d -> s (j d)", j=PACK)
+        for h in range(2):
+            nc.sync.dma_start(out=x_sb[:, 2 * h * D:2 * (h + 1) * D], in_=x_rows[:, 2 * h * D:2 * (h + 1) * D])
 
         nc.vector.memset(ts_row[0:P - 1, :].bitcast(I32), 0)
-        uw_rows = sb.tile([P, P], F32, name="uw_rows")
-        nc.vector.memset(uw_rows[0:P - 2 * PACK, :].bitcast(I32), 0)
+        uw_rows = sb.tile([P, R], F32, name="uw_rows")
+        nc.vector.memset(uw_rows[0:P - 2, :].bitcast(I32), 0)
         ones = sb.tile([P, P], F32, name="ones", tag="first")
         nc.vector.memset(ones[:], 1.0)
         ident = sb.tile([P, P], F32, name="ident")
@@ -70,14 +72,10 @@ def tile_attend_gspos_ns_w_kernel(tc, x, wT, us, ts, wt, offs, poffs, out):
         w_planes = wT.rearrange("(p t) c -> t p c", t=PACK)
         w = [sb.tile([P, T], F32, name="w%d" % t, tag="w%d" % t, align_bytes=64) for t in range(PACK)]
         nc.sync.dma_start(out=w[0][:], in_=w_planes[0])
-        nc.sync.dma_start(out=uw_rows[P - 2 * PACK:P - PACK, :], in_=us.rearrange("(b s) o -> b (s o)", b=PACK))
-        nc.sync.dma_start(out=uw_rows[P - PACK:P, :], in_=wt.rearrange("(b s) o -> b (s o)", b=PACK))
+        nc.sync.dma_start(out=uw_rows[P - 2:P - 1, :], in_=us.rearrange("r o -> o r"))
+        nc.sync.dma_start(out=uw_rows[P - 1:P, :], in_=wt.rearrange("r o -> o r"))
         for t in range(1, PACK):
             nc.sync.dma_start(out=w[t][:], in_=w_planes[t])
-        us_col = sb.tile([P, PACK], F32, name="us_col")
-        wt_col = sb.tile([P, PACK], F32, name="wt_col")
-        nc.sync.dma_start(out=us_col[:], in_=us.rearrange("(s j) o -> s (j o)", j=PACK))
-        nc.sync.dma_start(out=wt_col[:], in_=wt.rearrange("(s j) o -> s (j o)", j=PACK))
 
         ts_pos_row = sb.tile([P, R], F32, name="ts_pos_row")
         ts_neg_row = sb.tile([P, SLOTS], F32, name="ts_neg_row")
@@ -86,12 +84,12 @@ def tile_attend_gspos_ns_w_kernel(tc, x, wT, us, ts, wt, offs, poffs, out):
 
         x_r = sb.tile([P, D * PACK], BF16, name="x_r", tag="x_r", align_bytes=64)
         nc.vector.tensor_copy(x_r[:].rearrange("p (t m j) -> p m j t", t=PACK, j=PACK),
-                              x_sb[:].rearrange("p j (m t) -> p m j t", t=PACK))
+                              x_sb[:].rearrange("p (j m t) -> p m j t", j=PACK, t=PACK))
         x_r_codes, x_r_scales = quantize("x_r", x_r, E4M3X4, D)
         window.append(sb.tile([P, T], F32, name="window1", tag="x_r", align_bytes=64))
         nc.gpsimd.memset(window[1][:].bitcast(I32), 0)
 
-        x_planes = x_sb[:].rearrange("p j (m t) -> p j t m", t=PACK)
+        x_planes = x_sb[:].rearrange("p (j m t) -> p j t m", j=PACK, t=PACK)
         xT = sb.tile([P, PACK, R], F32, name="xT")
         for t in range(PACK):
             turned_x = bank(4 + t, "turned_x%d" % t)
@@ -99,7 +97,7 @@ def tile_attend_gspos_ns_w_kernel(tc, x, wT, us, ts, wt, offs, poffs, out):
                 nc.tensor.transpose(turned_x[:, j, :], x_planes[:, j, t, :], ident[:])
             nc.scalar.copy(xT[:, t, :].rearrange("p (s j) -> p s j", j=PACK), turned_x[:].rearrange("p j s -> p s j"))
 
-        x_d = sb.tile([P, R * PACK], BF16, name="x_d", tag="x_d", align_bytes=64)
+        x_d = sb.tile([P, R * PACK], BF16, name="x_d", align_bytes=64)
         x_d_view = x_d[:].rearrange("p (j s t) -> p s j t", j=PACK, t=PACK)
         xT_view = xT[:].rearrange("p t (s j) -> p s j t", j=PACK)
         for h in range(PACK):
@@ -113,11 +111,15 @@ def tile_attend_gspos_ns_w_kernel(tc, x, wT, us, ts, wt, offs, poffs, out):
         for b in range(PACK):
             nc.tensor.transpose(turned_neg[:, b, :], ts_neg_row[:, b * P:(b + 1) * P], ident[:])
         turned_uw = bank(1, "turned_uw")
-        nc.tensor.transpose(turned_uw[:, 0, :], uw_rows[:], ident[:])
+        dealt_uw = bank(2, "dealt_uw")
+        for b in range(PACK):
+            nc.tensor.transpose(turned_uw[:, b, :], uw_rows[:, b * P:(b + 1) * P], ident[:])
+        for j in range(PACK):
+            nc.tensor.transpose(dealt_uw[:, j, :], uw_rows[:].rearrange("p (s j) -> p j s", j=PACK)[:, j, :], ident[:])
         minus_us = sb.tile([P, PACK], F32, name="minus_us")
         wt_list = sb.tile([P, PACK], F32, name="wt_list")
-        nc.scalar.activation(minus_us[:], turned_uw[:, 0, P - 2 * PACK:P - PACK], COPY, scale=-1.0)
-        nc.scalar.copy(wt_list[:], turned_uw[:, 0, P - PACK:P])
+        nc.scalar.activation(minus_us[:], turned_uw[:, :, P - 2], COPY, scale=-1.0)
+        nc.scalar.copy(wt_list[:], turned_uw[:, :, P - 1])
         minus_us_ts = sb.tile([P, PACK], F32, name="minus_us_ts")
         minus_wu_ts = sb.tile([P, PACK], F32, name="minus_wu_ts")
         for b in range(PACK):
@@ -126,13 +128,16 @@ def tile_attend_gspos_ns_w_kernel(tc, x, wT, us, ts, wt, offs, poffs, out):
             nc.scalar.activation(minus_wu_ts[:, b:b + 1], minus_us_ts[:, b:b + 1], COPY, scale=wt_list[:, b:b + 1])
         ts_neg = sb.tile([P, PACK], F32, name="ts_neg")
         nc.scalar.copy(ts_neg[:], turned_neg[:, :, P - 1])
+        uw_col = sb.tile([P, 2, PACK], F32, name="uw_col")
+        nc.scalar.copy(uw_col[:], dealt_uw[:, :, P - 2:P].rearrange("p j v -> p v j"))
+        us_col = uw_col[:, 0, :]
         wu = sb.tile([P, PACK], F32, name="wu")
-        nc.gpsimd.tensor_tensor(wu[:], wt_col[:], us_col[:], MULT)
+        nc.gpsimd.tensor_tensor(wu[:], uw_col[:, 1, :], us_col, MULT)
 
         last = PACK - 1
         first_half, second_half, all_rows = slice(0, HALF), slice(HALF, R), slice(0, R)
         halves = (first_half, second_half)
-        w_d = [sb.tile([P, HALF * PACK], BF16, name="w_d0", align_bytes=64),
+        w_d = [sb.tile([P, HALF * PACK], BF16, name="w_d0", tag="w_d0", align_bytes=64),
                late.tile([P, HALF * PACK], BF16, name="w_d1", offset=4 * T - PACK * HALF, align_bytes=64)]
         low_planes = sb.tile([P, 2, SLOTS], BF16, name="low_planes")
         dots = [bank(h, "dots%d" % h) for h in range(2)]
@@ -152,10 +157,6 @@ def tile_attend_gspos_ns_w_kernel(tc, x, wT, us, ts, wt, offs, poffs, out):
                 nc.tensor.matmul(dots[b // 2][:, b % 2, :], lhsT=products[:, k * P:(k + 1) * P], rhs=ident[:], is_transpose=True,
                                  start=(t == 0 and b % 2 == 0), stop=(t == last and b % 2 == 1))
 
-        def gather_high_planes(h, planes, tile):
-            for t in planes:
-                nc.vector.tensor_copy(tile[:, t - 2, :], w[t][:].indirect(entries(neg, halves[h])))
-
         for t in range(2):
             gather_positives(t, all_rows)
             nc.vector.tensor_copy(low_planes[:, t, :], w[t][:].indirect(neg[:]))
@@ -163,31 +164,29 @@ def tile_attend_gspos_ns_w_kernel(tc, x, wT, us, ts, wt, offs, poffs, out):
             interleave_pair(0, h, low_planes[:, :, halves[h]])
         high_first = sb.tile([P, 2, HALF], BF16, name="high_first")
         gather_positives(2, all_rows)
-        gather_high_planes(0, (2,), high_first)
+        nc.vector.tensor_copy(high_first[:, 0, :], w[2][:].indirect(entries(neg, first_half)))
         for h in range(2):
             gather_positives(last, halves[h])
-        gather_high_planes(0, (last,), high_first)
+        nc.vector.tensor_copy(high_first[:, 1, :], w[last][:].indirect(entries(neg, first_half)))
         x_d_codes, x_d_scales = quantize("x_d", x_d, E4M3X4, R, scales_tag="products3_256")
 
         w_d_codes = sb.tile([P, SLOTS], U32, name="w_d_codes", align_bytes=64)
-        w_d_scales = sb.tile([P, SLOTS], U8, name="w_d_scales", align_bytes=64)
+        w_d_scales = []
 
-        def quantize_w_d(h, high_planes):
-            interleave_pair(1, h, high_planes[:])
-            nc.vector.quantize_mx(out=w_d_codes[:, halves[h]].bitcast(E4M3X4), scales=w_d_scales[:, halves[h]], in_=w_d[h][:])
+        def quantize_w_d(h, tag):
+            w_d_scales.append(sb.tile([P, HALF], U8, name="w_d_scales%d" % h, tag=tag, align_bytes=64))
+            nc.vector.quantize_mx(out=w_d_codes[:, halves[h]].bitcast(E4M3X4), scales=w_d_scales[h][:], in_=w_d[h][:])
 
         terms = sb.tile([P, PACK, P], F32, name="terms")
         spread = [bank(4 + h, "spread%d" % h) for h in range(2)]
         gp_row = sb.tile([P, R], F32, name="gp_row")
 
-        def spread_factor(h):
-            sig_p = w_d[h][:].bitcast(F32)[:, 1:4:2]
-            minus_sp = sb.tile([P, 2], F32, name="minus_sp%d" % h)
+        def spread_factor(h, minus_sp, sig_p):
             gp = sb.tile([P, 2], F32, name="gp%d" % h)
             for k in range(2):
                 b = 2 * h + k
                 nc.scalar.activation(terms[:, b, :], dots[h][:, k, :], COPY, scale=minus_us_ts[:, b:b + 1], accum_out=minus_sp[:, k:k + 1])
-            nc.scalar.activation(sig_p, minus_sp[:], SIGMOID)
+            nc.scalar.activation(sig_p, minus_sp, SIGMOID)
             for k in range(2):
                 b = 2 * h + k
                 nc.scalar.activation(gp[:, k:k + 1], sig_p[:, k:k + 1], COPY, scale=minus_wu_ts[:, b:b + 1])
@@ -206,34 +205,36 @@ def tile_attend_gspos_ns_w_kernel(tc, x, wT, us, ts, wt, offs, poffs, out):
             rows = [bank(2 * h + k, "score_rows%d_%d" % (h, k)) for k in range(2)]
             for k in range(2):
                 b = 2 * h + k
-                scores = bank((6, 0)[h] + k, "scores%d" % b)
+                scores = bank(6 + k, "scores%d" % b)
                 cols = slice(b * P, (b + 1) * P)
                 nc.tensor.matmul_mx(out=flat(scores),
-                                    lhsT=w_d_codes[:, cols].bitcast(E4M3X4), lhsT_scale=w_d_scales[:, cols],
+                                    lhsT=w_d_codes[:, cols].bitcast(E4M3X4), lhsT_scale=w_d_scales[h][:, k * P:(k + 1) * P],
                                     rhs=x_d_codes[:].bitcast(E4M3X4), rhs_scale=x_d_scales[:], start=True, stop=True)
                 nc.scalar.activation(scaled[:, k, :], flat(scores), COPY, scale=ts_neg[:, b:b + 1])
                 for j in range(PACK):
                     nc.tensor.transpose(rows[j // 2][:, 2 * (j % 2) + k, :], scaled[:, k, j * P:(j + 1) * P], ident[:])
             return rows
 
-        spread_factor(0)
-        quantize_w_d(0, high_first)
-        high_second = sb.tile([P, 2, HALF], BF16, name="high_second", tag="x_d", align_bytes=64)
-        gather_high_planes(1, (2, 3), high_second)
+        spread_factor(0, w_d[1][:].bitcast(F32)[:, 1:4:2], w_d[0][:].bitcast(F32)[:, 1:4:2])
+        interleave_pair(1, 0, high_first[:])
+        for t in (2, last):
+            nc.vector.tensor_copy(w_d[1][:].rearrange("p (i t) -> p t i", t=PACK)[:, t, :], w[t][:].indirect(entries(neg, second_half)))
+        quantize_w_d(0, "")
+        quantize_w_d(1, "w_d0")
         scatter_low_planes(0)
         rows_first = scale_scores(0)
-        spread_factor(1)
-        quantize_w_d(1, high_second)
+        second_columns = sb.tile([P, 2, 2], F32, name="second_columns")
+        spread_factor(1, second_columns[:, 0, :], second_columns[:, 1, :])
         scatter_low_planes(1)
         for t in (2, last):
             window.append(late.tile([P, T], F32, name="window%d" % t, offset=4 * T * (t - 2), align_bytes=64))
             nc.gpsimd.memset(window[t][:].bitcast(I32), 0)
         scatter_positives(2, all_rows, gp_row[:])
 
-        g_codes = sb.tile([P, SLOTS], U32, name="g_codes", align_bytes=64)
-        g_scales = sb.tile([P, SLOTS], U8, name="g_scales", align_bytes=64)
-        nc.vector.memset(g_codes[:, second_half].bitcast(I32), 0)
-        nc.vector.memset(g_scales[:, second_half].bitcast(I32), 0)
+        g_codes = sb.tile([P, SLOTS], U32, name="g_codes", tag="w0", align_bytes=64)
+        g_scales = sb.tile([P, SLOTS], U8, name="g_scales", tag="w1", align_bytes=64)
+        nc.gpsimd.memset(g_codes[:, second_half].bitcast(I32), 0)
+        nc.gpsimd.memset(g_scales[:, second_half].bitcast(I32), 0)
 
         def weigh(h, rows):
             sig = sb.tile([P, PACK, HALF], F32, name="sig%d" % h)
@@ -250,7 +251,7 @@ def tile_attend_gspos_ns_w_kernel(tc, x, wT, us, ts, wt, offs, poffs, out):
         def round_g(h, slot_rows):
             g_slots = sb.tile([P, 2, R], BF16, name="g_slots%d" % h, tag="g_slots%d" % h)
             g = sb.tile([P, HALF * PACK], BF16, name="g%d" % h, align_bytes=64)
-            pairs = bank((6, 0)[h], "pairs%d" % h)
+            pairs = bank(h, "pairs%d" % h)
             for k in range(2):
                 nc.scalar.activation(g_slots[:, k, :].rearrange("p (u s e) -> p u s e", u=2, e=2),
                                      slot_rows[k][:].rearrange("p (u e) s -> p u s e", u=2), COPY,

@@ -56,16 +56,16 @@ def tile_attend_gspos_ns_w_kernel(tc, x, wT, us, ts, wt, offs, poffs, out):
         for h in range(2):
             nc.sync.dma_start(out=x_sb[:, 2 * h * D:2 * (h + 1) * D], in_=x_rows[:, 2 * h * D:2 * (h + 1) * D])
 
-        nc.vector.memset(ts_row[0:P - 1, :].bitcast(I32), 0)
         uw_rows = sb.tile([P, R], F32, name="uw_rows")
         nc.vector.memset(uw_rows[0:P - 2, :].bitcast(I32), 0)
+        nc.vector.memset(ts_row[0:P - 1, :].bitcast(I32), 0)
         ones = sb.tile([P, P], F32, name="ones", tag="first")
         nc.vector.memset(ones[:], 1.0)
         ident = sb.tile([P, P], F32, name="ident")
         nc.gpsimd.affine_select(out=ident[:], in_=ones[:], compare_op=mybir.AluOpType.is_equal, fill=0.0, base=0,
                                 pattern=[[-1, P]], channel_multiplier=1)
         table_warm_up = sb.tile([P, 1], F32, name="table_warm_up")
-        nc.scalar.activation(table_warm_up[:], ident[:, 0:1], SIGMOID)
+        nc.scalar.activation(table_warm_up[0:P // 2, :], uw_rows[0:P // 2, 0:1], SIGMOID)
         window = [sb.tile([P, T], F32, name="window0", tag="first")]
         nc.gpsimd.memset(window[0][:].bitcast(I32), 0)
 
@@ -83,8 +83,10 @@ def tile_attend_gspos_ns_w_kernel(tc, x, wT, us, ts, wt, offs, poffs, out):
         nc.vector.tensor_copy(ts_neg_row[:], ts_row[:].indirect(neg[:]))
 
         x_r = sb.tile([P, D * PACK], BF16, name="x_r", tag="x_r", align_bytes=64)
-        nc.vector.tensor_copy(x_r[:].rearrange("p (t m j) -> p m j t", t=PACK, j=PACK),
-                              x_sb[:].rearrange("p (j m t) -> p m j t", j=PACK, t=PACK))
+        x_r_view = x_r[:].rearrange("p (t m j) -> p m j t", t=PACK, j=PACK)
+        x_sb_view = x_sb[:].rearrange("p (j m t) -> p m j t", j=PACK, t=PACK)
+        nc.vector.tensor_copy(x_r_view[:, :, :, 0:2], x_sb_view[:, :, :, 0:2])
+        nc.scalar.copy(x_r_view[:, :, :, 2:PACK], x_sb_view[:, :, :, 2:PACK])
         x_r_codes, x_r_scales = quantize("x_r", x_r, E4M3X4, D)
         window.append(sb.tile([P, T], F32, name="window1", tag="x_r", align_bytes=64))
         nc.gpsimd.memset(window[1][:].bitcast(I32), 0)
@@ -97,7 +99,7 @@ def tile_attend_gspos_ns_w_kernel(tc, x, wT, us, ts, wt, offs, poffs, out):
                 nc.tensor.transpose(turned_x[:, j, :], x_planes[:, j, t, :], ident[:])
             nc.scalar.copy(xT[:, t, :].rearrange("p (s j) -> p s j", j=PACK), turned_x[:].rearrange("p j s -> p s j"))
 
-        x_d = sb.tile([P, R * PACK], BF16, name="x_d", align_bytes=64)
+        x_d = sb.tile([P, R * PACK], BF16, name="x_d", tag="x_d", align_bytes=64)
         x_d_view = x_d[:].rearrange("p (j s t) -> p s j t", j=PACK, t=PACK)
         xT_view = xT[:].rearrange("p t (s j) -> p s j t", j=PACK)
         for h in range(PACK):
@@ -137,7 +139,7 @@ def tile_attend_gspos_ns_w_kernel(tc, x, wT, us, ts, wt, offs, poffs, out):
         last = PACK - 1
         first_half, second_half, all_rows = slice(0, HALF), slice(HALF, R), slice(0, R)
         halves = (first_half, second_half)
-        w_d = [sb.tile([P, HALF * PACK], BF16, name="w_d0", tag="w_d0", align_bytes=64),
+        w_d = [sb.tile([P, HALF * PACK], BF16, name="w_d0", align_bytes=64),
                late.tile([P, HALF * PACK], BF16, name="w_d1", offset=4 * T - PACK * HALF, align_bytes=64)]
         low_planes = sb.tile([P, 2, SLOTS], BF16, name="low_planes")
         dots = [bank(h, "dots%d" % h) for h in range(2)]
@@ -162,41 +164,49 @@ def tile_attend_gspos_ns_w_kernel(tc, x, wT, us, ts, wt, offs, poffs, out):
             nc.vector.tensor_copy(low_planes[:, t, :], w[t][:].indirect(neg[:]))
         for h in range(2):
             interleave_pair(0, h, low_planes[:, :, halves[h]])
-        high_first = sb.tile([P, 2, HALF], BF16, name="high_first")
+        def gather_into_words(t):
+            nc.vector.tensor_copy(w_d[0][:].rearrange("p (i t) -> p t i", t=PACK)[:, t, :], w[t][:].indirect(entries(neg, first_half)))
+
         gather_positives(2, all_rows)
-        nc.vector.tensor_copy(high_first[:, 0, :], w[2][:].indirect(entries(neg, first_half)))
-        for h in range(2):
-            gather_positives(last, halves[h])
-        nc.vector.tensor_copy(high_first[:, 1, :], w[last][:].indirect(entries(neg, first_half)))
-        x_d_codes, x_d_scales = quantize("x_d", x_d, E4M3X4, R, scales_tag="products3_256")
+        gather_into_words(2)
+        gather_positives(last, first_half)
+        gather_into_words(last)
+        gather_positives(last, second_half)
+        x_d_codes, x_d_scales = quantize("x_d", x_d, E4M3X4, R, scales_tag="products3_0")
 
         w_d_codes = sb.tile([P, SLOTS], U32, name="w_d_codes", align_bytes=64)
-        w_d_scales = []
+        w_d_scales = sb.tile([P, SLOTS], U8, name="w_d_scales", align_bytes=64)
 
-        def quantize_w_d(h, tag):
-            w_d_scales.append(sb.tile([P, HALF], U8, name="w_d_scales%d" % h, tag=tag, align_bytes=64))
-            nc.vector.quantize_mx(out=w_d_codes[:, halves[h]].bitcast(E4M3X4), scales=w_d_scales[h][:], in_=w_d[h][:])
+        def quantize_w_d(h):
+            nc.vector.quantize_mx(out=w_d_codes[:, halves[h]].bitcast(E4M3X4), scales=w_d_scales[:, halves[h]], in_=w_d[h][:])
+
+        quantize_w_d(0)
+        high_second = sb.tile([P, 2, HALF], BF16, name="high_second", tag="x_d", align_bytes=64)
+        for t in (2, last):
+            nc.vector.tensor_copy(high_second[:, t - 2, :], w[t][:].indirect(entries(neg, second_half)))
 
         terms = sb.tile([P, PACK, P], F32, name="terms")
-        spread = [bank(4 + h, "spread%d" % h) for h in range(2)]
+        first_spreads = [bank(n, "spread%d" % k) for k, n in enumerate((4, 6))]
+        second_spread = bank(5, "second_spread")
+        spread = [first_spreads[0][:, 0, :], first_spreads[1][:, 0, :], second_spread[:, 0, :], second_spread[:, 1, :]]
         gp_row = sb.tile([P, R], F32, name="gp_row")
 
-        def spread_factor(h, minus_sp, sig_p):
-            gp = sb.tile([P, 2], F32, name="gp%d" % h)
+        def spread_factor(h, gp):
+            minus_sp = sb.tile([P, 2], F32, name="minus_sp%d" % h, tag="column%d" % h)
+            sig_p = sb.tile([P, 2], F32, name="sig_p%d" % h, tag="column%d" % (h + 1))
             for k in range(2):
                 b = 2 * h + k
                 nc.scalar.activation(terms[:, b, :], dots[h][:, k, :], COPY, scale=minus_us_ts[:, b:b + 1], accum_out=minus_sp[:, k:k + 1])
-            nc.scalar.activation(sig_p, minus_sp, SIGMOID)
+            nc.scalar.activation(sig_p[:], minus_sp[:], SIGMOID)
             for k in range(2):
                 b = 2 * h + k
                 nc.scalar.activation(gp[:, k:k + 1], sig_p[:, k:k + 1], COPY, scale=minus_wu_ts[:, b:b + 1])
-                nc.tensor.transpose(spread[h][:, k, :], gp[:, k:k + 1].to_broadcast([P, P]), ident[:])
+                nc.tensor.transpose(spread[b], gp[:, k:k + 1].to_broadcast([P, P]), ident[:])
 
         def scatter_positives(t, rows, factors):
             nc.vector.tensor_tensor(window[t][:].indirect(entries(pos, rows)), xT[:, t, rows], factors, MULT)
 
         def scatter_low_planes(h):
-            nc.scalar.copy(gp_row[:, halves[h]], flat(spread[h])[:, 0:HALF])
             for t in range(2):
                 scatter_positives(t, halves[h], gp_row[:, halves[h]])
 
@@ -205,26 +215,26 @@ def tile_attend_gspos_ns_w_kernel(tc, x, wT, us, ts, wt, offs, poffs, out):
             rows = [bank(2 * h + k, "score_rows%d_%d" % (h, k)) for k in range(2)]
             for k in range(2):
                 b = 2 * h + k
-                scores = bank(6 + k, "scores%d" % b)
+                scores = bank((4, 6, 0, 1)[b], "scores%d" % b)
                 cols = slice(b * P, (b + 1) * P)
                 nc.tensor.matmul_mx(out=flat(scores),
-                                    lhsT=w_d_codes[:, cols].bitcast(E4M3X4), lhsT_scale=w_d_scales[h][:, k * P:(k + 1) * P],
+                                    lhsT=w_d_codes[:, cols].bitcast(E4M3X4), lhsT_scale=w_d_scales[:, cols],
                                     rhs=x_d_codes[:].bitcast(E4M3X4), rhs_scale=x_d_scales[:], start=True, stop=True)
                 nc.scalar.activation(scaled[:, k, :], flat(scores), COPY, scale=ts_neg[:, b:b + 1])
                 for j in range(PACK):
                     nc.tensor.transpose(rows[j // 2][:, 2 * (j % 2) + k, :], scaled[:, k, j * P:(j + 1) * P], ident[:])
             return rows
 
-        spread_factor(0, w_d[1][:].bitcast(F32)[:, 1:4:2], w_d[0][:].bitcast(F32)[:, 1:4:2])
-        interleave_pair(1, 0, high_first[:])
-        for t in (2, last):
-            nc.vector.tensor_copy(w_d[1][:].rearrange("p (i t) -> p t i", t=PACK)[:, t, :], w[t][:].indirect(entries(neg, second_half)))
-        quantize_w_d(0, "")
-        quantize_w_d(1, "w_d0")
+        gp_first = sb.tile([P, 2], F32, name="gp_first")
+        spread_factor(0, gp_first[:])
+        for b in range(2):
+            nc.scalar.copy(gp_row[:, b * P:(b + 1) * P], spread[b])
         scatter_low_planes(0)
         rows_first = scale_scores(0)
-        second_columns = sb.tile([P, 2, 2], F32, name="second_columns")
-        spread_factor(1, second_columns[:, 0, :], second_columns[:, 1, :])
+        spread_factor(1, w_d[1][:].bitcast(F32)[:, 1:4:2])
+        interleave_pair(1, 1, high_second[:])
+        quantize_w_d(1)
+        nc.scalar.copy(gp_row[:, second_half], flat(second_spread)[:, 0:HALF])
         scatter_low_planes(1)
         for t in (2, last):
             window.append(late.tile([P, T], F32, name="window%d" % t, offset=4 * T * (t - 2), align_bytes=64))
@@ -251,7 +261,7 @@ def tile_attend_gspos_ns_w_kernel(tc, x, wT, us, ts, wt, offs, poffs, out):
         def round_g(h, slot_rows):
             g_slots = sb.tile([P, 2, R], BF16, name="g_slots%d" % h, tag="g_slots%d" % h)
             g = sb.tile([P, HALF * PACK], BF16, name="g%d" % h, align_bytes=64)
-            pairs = bank(h, "pairs%d" % h)
+            pairs = bank((6, 0)[h], "pairs%d" % h)
             for k in range(2):
                 nc.scalar.activation(g_slots[:, k, :].rearrange("p (u s e) -> p u s e", u=2, e=2),
                                      slot_rows[k][:].rearrange("p (u e) s -> p u s e", u=2), COPY,

@@ -11,6 +11,7 @@ U8 = mybir.dt.uint8
 E4M3X4 = mybir.dt.float8_e4m3fn_x4
 E5M2X4 = mybir.dt.float8_e5m2_x4
 MULT = mybir.AluOpType.mult
+ADD = mybir.AluOpType.add
 COPY = mybir.ActivationFunctionType.Copy
 SIGMOID = mybir.ActivationFunctionType.Sigmoid
 
@@ -39,16 +40,17 @@ def tile_attend_gspos_ns_w_kernel(tc, x, wT, us, ts, wt, offs, poffs, out):
         def flat(tile):
             return tile[:].rearrange("p a b -> p (a b)")
 
-        def quantize(name, grouped, fmt, words, scales_tag=""):
-            codes = sb.tile([P, words], U32, name=name + "_codes", align_bytes=64)
-            scales = sb.tile([P, words], U8, name=name + "_scales", tag=scales_tag, align_bytes=64)
-            nc.vector.quantize_mx(out=codes[:].bitcast(fmt), scales=scales[:], in_=grouped[:])
-            return codes, scales
+        def entries(listed, part):
+            return listed[:, part.start // 16:part.stop // 16]
+
+        first_half, second_half, everything = slice(0, HALF), slice(HALF, R), slice(0, R)
+        halves = (first_half, second_half)
+        last = PACK - 1
 
         neg = lists.tile([P, SLOTS // 16], U16, name="neg")
         pos = lists.tile([P, R // 16], U16, name="pos")
-        nc.sync.dma_start(pos[:], poffs)
         nc.sync.dma_start(neg[:], offs)
+        nc.sync.dma_start(pos[:], poffs)
         ts_row = sb.tile([P, T], F32, name="ts_row")
         nc.sync.dma_start(out=ts_row[P - 1:P, :], in_=ts[0:1, :])
         x_sb = sb.tile([P, PACK * D], F32, name="x_sb")
@@ -57,39 +59,38 @@ def tile_attend_gspos_ns_w_kernel(tc, x, wT, us, ts, wt, offs, poffs, out):
             nc.sync.dma_start(out=x_sb[:, 2 * h * D:2 * (h + 1) * D], in_=x_rows[:, 2 * h * D:2 * (h + 1) * D])
 
         uw_rows = sb.tile([P, R], F32, name="uw_rows")
+        ones = sb.tile([P, P], F32, name="ones")
         nc.vector.memset(uw_rows[0:P - 2, :].bitcast(I32), 0)
-        nc.vector.memset(ts_row[0:P - 1, :].bitcast(I32), 0)
-        ones = sb.tile([P, P], F32, name="ones", tag="first")
         nc.vector.memset(ones[:], 1.0)
+        nc.vector.memset(ts_row[0:P - 1, :].bitcast(I32), 0)
         ident = sb.tile([P, P], F32, name="ident")
         nc.gpsimd.affine_select(out=ident[:], in_=ones[:], compare_op=mybir.AluOpType.is_equal, fill=0.0, base=0,
                                 pattern=[[-1, P]], channel_multiplier=1)
         table_warm_up = sb.tile([P, 1], F32, name="table_warm_up")
         nc.scalar.activation(table_warm_up[0:P // 2, :], uw_rows[0:P // 2, 0:1], SIGMOID)
-        window = [sb.tile([P, T], F32, name="window0", tag="first")]
-        nc.gpsimd.memset(window[0][:].bitcast(I32), 0)
+        window = [sb.tile([P, T], F32, name="window%d" % t) for t in range(2)]
+        for t in range(2):
+            nc.vector.memset(window[t][:].bitcast(I32), 0)
 
         w_planes = wT.rearrange("(p t) c -> t p c", t=PACK)
-        w = [sb.tile([P, T], F32, name="w%d" % t, tag="w%d" % t, align_bytes=64) for t in range(PACK)]
+        w = [sb.tile([P, T], F32, name="w%d" % t) for t in range(PACK)]
         nc.sync.dma_start(out=w[0][:], in_=w_planes[0])
         nc.sync.dma_start(out=uw_rows[P - 2:P - 1, :], in_=us.rearrange("r o -> o r"))
         nc.sync.dma_start(out=uw_rows[P - 1:P, :], in_=wt.rearrange("r o -> o r"))
         for t in range(1, PACK):
             nc.sync.dma_start(out=w[t][:], in_=w_planes[t])
 
-        ts_pos_row = sb.tile([P, R], F32, name="ts_pos_row")
         ts_neg_row = sb.tile([P, SLOTS], F32, name="ts_neg_row")
-        nc.vector.tensor_copy(ts_pos_row[:], ts_row[:].indirect(pos[:]))
-        nc.vector.tensor_copy(ts_neg_row[:], ts_row[:].indirect(neg[:]))
+        ts_pos_row = sb.tile([P, R], F32, name="ts_pos_row")
+        nc.scalar.activation(ts_neg_row[:], ts_row[:].indirect(neg[:]), COPY)
+        nc.scalar.activation(ts_pos_row[:], ts_row[:].indirect(pos[:]), COPY)
 
-        x_r = sb.tile([P, D * PACK], BF16, name="x_r", tag="x_r", align_bytes=64)
-        x_r_view = x_r[:].rearrange("p (t m j) -> p m j t", t=PACK, j=PACK)
-        x_sb_view = x_sb[:].rearrange("p (j m t) -> p m j t", j=PACK, t=PACK)
-        nc.vector.tensor_copy(x_r_view[:, :, :, 0:2], x_sb_view[:, :, :, 0:2])
-        nc.scalar.copy(x_r_view[:, :, :, 2:PACK], x_sb_view[:, :, :, 2:PACK])
-        x_r_codes, x_r_scales = quantize("x_r", x_r, E4M3X4, D)
-        window.append(sb.tile([P, T], F32, name="window1", tag="x_r", align_bytes=64))
-        nc.gpsimd.memset(window[1][:].bitcast(I32), 0)
+        x_r = sb.tile([P, D * PACK], BF16, name="x_r", align_bytes=64)
+        nc.vector.tensor_copy(x_r[:].rearrange("p (t m j) -> p m j t", t=PACK, j=PACK),
+                              x_sb[:].rearrange("p (j m t) -> p m j t", j=PACK, t=PACK))
+        x_r_codes = sb.tile([P, D], U32, name="x_r_codes", align_bytes=64)
+        x_r_scales = sb.tile([P, D], U8, name="x_r_scales", align_bytes=64)
+        nc.vector.quantize_mx(out=x_r_codes[:].bitcast(E4M3X4), scales=x_r_scales[:], in_=x_r[:])
 
         x_planes = x_sb[:].rearrange("p (j m t) -> p j t m", j=PACK, t=PACK)
         xT = sb.tile([P, PACK, R], F32, name="xT")
@@ -99,208 +100,177 @@ def tile_attend_gspos_ns_w_kernel(tc, x, wT, us, ts, wt, offs, poffs, out):
                 nc.tensor.transpose(turned_x[:, j, :], x_planes[:, j, t, :], ident[:])
             nc.scalar.copy(xT[:, t, :].rearrange("p (s j) -> p s j", j=PACK), turned_x[:].rearrange("p j s -> p s j"))
 
-        x_d = sb.tile([P, R * PACK], BF16, name="x_d", tag="x_d", align_bytes=64)
-        x_d_view = x_d[:].rearrange("p (j s t) -> p s j t", j=PACK, t=PACK)
-        xT_view = xT[:].rearrange("p t (s j) -> p s j t", j=PACK)
-        for h in range(PACK):
-            part = slice(h * 32, (h + 1) * 32)
-            nc.scalar.copy(x_d_view[:, part], xT_view[:, part])
-
+        turned_neg = bank(3, "turned_neg")
         turned_pos = bank(0, "turned_pos")
-        turned_neg = bank(7, "turned_neg")
-        for b in range(PACK):
-            nc.tensor.transpose(turned_pos[:, b, :], ts_pos_row[:, b * P:(b + 1) * P], ident[:])
-        for b in range(PACK):
-            nc.tensor.transpose(turned_neg[:, b, :], ts_neg_row[:, b * P:(b + 1) * P], ident[:])
         turned_uw = bank(1, "turned_uw")
         dealt_uw = bank(2, "dealt_uw")
+        for b in range(PACK):
+            nc.tensor.transpose(turned_neg[:, b, :], ts_neg_row[:, b * P:(b + 1) * P], ident[:])
+        for b in range(PACK):
+            nc.tensor.transpose(turned_pos[:, b, :], ts_pos_row[:, b * P:(b + 1) * P], ident[:])
         for b in range(PACK):
             nc.tensor.transpose(turned_uw[:, b, :], uw_rows[:, b * P:(b + 1) * P], ident[:])
         for j in range(PACK):
             nc.tensor.transpose(dealt_uw[:, j, :], uw_rows[:].rearrange("p (s j) -> p j s", j=PACK)[:, j, :], ident[:])
-        minus_us = sb.tile([P, PACK], F32, name="minus_us")
-        wt_list = sb.tile([P, PACK], F32, name="wt_list")
-        nc.scalar.activation(minus_us[:], turned_uw[:, :, P - 2], COPY, scale=-1.0)
-        nc.scalar.copy(wt_list[:], turned_uw[:, :, P - 1])
-        minus_us_ts = sb.tile([P, PACK], F32, name="minus_us_ts")
-        minus_wu_ts = sb.tile([P, PACK], F32, name="minus_wu_ts")
-        for b in range(PACK):
-            nc.scalar.activation(minus_us_ts[:, b:b + 1], turned_pos[:, b, P - 1:P], COPY, scale=minus_us[:, b:b + 1])
-        for b in range(PACK):
-            nc.scalar.activation(minus_wu_ts[:, b:b + 1], minus_us_ts[:, b:b + 1], COPY, scale=wt_list[:, b:b + 1])
         ts_neg = sb.tile([P, PACK], F32, name="ts_neg")
         nc.scalar.copy(ts_neg[:], turned_neg[:, :, P - 1])
+        spread_ts = bank(3, "spread_ts")
+        for b in range(PACK):
+            nc.tensor.transpose(spread_ts[:, b, :], ts_neg[:, b:b + 1].to_broadcast([P, P]), ident[:])
+        minus_ts_pos = sb.tile([P, PACK], F32, name="minus_ts_pos")
+        nc.scalar.activation(minus_ts_pos[:], turned_pos[:, :, P - 1], COPY, scale=-1.0)
+        uw_list = sb.tile([P, 2, PACK], F32, name="uw_list")
+        nc.scalar.copy(uw_list[:], turned_uw[:, :, P - 2:P].rearrange("p b v -> p v b"))
         uw_col = sb.tile([P, 2, PACK], F32, name="uw_col")
         nc.scalar.copy(uw_col[:], dealt_uw[:, :, P - 2:P].rearrange("p j v -> p v j"))
+        ts_all = sb.tile([P, SLOTS], F32, name="ts_all")
+        nc.scalar.copy(ts_all[:], flat(spread_ts))
         us_col = uw_col[:, 0, :]
         wu = sb.tile([P, PACK], F32, name="wu")
+        minus_us_ts = sb.tile([P, PACK], F32, name="minus_us_ts")
+        minus_wu_ts = sb.tile([P, PACK], F32, name="minus_wu_ts")
         nc.gpsimd.tensor_tensor(wu[:], uw_col[:, 1, :], us_col, MULT)
+        nc.gpsimd.tensor_tensor(minus_us_ts[:], minus_ts_pos[:], uw_list[:, 0, :], MULT)
+        nc.gpsimd.tensor_tensor(minus_wu_ts[:], minus_us_ts[:], uw_list[:, 1, :], MULT)
 
-        last = PACK - 1
-        first_half, second_half, all_rows = slice(0, HALF), slice(HALF, R), slice(0, R)
-        halves = (first_half, second_half)
-        w_d = [sb.tile([P, HALF * PACK], BF16, name="w_d0", align_bytes=64),
-               late.tile([P, HALF * PACK], BF16, name="w_d1", offset=4 * T - PACK * HALF, align_bytes=64)]
-        low_planes = sb.tile([P, 2, SLOTS], BF16, name="low_planes")
-        dots = [bank(h, "dots%d" % h) for h in range(2)]
+        w_d = [sb.tile([P, HALF * PACK], BF16, name="w_d%d" % h, align_bytes=64) for h in range(2)]
+        pairs = [sb.tile([P, 2, SLOTS], BF16, name="pair%d" % u) for u in range(2)]
+        dots = bank(0, "dots")
 
-        def entries(listed, part):
-            return listed[:, part.start // 16:part.stop // 16]
+        def gather_positives(t):
+            products = sb.tile([P, R], F32, name="products%d" % t)
+            nc.vector.tensor_tensor(products[:], w[t][:].indirect(pos[:]), xT[:, t, :], MULT)
+            for b in range(PACK):
+                nc.tensor.matmul(dots[:, b, :], lhsT=products[:, b * P:(b + 1) * P], rhs=ident[:], is_transpose=True,
+                                 start=(t == 0 and b == 0), stop=(t == last and b == last))
 
-        def interleave_pair(u, h, planes):
+        def gather_negatives(t, slots):
+            nc.scalar.activation(pairs[t // 2][:, t % 2, slots], w[t][:].indirect(entries(neg, slots)), COPY)
+
+        def interleave_pair(u, h):
             nc.scalar.copy(w_d[h][:].rearrange("p (c i t) -> p c t i", i=PACK, t=PACK)[:, :, 2 * u:2 * u + 2, :],
-                           planes.rearrange("p t (c i) -> p c t i", i=PACK))
+                           pairs[u][:, :, halves[h]].rearrange("p t (c i) -> p c t i", i=PACK))
 
-        def gather_positives(t, rows):
-            name = "products%d_%d" % (t, rows.start)
-            products = sb.tile([P, rows.stop - rows.start], F32, name=name, tag=name, align_bytes=64)
-            nc.vector.tensor_tensor(products[:], w[t][:].indirect(entries(pos, rows)), xT[:, t, rows], MULT)
-            for k, b in enumerate(range(rows.start // P, rows.stop // P)):
-                nc.tensor.matmul(dots[b // 2][:, b % 2, :], lhsT=products[:, k * P:(k + 1) * P], rhs=ident[:], is_transpose=True,
-                                 start=(t == 0 and b % 2 == 0), stop=(t == last and b % 2 == 1))
+        x_d = sb.tile([P, R * PACK], BF16, name="x_d", align_bytes=64)
+        x_d_codes = sb.tile([P, R], U32, name="x_d_codes", align_bytes=64)
+        x_d_scales = sb.tile([P, R], U8, name="x_d_scales", align_bytes=64)
+        factors = sb.tile([P, PACK, SLOTS], F32, name="factors")
 
-        for t in range(2):
-            gather_positives(t, all_rows)
-            nc.vector.tensor_copy(low_planes[:, t, :], w[t][:].indirect(neg[:]))
+        gather_positives(0)
+        gather_negatives(0, everything)
+        nc.vector.tensor_copy(x_d[:].rearrange("p (j s t) -> p s j t", j=PACK, t=PACK),
+                              xT[:].rearrange("p t (s j) -> p s j t", j=PACK))
+        gather_positives(1)
+        gather_negatives(1, everything)
+        nc.vector.quantize_mx(out=x_d_codes[:].bitcast(E4M3X4), scales=x_d_scales[:], in_=x_d[:])
         for h in range(2):
-            interleave_pair(0, h, low_planes[:, :, halves[h]])
-        def gather_into_words(t):
-            nc.vector.tensor_copy(w_d[0][:].rearrange("p (i t) -> p t i", t=PACK)[:, t, :], w[t][:].indirect(entries(neg, first_half)))
-
-        gather_positives(2, all_rows)
-        gather_into_words(2)
-        gather_positives(last, first_half)
-        gather_into_words(last)
-        gather_positives(last, second_half)
-        x_d_codes, x_d_scales = quantize("x_d", x_d, E4M3X4, R, scales_tag="products3_0")
+            interleave_pair(0, h)
+        gather_positives(2)
+        gather_negatives(2, everything)
+        for j in range(PACK):
+            nc.vector.tensor_scalar(factors[:, j, :], ts_all[:], wu[:, j:j + 1], None, MULT)
+        gather_positives(last)
+        for h in range(2):
+            gather_negatives(last, halves[h])
+            interleave_pair(1, h)
 
         w_d_codes = sb.tile([P, SLOTS], U32, name="w_d_codes", align_bytes=64)
         w_d_scales = sb.tile([P, SLOTS], U8, name="w_d_scales", align_bytes=64)
+        g_codes = sb.tile([P, SLOTS], U32, name="g_codes", align_bytes=64)
+        g_scales = sb.tile([P, SLOTS], U8, name="g_scales", align_bytes=64)
+        sig_second = sb.tile([P, PACK * HALF + HALF], F32, name="sig_second")
+        sig_first = sb.tile([P, PACK * HALF], F32, name="sig_first")
+        sig = [tile[:, 0:PACK * HALF].rearrange("p (j i) -> p j i", j=PACK) for tile in (sig_first, sig_second)]
+        gp_row = sig_second[:, PACK * HALF - HALF:PACK * HALF + HALF]
+        scaled = [sb.tile([P, PACK, HALF], F32, name="scaled%d" % h) for h in range(2)]
+        g = [sb.tile([P, HALF * PACK], BF16, name="g0", align_bytes=64),
+             late.tile([P, HALF * PACK], BF16, name="g1", offset=4 * T - PACK * HALF, align_bytes=64)]
 
-        def quantize_w_d(h):
+        def scores(h):
             nc.vector.quantize_mx(out=w_d_codes[:, halves[h]].bitcast(E4M3X4), scales=w_d_scales[:, halves[h]], in_=w_d[h][:])
+            banks = [bank(4 + 2 * h + k, "scores%d_%d" % (h, k)) for k in range(2)]
+            for j in range(PACK):
+                rows = slice(j * P, (j + 1) * P)
+                nc.tensor.matmul_mx(out=flat(banks[j // 2])[:, halves[j % 2]],
+                                    lhsT=x_d_codes[:, rows].bitcast(E4M3X4), lhsT_scale=x_d_scales[:, rows],
+                                    rhs=w_d_codes[:, halves[h]].bitcast(E4M3X4), rhs_scale=w_d_scales[:, halves[h]],
+                                    start=True, stop=True)
+            return banks
 
-        quantize_w_d(0)
-        high_second = sb.tile([P, 2, HALF], BF16, name="high_second", tag="x_d", align_bytes=64)
-        for t in (2, last):
-            nc.vector.tensor_copy(high_second[:, t - 2, :], w[t][:].indirect(entries(neg, second_half)))
+        def squash(h, k, scores_bank):
+            nc.vector.tensor_tensor(scaled[h][:, 2 * k:2 * k + 2, :], flat(scores_bank).rearrange("p (j i) -> p j i", j=2),
+                                    ts_all[:, halves[h]].unsqueeze(1).to_broadcast([P, 2, HALF]), MULT)
+            for j in (2 * k, 2 * k + 1):
+                nc.scalar.activation(sig[h][:, j, :], scaled[h][:, j, :], SIGMOID, scale=us_col[:, j:j + 1])
 
-        terms = sb.tile([P, PACK, P], F32, name="terms")
-        first_spreads = [bank(n, "spread%d" % k) for k, n in enumerate((4, 6))]
-        second_spread = bank(5, "second_spread")
-        spread = [first_spreads[0][:, 0, :], first_spreads[1][:, 0, :], second_spread[:, 0, :], second_spread[:, 1, :]]
-        gp_row = sb.tile([P, R], F32, name="gp_row")
+        def weigh(h):
+            nc.vector.tensor_tensor(g[h][:].rearrange("p (c i j) -> p c j i", i=PACK, j=PACK),
+                                    sig[h].rearrange("p j (c i) -> p c j i", i=PACK),
+                                    factors[:, :, halves[h]].rearrange("p j (c i) -> p c j i", i=PACK), MULT)
 
-        def spread_factor(h, gp):
-            minus_sp = sb.tile([P, 2], F32, name="minus_sp%d" % h, tag="column%d" % h)
-            sig_p = sb.tile([P, 2], F32, name="sig_p%d" % h, tag="column%d" % (h + 1))
-            for k in range(2):
-                b = 2 * h + k
-                nc.scalar.activation(terms[:, b, :], dots[h][:, k, :], COPY, scale=minus_us_ts[:, b:b + 1], accum_out=minus_sp[:, k:k + 1])
-            nc.scalar.activation(sig_p[:], minus_sp[:], SIGMOID)
-            for k in range(2):
-                b = 2 * h + k
-                nc.scalar.activation(gp[:, k:k + 1], sig_p[:, k:k + 1], COPY, scale=minus_wu_ts[:, b:b + 1])
-                nc.tensor.transpose(spread[b], gp[:, k:k + 1].to_broadcast([P, P]), ident[:])
+        def quantize_g(h):
+            nc.vector.quantize_mx(out=g_codes[:, halves[h]].bitcast(E5M2X4), scales=g_scales[:, halves[h]], in_=g[h][:])
 
-        def scatter_positives(t, rows, factors):
-            nc.vector.tensor_tensor(window[t][:].indirect(entries(pos, rows)), xT[:, t, rows], factors, MULT)
+        def scatter_negatives(t, slots, n):
+            name = "%d_%d" % (t, slots.start)
+            width = slots.stop - slots.start
+            sums = flat(bank(n, "sums" + name))[:, 0:width]
+            cols = slice(t * P, (t + 1) * P)
+            nc.tensor.matmul_mx(out=sums,
+                                lhsT=x_r_codes[:, cols].bitcast(E4M3X4), lhsT_scale=x_r_scales[:, cols],
+                                rhs=g_codes[:, slots].bitcast(E5M2X4), rhs_scale=g_scales[:, slots], start=True, stop=True)
+            dn = sb.tile([P, width], F32, name="dn" + name, tag="dn")
+            nc.scalar.copy(dn[:], sums)
+            for start in range(slots.start, slots.stop, HALF):
+                part = slice(start, start + HALF)
+                nc.scalar.activation(window[t][:].indirect(entries(neg, part)),
+                                     dn[:, start - slots.start:start - slots.start + HALF], COPY)
 
-        def scatter_low_planes(h):
-            for t in range(2):
-                scatter_positives(t, halves[h], gp_row[:, halves[h]])
+        def scatter_positives(t, rows):
+            nc.vector.tensor_tensor(window[t][:].indirect(entries(pos, rows)), xT[:, t, rows], gp_row[:, rows], MULT)
 
-        def scale_scores(h):
-            scaled = sb.tile([P, 2, R], F32, name="scaled%d" % h)
-            rows = [bank(2 * h + k, "score_rows%d_%d" % (h, k)) for k in range(2)]
-            for k in range(2):
-                b = 2 * h + k
-                scores = bank((4, 6, 0, 1)[b], "scores%d" % b)
-                cols = slice(b * P, (b + 1) * P)
-                nc.tensor.matmul_mx(out=flat(scores),
-                                    lhsT=w_d_codes[:, cols].bitcast(E4M3X4), lhsT_scale=w_d_scales[:, cols],
-                                    rhs=x_d_codes[:].bitcast(E4M3X4), rhs_scale=x_d_scales[:], start=True, stop=True)
-                nc.scalar.activation(scaled[:, k, :], flat(scores), COPY, scale=ts_neg[:, b:b + 1])
-                for j in range(PACK):
-                    nc.tensor.transpose(rows[j // 2][:, 2 * (j % 2) + k, :], scaled[:, k, j * P:(j + 1) * P], ident[:])
-            return rows
+        out_planes = out.rearrange("(p t) c -> t p c", t=PACK)
 
-        gp_first = sb.tile([P, 2], F32, name="gp_first")
-        spread_factor(0, gp_first[:])
-        for b in range(2):
-            nc.scalar.copy(gp_row[:, b * P:(b + 1) * P], spread[b])
-        scatter_low_planes(0)
-        rows_first = scale_scores(0)
-        spread_factor(1, w_d[1][:].bitcast(F32)[:, 1:4:2])
-        interleave_pair(1, 1, high_second[:])
-        quantize_w_d(1)
-        nc.scalar.copy(gp_row[:, second_half], flat(second_spread)[:, 0:HALF])
-        scatter_low_planes(1)
+        def store(t):
+            nc.sync.dma_start(out=out_planes[t], in_=window[t][:])
+
+        first_scores = scores(0)
+        s0 = sb.tile([P, PACK], F32, name="s0")
+        nc.vector.tensor_reduce(s0[:], dots[:], mybir.AxisListType.X, ADD)
+        squash(0, 0, first_scores[0])
+        second_scores = scores(1)
+        squash(0, 1, first_scores[1])
+
+        sig_p = sb.tile([P, PACK], F32, name="sig_p")
+        gp = sb.tile([P, PACK], F32, name="gp")
+        spread_gp = [bank(1 + h, "spread_gp%d" % h) for h in range(2)]
+        for b in range(PACK):
+            nc.scalar.activation(sig_p[:, b:b + 1], s0[:, b:b + 1], SIGMOID, scale=minus_us_ts[:, b:b + 1])
+        for b in range(PACK):
+            nc.scalar.activation(gp[:, b:b + 1], sig_p[:, b:b + 1], COPY, scale=minus_wu_ts[:, b:b + 1])
+            nc.tensor.transpose(spread_gp[b // 2][:, b % 2, :], gp[:, b:b + 1].to_broadcast([P, P]), ident[:])
+
+        squash(1, 0, second_scores[0])
+        weigh(0)
+        squash(1, 1, second_scores[1])
+        quantize_g(0)
+        nc.scalar.copy(gp_row[:, second_half], flat(spread_gp[1])[:, 0:HALF])
+        scatter_negatives(0, first_half, 3)
+        weigh(1)
+        nc.vector.tensor_copy(gp_row[:, first_half], flat(spread_gp[0])[:, 0:HALF])
+        quantize_g(1)
         for t in (2, last):
             window.append(late.tile([P, T], F32, name="window%d" % t, offset=4 * T * (t - 2), align_bytes=64))
             nc.gpsimd.memset(window[t][:].bitcast(I32), 0)
-        scatter_positives(2, all_rows, gp_row[:])
-
-        g_codes = sb.tile([P, SLOTS], U32, name="g_codes", tag="w0", align_bytes=64)
-        g_scales = sb.tile([P, SLOTS], U8, name="g_scales", tag="w1", align_bytes=64)
-        nc.gpsimd.memset(g_codes[:, second_half].bitcast(I32), 0)
-        nc.gpsimd.memset(g_scales[:, second_half].bitcast(I32), 0)
-
-        def weigh(h, rows):
-            sig = sb.tile([P, PACK, HALF], F32, name="sig%d" % h)
-            weighted = sb.tile([P, PACK, HALF], F32, name="weighted%d" % h, tag="weighted%d" % h)
-            slot_rows = [bank(4 + 2 * h + k, "slot_rows%d_%d" % (h, k)) for k in range(2)]
-            for j in range(PACK):
-                nc.scalar.activation(sig[:, j, :], flat(rows[j // 2])[:, (j % 2) * HALF:(j % 2 + 1) * HALF], SIGMOID,
-                                     scale=us_col[:, j:j + 1])
-                nc.scalar.activation(weighted[:, j, :], sig[:, j, :], COPY, scale=wu[:, j:j + 1])
-                for k in range(2):
-                    nc.tensor.transpose(slot_rows[k][:, j, :], weighted[:, j, k * P:(k + 1) * P], ident[:])
-            return slot_rows
-
-        def round_g(h, slot_rows):
-            g_slots = sb.tile([P, 2, R], BF16, name="g_slots%d" % h, tag="g_slots%d" % h)
-            g = sb.tile([P, HALF * PACK], BF16, name="g%d" % h, align_bytes=64)
-            pairs = bank((6, 0)[h], "pairs%d" % h)
-            for k in range(2):
-                nc.scalar.activation(g_slots[:, k, :].rearrange("p (u s e) -> p u s e", u=2, e=2),
-                                     slot_rows[k][:].rearrange("p (u e) s -> p u s e", u=2), COPY,
-                                     scale=ts_neg[:, 2 * h + k:2 * h + k + 1])
-                words = g_slots[:, k, :].bitcast(F32)
-                for u in range(2):
-                    nc.tensor.transpose(pairs[:, 2 * k + u, :], words[:, u * P:(u + 1) * P], ident[:])
-            nc.scalar.copy(g[:].bitcast(F32).rearrange("p (k i u) -> p k i u", k=2, u=2),
-                           pairs[:].rearrange("p (k u) i -> p k i u", u=2))
-            return g
-
-        def quantize_g(g, slots):
-            nc.vector.quantize_mx(out=g_codes[:, slots].bitcast(E5M2X4), scales=g_scales[:, slots], in_=g[:])
-
-        def product(t, n, name):
-            sums = bank(n, name)
-            cols = slice(t * P, (t + 1) * P)
-            nc.tensor.matmul_mx(out=flat(sums),
-                                lhsT=x_r_codes[:, cols].bitcast(E4M3X4), lhsT_scale=x_r_scales[:, cols],
-                                rhs=g_codes[:].bitcast(E5M2X4), rhs_scale=g_scales[:], start=True, stop=True)
-            return flat(sums)
-
-        def scatter_negatives(t, sums, slots, name, tag=""):
-            dn = sb.tile([P, slots.stop - slots.start], F32, name=name, tag=tag)
-            nc.scalar.copy(dn[:], sums[:, slots])
-            nc.vector.tensor_copy(window[t][:].indirect(entries(neg, slots)), dn[:])
-
-        quantize_g(round_g(0, weigh(0, rows_first)), first_half)
-        gp_last = sb.tile([P, R], F32, name="gp_last", tag="weighted0")
-        nc.sync.dma_start(out=gp_last[:], in_=gp_row[:])
-        scatter_positives(last, all_rows, gp_last[:])
-        slot_rows = weigh(1, scale_scores(1))
-        scatter_negatives(0, product(0, 3, "early0"), first_half, "dn0_first")
-        g_second = round_g(1, slot_rows)
-        early = product(1, 7, "early1")
-        quantize_g(g_second, second_half)
-        scatter_negatives(1, early, first_half, "dn1_first", tag="g_slots1")
-        out_planes = out.rearrange("(p t) c -> t p c", t=PACK)
-        for t in range(PACK):
-            sums = product(t, (2, 4, 5, 6)[t], "sums%d" % t)
-            scatter_negatives(t, sums, second_half if t < 2 else all_rows, "dn%d" % t)
-            nc.sync.dma_start(out=out_planes[t], in_=window[t][:])
+        scatter_positives(1, everything)
+        scatter_negatives(0, second_half, 0)
+        scatter_positives(0, everything)
+        store(0)
+        scatter_negatives(2, everything, 4)
+        scatter_negatives(1, everything, 5)
+        store(1)
+        scatter_positives(last, everything)
+        scatter_positives(2, everything)
+        store(2)
+        scatter_negatives(last, everything, 6)
+        store(last)

@@ -11,7 +11,6 @@ U8 = mybir.dt.uint8
 E4M3X4 = mybir.dt.float8_e4m3fn_x4
 E5M2X4 = mybir.dt.float8_e5m2_x4
 MULT = mybir.AluOpType.mult
-ADD = mybir.AluOpType.add
 COPY = mybir.ActivationFunctionType.Copy
 SIGMOID = mybir.ActivationFunctionType.Sigmoid
 
@@ -58,18 +57,18 @@ def tile_attend_gspos_ns_w_kernel(tc, x, wT, us, ts, wt, offs, poffs, out):
         for h in range(2):
             nc.sync.dma_start(out=x_sb[:, 2 * h * D:2 * (h + 1) * D], in_=x_rows[:, 2 * h * D:2 * (h + 1) * D])
 
-        uw_rows = sb.tile([P, R], F32, name="uw_rows")
         ones = sb.tile([P, P], F32, name="ones")
-        nc.vector.memset(uw_rows[0:P - 2, :].bitcast(I32), 0)
+        uw_rows = sb.tile([P, R], F32, name="uw_rows")
         nc.vector.memset(ones[:], 1.0)
         nc.vector.memset(ts_row[0:P - 1, :].bitcast(I32), 0)
+        nc.vector.memset(uw_rows[0:P - 2, :].bitcast(I32), 0)
         ident = sb.tile([P, P], F32, name="ident")
         nc.gpsimd.affine_select(out=ident[:], in_=ones[:], compare_op=mybir.AluOpType.is_equal, fill=0.0, base=0,
                                 pattern=[[-1, P]], channel_multiplier=1)
         table_warm_up = sb.tile([P, 1], F32, name="table_warm_up")
-        nc.scalar.activation(table_warm_up[0:P // 2, :], uw_rows[0:P // 2, 0:1], SIGMOID)
-        window = [sb.tile([P, T], F32, name="window%d" % t) for t in range(2)]
-        for t in range(2):
+        nc.scalar.activation(table_warm_up[0:P // 2, :], ones[0:P // 2, 0:1], SIGMOID)
+        window = {t: sb.tile([P, T], F32, name="window%d" % t) for t in (0, last)}
+        for t in (0, last):
             nc.vector.memset(window[t][:].bitcast(I32), 0)
 
         w_planes = wT.rearrange("(p t) c -> t p c", t=PACK)
@@ -79,15 +78,20 @@ def tile_attend_gspos_ns_w_kernel(tc, x, wT, us, ts, wt, offs, poffs, out):
         nc.sync.dma_start(out=uw_rows[P - 1:P, :], in_=wt.rearrange("r o -> o r"))
         for t in range(1, PACK):
             nc.sync.dma_start(out=w[t][:], in_=w_planes[t])
+        us_col = sb.tile([P, PACK], F32, name="us_col")
+        wt_col = sb.tile([P, PACK], F32, name="wt_col")
+        nc.sync.dma_start(out=us_col[:], in_=us.rearrange("(s j) o -> s (j o)", j=PACK))
+        nc.sync.dma_start(out=wt_col[:], in_=wt.rearrange("(s j) o -> s (j o)", j=PACK))
 
         ts_neg_row = sb.tile([P, SLOTS], F32, name="ts_neg_row")
         ts_pos_row = sb.tile([P, R], F32, name="ts_pos_row")
         nc.scalar.activation(ts_neg_row[:], ts_row[:].indirect(neg[:]), COPY)
-        nc.scalar.activation(ts_pos_row[:], ts_row[:].indirect(pos[:]), COPY)
+        nc.vector.tensor_copy(ts_pos_row[:], ts_row[:].indirect(pos[:]))
 
         x_r = sb.tile([P, D * PACK], BF16, name="x_r", align_bytes=64)
-        nc.vector.tensor_copy(x_r[:].rearrange("p (t m j) -> p m j t", t=PACK, j=PACK),
-                              x_sb[:].rearrange("p (j m t) -> p m j t", j=PACK, t=PACK))
+        for h in range(2):
+            nc.vector.tensor_copy(x_r[:].rearrange("p (t m j) -> p m j t", t=PACK, j=PACK)[:, :, 2 * h:2 * h + 2, :],
+                                  x_sb[:].rearrange("p (j m t) -> p m j t", j=PACK, t=PACK)[:, :, 2 * h:2 * h + 2, :])
         x_r_codes = sb.tile([P, D], U32, name="x_r_codes", align_bytes=64)
         x_r_scales = sb.tile([P, D], U8, name="x_r_scales", align_bytes=64)
         nc.vector.quantize_mx(out=x_r_codes[:].bitcast(E4M3X4), scales=x_r_scales[:], in_=x_r[:])
@@ -95,47 +99,33 @@ def tile_attend_gspos_ns_w_kernel(tc, x, wT, us, ts, wt, offs, poffs, out):
         x_planes = x_sb[:].rearrange("p (j m t) -> p j t m", j=PACK, t=PACK)
         xT = sb.tile([P, PACK, R], F32, name="xT")
         for t in range(PACK):
-            turned_x = bank(4 + t, "turned_x%d" % t)
+            turned_x = bank(4 + t % 2, "turned_x%d" % t)
             for j in range(PACK):
                 nc.tensor.transpose(turned_x[:, j, :], x_planes[:, j, t, :], ident[:])
             nc.scalar.copy(xT[:, t, :].rearrange("p (s j) -> p s j", j=PACK), turned_x[:].rearrange("p j s -> p s j"))
 
-        turned_neg = bank(3, "turned_neg")
-        turned_pos = bank(0, "turned_pos")
-        turned_uw = bank(1, "turned_uw")
-        dealt_uw = bank(2, "dealt_uw")
+        turned_neg = bank(4, "turned_neg")
         for b in range(PACK):
             nc.tensor.transpose(turned_neg[:, b, :], ts_neg_row[:, b * P:(b + 1) * P], ident[:])
-        for b in range(PACK):
-            nc.tensor.transpose(turned_pos[:, b, :], ts_pos_row[:, b * P:(b + 1) * P], ident[:])
-        for b in range(PACK):
-            nc.tensor.transpose(turned_uw[:, b, :], uw_rows[:, b * P:(b + 1) * P], ident[:])
-        for j in range(PACK):
-            nc.tensor.transpose(dealt_uw[:, j, :], uw_rows[:].rearrange("p (s j) -> p j s", j=PACK)[:, j, :], ident[:])
         ts_neg = sb.tile([P, PACK], F32, name="ts_neg")
         nc.scalar.copy(ts_neg[:], turned_neg[:, :, P - 1])
+        turned_uw = bank(5, "turned_uw")
+        for b in range(PACK):
+            nc.tensor.transpose(turned_uw[:, b, :], uw_rows[:, b * P:(b + 1) * P], ident[:])
+        uw_list = sb.tile([P, 2, PACK], F32, name="uw_list")
+        nc.scalar.copy(uw_list[:], turned_uw[:, :, P - 2:P].rearrange("p b v -> p v b"))
         spread_ts = bank(3, "spread_ts")
         for b in range(PACK):
             nc.tensor.transpose(spread_ts[:, b, :], ts_neg[:, b:b + 1].to_broadcast([P, P]), ident[:])
-        minus_ts_pos = sb.tile([P, PACK], F32, name="minus_ts_pos")
-        nc.scalar.activation(minus_ts_pos[:], turned_pos[:, :, P - 1], COPY, scale=-1.0)
-        uw_list = sb.tile([P, 2, PACK], F32, name="uw_list")
-        nc.scalar.copy(uw_list[:], turned_uw[:, :, P - 2:P].rearrange("p b v -> p v b"))
-        uw_col = sb.tile([P, 2, PACK], F32, name="uw_col")
-        nc.scalar.copy(uw_col[:], dealt_uw[:, :, P - 2:P].rearrange("p j v -> p v j"))
+        turned_pos = bank(4, "turned_pos")
+        for b in range(PACK):
+            nc.tensor.transpose(turned_pos[:, b, :], ts_pos_row[:, b * P:(b + 1) * P], ident[:])
         ts_all = sb.tile([P, SLOTS], F32, name="ts_all")
         nc.scalar.copy(ts_all[:], flat(spread_ts))
-        us_col = uw_col[:, 0, :]
-        wu = sb.tile([P, PACK], F32, name="wu")
-        minus_us_ts = sb.tile([P, PACK], F32, name="minus_us_ts")
-        minus_wu_ts = sb.tile([P, PACK], F32, name="minus_wu_ts")
-        nc.gpsimd.tensor_tensor(wu[:], uw_col[:, 1, :], us_col, MULT)
-        nc.gpsimd.tensor_tensor(minus_us_ts[:], minus_ts_pos[:], uw_list[:, 0, :], MULT)
-        nc.gpsimd.tensor_tensor(minus_wu_ts[:], minus_us_ts[:], uw_list[:, 1, :], MULT)
 
-        w_d = [sb.tile([P, HALF * PACK], BF16, name="w_d%d" % h, align_bytes=64) for h in range(2)]
-        pairs = [sb.tile([P, 2, SLOTS], BF16, name="pair%d" % u) for u in range(2)]
-        dots = bank(0, "dots")
+        w_d = [sb.tile([P, HALF * PACK], BF16, name="w_d%d" % h, tag="w_d%d" % h, align_bytes=64) for h in range(2)]
+        pairs = [sb.tile([P, 2, SLOTS], BF16, name="pair%d" % u, tag="pair%d" % u) for u in range(2)]
+        dots = bank(3, "dots")
 
         def gather_positives(t):
             products = sb.tile([P, R], F32, name="products%d" % t)
@@ -147,32 +137,33 @@ def tile_attend_gspos_ns_w_kernel(tc, x, wT, us, ts, wt, offs, poffs, out):
         def gather_negatives(t, slots):
             nc.scalar.activation(pairs[t // 2][:, t % 2, slots], w[t][:].indirect(entries(neg, slots)), COPY)
 
-        def interleave_pair(u, h):
-            nc.scalar.copy(w_d[h][:].rearrange("p (c i t) -> p c t i", i=PACK, t=PACK)[:, :, 2 * u:2 * u + 2, :],
-                           pairs[u][:, :, halves[h]].rearrange("p t (c i) -> p c t i", i=PACK))
+        def interleave_pair(u, h, copy):
+            copy(w_d[h][:].rearrange("p (c i t) -> p c t i", i=PACK, t=PACK)[:, :, 2 * u:2 * u + 2, :],
+                 pairs[u][:, :, halves[h]].rearrange("p t (c i) -> p c t i", i=PACK))
 
         x_d = sb.tile([P, R * PACK], BF16, name="x_d", align_bytes=64)
         x_d_codes = sb.tile([P, R], U32, name="x_d_codes", align_bytes=64)
         x_d_scales = sb.tile([P, R], U8, name="x_d_scales", align_bytes=64)
-        factors = sb.tile([P, PACK, SLOTS], F32, name="factors")
+
+        def round_x_d(u):
+            nc.vector.tensor_copy(x_d[:].rearrange("p (j s t) -> p s j t", j=PACK, t=PACK)[:, :, :, 2 * u:2 * u + 2],
+                                  xT[:, 2 * u:2 * u + 2, :].rearrange("p t (s j) -> p s j t", j=PACK))
 
         gather_positives(0)
         gather_negatives(0, everything)
-        nc.vector.tensor_copy(x_d[:].rearrange("p (j s t) -> p s j t", j=PACK, t=PACK),
-                              xT[:].rearrange("p t (s j) -> p s j t", j=PACK))
+        round_x_d(0)
         gather_positives(1)
         gather_negatives(1, everything)
-        nc.vector.quantize_mx(out=x_d_codes[:].bitcast(E4M3X4), scales=x_d_scales[:], in_=x_d[:])
+        round_x_d(1)
         for h in range(2):
-            interleave_pair(0, h)
+            interleave_pair(0, h, nc.vector.tensor_copy)
+        nc.vector.quantize_mx(out=x_d_codes[:].bitcast(E4M3X4), scales=x_d_scales[:], in_=x_d[:])
         gather_positives(2)
         gather_negatives(2, everything)
-        for j in range(PACK):
-            nc.vector.tensor_scalar(factors[:, j, :], ts_all[:], wu[:, j:j + 1], None, MULT)
         gather_positives(last)
         for h in range(2):
             gather_negatives(last, halves[h])
-            interleave_pair(1, h)
+            interleave_pair(1, h, nc.scalar.copy)
 
         w_d_codes = sb.tile([P, SLOTS], U32, name="w_d_codes", align_bytes=64)
         w_d_scales = sb.tile([P, SLOTS], U8, name="w_d_scales", align_bytes=64)
@@ -182,13 +173,12 @@ def tile_attend_gspos_ns_w_kernel(tc, x, wT, us, ts, wt, offs, poffs, out):
         sig_first = sb.tile([P, PACK * HALF], F32, name="sig_first")
         sig = [tile[:, 0:PACK * HALF].rearrange("p (j i) -> p j i", j=PACK) for tile in (sig_first, sig_second)]
         gp_row = sig_second[:, PACK * HALF - HALF:PACK * HALF + HALF]
-        scaled = [sb.tile([P, PACK, HALF], F32, name="scaled%d" % h) for h in range(2)]
-        g = [sb.tile([P, HALF * PACK], BF16, name="g0", align_bytes=64),
-             late.tile([P, HALF * PACK], BF16, name="g1", offset=4 * T - PACK * HALF, align_bytes=64)]
+        scaled = [sb.tile([P, PACK, HALF], F32, name="scaled%d" % h, tag="scaled%d" % h) for h in range(2)]
+        g = [late.tile([P, HALF * PACK], BF16, name="g%d" % h, offset=4 * T - PACK * HALF, align_bytes=64) for h in range(2)]
 
         def scores(h):
             nc.vector.quantize_mx(out=w_d_codes[:, halves[h]].bitcast(E4M3X4), scales=w_d_scales[:, halves[h]], in_=w_d[h][:])
-            banks = [bank(4 + 2 * h + k, "scores%d_%d" % (h, k)) for k in range(2)]
+            banks = [bank((0, 6)[h] + k, "scores%d_%d" % (h, k)) for k in range(2)]
             for j in range(PACK):
                 rows = slice(j * P, (j + 1) * P)
                 nc.tensor.matmul_mx(out=flat(banks[j // 2])[:, halves[j % 2]],
@@ -206,25 +196,24 @@ def tile_attend_gspos_ns_w_kernel(tc, x, wT, us, ts, wt, offs, poffs, out):
         def weigh(h):
             nc.vector.tensor_tensor(g[h][:].rearrange("p (c i j) -> p c j i", i=PACK, j=PACK),
                                     sig[h].rearrange("p j (c i) -> p c j i", i=PACK),
-                                    factors[:, :, halves[h]].rearrange("p j (c i) -> p c j i", i=PACK), MULT)
+                                    factors[h][:].rearrange("p j (c i) -> p c j i", i=PACK), MULT)
 
         def quantize_g(h):
             nc.vector.quantize_mx(out=g_codes[:, halves[h]].bitcast(E5M2X4), scales=g_scales[:, halves[h]], in_=g[h][:])
 
-        def scatter_negatives(t, slots, n):
-            name = "%d_%d" % (t, slots.start)
-            width = slots.stop - slots.start
-            sums = flat(bank(n, "sums" + name))[:, 0:width]
+        def product(t, h, n, tag, copy):
+            name = "%d_%d" % (t, h)
+            sums = flat(bank(n, "sums" + name))[:, first_half]
             cols = slice(t * P, (t + 1) * P)
             nc.tensor.matmul_mx(out=sums,
                                 lhsT=x_r_codes[:, cols].bitcast(E4M3X4), lhsT_scale=x_r_scales[:, cols],
-                                rhs=g_codes[:, slots].bitcast(E5M2X4), rhs_scale=g_scales[:, slots], start=True, stop=True)
-            dn = sb.tile([P, width], F32, name="dn" + name, tag="dn")
-            nc.scalar.copy(dn[:], sums)
-            for start in range(slots.start, slots.stop, HALF):
-                part = slice(start, start + HALF)
-                nc.scalar.activation(window[t][:].indirect(entries(neg, part)),
-                                     dn[:, start - slots.start:start - slots.start + HALF], COPY)
+                                rhs=g_codes[:, halves[h]].bitcast(E5M2X4), rhs_scale=g_scales[:, halves[h]], start=True, stop=True)
+            dn = sb.tile([P, HALF], F32, name="dn" + name, tag="dn%d" % tag)
+            copy(dn[:], sums)
+            return dn
+
+        def scatter_negatives(t, h, dn):
+            nc.scalar.activation(window[t][:].indirect(entries(neg, halves[h])), dn[:], COPY)
 
         def scatter_positives(t, rows):
             nc.vector.tensor_tensor(window[t][:].indirect(entries(pos, rows)), xT[:, t, rows], gp_row[:, rows], MULT)
@@ -235,42 +224,56 @@ def tile_attend_gspos_ns_w_kernel(tc, x, wT, us, ts, wt, offs, poffs, out):
             nc.sync.dma_start(out=out_planes[t], in_=window[t][:])
 
         first_scores = scores(0)
-        s0 = sb.tile([P, PACK], F32, name="s0")
-        nc.vector.tensor_reduce(s0[:], dots[:], mybir.AxisListType.X, ADD)
-        squash(0, 0, first_scores[0])
+        wu = sb.tile([P, PACK], F32, name="wu")
+        minus_us_ts = sb.tile([P, PACK], F32, name="minus_us_ts")
+        minus_wu_ts = sb.tile([P, PACK], F32, name="minus_wu_ts")
+        nc.vector.tensor_tensor(wu[:], us_col[:], wt_col[:], MULT)
+        nc.vector.scalar_tensor_tensor(minus_us_ts[:], turned_pos[:, :, P - 1], -1.0, uw_list[:, 0, :], MULT, MULT)
+        factors = [sb.tile([P, PACK, HALF], F32, name="factors0")]
+        for j in range(PACK):
+            nc.vector.tensor_scalar(factors[0][:, j, :], ts_all[:, first_half], wu[:, j:j + 1], None, MULT)
+        nc.vector.tensor_tensor(minus_wu_ts[:], minus_us_ts[:], uw_list[:, 1, :], MULT)
         second_scores = scores(1)
-        squash(0, 1, first_scores[1])
-
+        terms = sb.tile([P, PACK, P], F32, name="terms", tag="pair1")
+        minus_sp = sb.tile([P, PACK], F32, name="minus_sp")
         sig_p = sb.tile([P, PACK], F32, name="sig_p")
         gp = sb.tile([P, PACK], F32, name="gp")
-        spread_gp = [bank(1 + h, "spread_gp%d" % h) for h in range(2)]
+        spread_gp = [bank((2, 5)[h], "spread_gp%d" % h) for h in range(2)]
         for b in range(PACK):
-            nc.scalar.activation(sig_p[:, b:b + 1], s0[:, b:b + 1], SIGMOID, scale=minus_us_ts[:, b:b + 1])
+            nc.scalar.activation(terms[:, b, :], dots[:, b, :], COPY, scale=minus_us_ts[:, b:b + 1], accum_out=minus_sp[:, b:b + 1])
+        nc.scalar.activation(sig_p[:], minus_sp[:], SIGMOID)
         for b in range(PACK):
             nc.scalar.activation(gp[:, b:b + 1], sig_p[:, b:b + 1], COPY, scale=minus_wu_ts[:, b:b + 1])
             nc.tensor.transpose(spread_gp[b // 2][:, b % 2, :], gp[:, b:b + 1].to_broadcast([P, P]), ident[:])
-
-        squash(1, 0, second_scores[0])
+        for h, banks in enumerate((first_scores, second_scores)):
+            for k in range(2):
+                squash(h, k, banks[k])
         weigh(0)
-        squash(1, 1, second_scores[1])
+        factors.append(sb.tile([P, PACK, HALF], F32, name="factors1", tag="scaled0"))
+        for j in range(2):
+            nc.scalar.activation(factors[1][:, j, :], ts_all[:, second_half], COPY, scale=wu[:, j:j + 1])
+        for j in range(2, PACK):
+            nc.vector.tensor_scalar(factors[1][:, j, :], ts_all[:, second_half], wu[:, j:j + 1], None, MULT)
         quantize_g(0)
+
         nc.scalar.copy(gp_row[:, second_half], flat(spread_gp[1])[:, 0:HALF])
-        scatter_negatives(0, first_half, 3)
+        scatter_negatives(0, 0, product(0, 0, 4, 0, nc.scalar.copy))
         weigh(1)
         nc.vector.tensor_copy(gp_row[:, first_half], flat(spread_gp[0])[:, 0:HALF])
         quantize_g(1)
-        for t in (2, last):
-            window.append(late.tile([P, T], F32, name="window%d" % t, offset=4 * T * (t - 2), align_bytes=64))
+        for t in (1, 2):
+            window[t] = late.tile([P, T], F32, name="window%d" % t, offset=4 * T * (t - 1), align_bytes=64)
             nc.gpsimd.memset(window[t][:].bitcast(I32), 0)
-        scatter_positives(1, everything)
-        scatter_negatives(0, second_half, 0)
-        scatter_positives(0, everything)
-        store(0)
-        scatter_negatives(2, everything, 4)
-        scatter_negatives(1, everything, 5)
-        store(1)
         scatter_positives(last, everything)
-        scatter_positives(2, everything)
-        store(2)
-        scatter_negatives(last, everything, 6)
+        second = product(0, 1, 3, 1, nc.scalar.copy)
+        first = product(1, 0, 0, 2, nc.scalar.copy)
+        scatter_negatives(0, 1, second)
+        later = [product(t, 1, 4 + t, 2 + t, nc.vector.tensor_copy) for t in range(1, PACK)]
+        for t in range(1, PACK):
+            scatter_positives(t - 1, everything)
+            store(t - 1)
+            scatter_negatives(t, 0, first)
+            if t < last:
+                first = product(t + 1, 0, t % 2, 1, nc.scalar.copy)
+            scatter_negatives(t, 1, later[t - 1])
         store(last)

@@ -89,9 +89,8 @@ def tile_attend_gspos_ns_w_kernel(tc, x, wT, us, ts, wt, offs, poffs, out):
         nc.vector.tensor_copy(ts_pos_row[:], ts_row[:].indirect(pos[:]))
 
         x_r = sb.tile([P, D * PACK], BF16, name="x_r", align_bytes=64)
-        for h in range(2):
-            nc.vector.tensor_copy(x_r[:].rearrange("p (t m j) -> p m j t", t=PACK, j=PACK)[:, :, 2 * h:2 * h + 2, :],
-                                  x_sb[:].rearrange("p (j m t) -> p m j t", j=PACK, t=PACK)[:, :, 2 * h:2 * h + 2, :])
+        nc.vector.tensor_copy(x_r[:].rearrange("p (t m j) -> p m j t", t=PACK, j=PACK),
+                              x_sb[:].rearrange("p (j m t) -> p m j t", j=PACK, t=PACK))
         x_r_codes = sb.tile([P, D], U32, name="x_r_codes", align_bytes=64)
         x_r_scales = sb.tile([P, D], U8, name="x_r_scales", align_bytes=64)
         nc.vector.quantize_mx(out=x_r_codes[:].bitcast(E4M3X4), scales=x_r_scales[:], in_=x_r[:])
@@ -124,7 +123,7 @@ def tile_attend_gspos_ns_w_kernel(tc, x, wT, us, ts, wt, offs, poffs, out):
         nc.scalar.copy(ts_all[:], flat(spread_ts))
 
         w_d = [sb.tile([P, HALF * PACK], BF16, name="w_d%d" % h, tag="w_d%d" % h, align_bytes=64) for h in range(2)]
-        pairs = [sb.tile([P, 2, SLOTS], BF16, name="pair%d" % u, tag="pair%d" % u) for u in range(2)]
+        planes = sb.tile([P, PACK, SLOTS], BF16, name="planes", tag="planes")
         dots = bank(3, "dots")
 
         def gather_positives(t):
@@ -135,35 +134,30 @@ def tile_attend_gspos_ns_w_kernel(tc, x, wT, us, ts, wt, offs, poffs, out):
                                  start=(t == 0 and b == 0), stop=(t == last and b == last))
 
         def gather_negatives(t, slots):
-            nc.scalar.activation(pairs[t // 2][:, t % 2, slots], w[t][:].indirect(entries(neg, slots)), COPY)
+            nc.scalar.activation(planes[:, t, slots], w[t][:].indirect(entries(neg, slots)), COPY)
 
-        def interleave_pair(u, h, copy):
-            copy(w_d[h][:].rearrange("p (c i t) -> p c t i", i=PACK, t=PACK)[:, :, 2 * u:2 * u + 2, :],
-                 pairs[u][:, :, halves[h]].rearrange("p t (c i) -> p c t i", i=PACK))
+        def interleave(h, copy):
+            copy(w_d[h][:].rearrange("p (c i t) -> p c t i", i=PACK, t=PACK),
+                 planes[:, :, halves[h]].rearrange("p t (c i) -> p c t i", i=PACK))
 
         x_d = sb.tile([P, R * PACK], BF16, name="x_d", align_bytes=64)
         x_d_codes = sb.tile([P, R], U32, name="x_d_codes", align_bytes=64)
         x_d_scales = sb.tile([P, R], U8, name="x_d_scales", align_bytes=64)
 
-        def round_x_d(u):
-            nc.vector.tensor_copy(x_d[:].rearrange("p (j s t) -> p s j t", j=PACK, t=PACK)[:, :, :, 2 * u:2 * u + 2],
-                                  xT[:, 2 * u:2 * u + 2, :].rearrange("p t (s j) -> p s j t", j=PACK))
-
         gather_positives(0)
         gather_negatives(0, everything)
-        round_x_d(0)
         gather_positives(1)
         gather_negatives(1, everything)
-        round_x_d(1)
-        for h in range(2):
-            interleave_pair(0, h, nc.vector.tensor_copy)
-        nc.vector.quantize_mx(out=x_d_codes[:].bitcast(E4M3X4), scales=x_d_scales[:], in_=x_d[:])
+        nc.vector.tensor_copy(x_d[:].rearrange("p (j s t) -> p s j t", j=PACK, t=PACK),
+                              xT[:].rearrange("p t (s j) -> p s j t", j=PACK))
         gather_positives(2)
         gather_negatives(2, everything)
+        nc.vector.quantize_mx(out=x_d_codes[:].bitcast(E4M3X4), scales=x_d_scales[:], in_=x_d[:])
         gather_positives(last)
         for h in range(2):
             gather_negatives(last, halves[h])
-            interleave_pair(1, h, nc.scalar.copy)
+        interleave(0, nc.vector.tensor_copy)
+        interleave(1, nc.scalar.copy)
 
         w_d_codes = sb.tile([P, SLOTS], U32, name="w_d_codes", align_bytes=64)
         w_d_scales = sb.tile([P, SLOTS], U8, name="w_d_scales", align_bytes=64)
@@ -234,7 +228,7 @@ def tile_attend_gspos_ns_w_kernel(tc, x, wT, us, ts, wt, offs, poffs, out):
             nc.vector.tensor_scalar(factors[0][:, j, :], ts_all[:, first_half], wu[:, j:j + 1], None, MULT)
         nc.vector.tensor_tensor(minus_wu_ts[:], minus_us_ts[:], uw_list[:, 1, :], MULT)
         second_scores = scores(1)
-        terms = sb.tile([P, PACK, P], F32, name="terms", tag="pair1")
+        terms = sb.tile([P, PACK, P], F32, name="terms", tag="planes")
         minus_sp = sb.tile([P, PACK], F32, name="minus_sp")
         sig_p = sb.tile([P, PACK], F32, name="sig_p")
         gp = sb.tile([P, PACK], F32, name="gp")

@@ -48,16 +48,16 @@ def tile_attend_gspos_ns_w_kernel(tc, x, wT, us, ts, wt, offs, poffs, out):
 
         neg = lists.tile([P, SLOTS // 16], U16, name="neg")
         pos = lists.tile([P, R // 16], U16, name="pos")
-        nc.sync.dma_start(neg[:], offs)
-        nc.sync.dma_start(pos[:], poffs)
         ts_row = sb.tile([P, T], F32, name="ts_row")
-        nc.sync.dma_start(out=ts_row[P - 1:P, :], in_=ts[0:1, :])
         x_sb = sb.tile([P, PACK * D], F32, name="x_sb")
         x_rows = x.rearrange("(s j) d -> s (j d)", j=PACK)
-        for h in range(2):
-            nc.sync.dma_start(out=x_sb[:, 2 * h * D:2 * (h + 1) * D], in_=x_rows[:, 2 * h * D:2 * (h + 1) * D])
+        nc.sync.dma_start(out=x_sb[:, 0:2 * D], in_=x_rows[:, 0:2 * D])
+        nc.sync.dma_start(neg[:], offs)
+        nc.sync.dma_start(pos[:], poffs)
+        nc.sync.dma_start(out=ts_row[P - 1:P, :], in_=ts[0:1, :])
+        nc.sync.dma_start(out=x_sb[:, 2 * D:PACK * D], in_=x_rows[:, 2 * D:PACK * D])
 
-        ones = sb.tile([P, P], F32, name="ones")
+        ones = sb.tile([P, P], F32, name="ones", tag="ones")
         uw_rows = sb.tile([P, R], F32, name="uw_rows")
         nc.vector.memset(ones[:], 1.0)
         nc.vector.memset(ts_row[0:P - 1, :].bitcast(I32), 0)
@@ -67,9 +67,8 @@ def tile_attend_gspos_ns_w_kernel(tc, x, wT, us, ts, wt, offs, poffs, out):
                                 pattern=[[-1, P]], channel_multiplier=1)
         table_warm_up = sb.tile([P, 1], F32, name="table_warm_up")
         nc.scalar.activation(table_warm_up[0:P // 2, :], ones[0:P // 2, 0:1], SIGMOID)
-        window = {t: sb.tile([P, T], F32, name="window%d" % t) for t in (0, last)}
-        for t in (0, last):
-            nc.vector.memset(window[t][:].bitcast(I32), 0)
+        window = {0: sb.tile([P, T], F32, name="window0", tag="ones")}
+        nc.gpsimd.memset(window[0][:].bitcast(I32), 0)
 
         w_planes = wT.rearrange("(p t) c -> t p c", t=PACK)
         w = [sb.tile([P, T], F32, name="w%d" % t) for t in range(PACK)]
@@ -122,12 +121,16 @@ def tile_attend_gspos_ns_w_kernel(tc, x, wT, us, ts, wt, offs, poffs, out):
         ts_all = sb.tile([P, SLOTS], F32, name="ts_all")
         nc.scalar.copy(ts_all[:], flat(spread_ts))
 
-        w_d = [sb.tile([P, HALF * PACK], BF16, name="w_d%d" % h, tag="w_d%d" % h, align_bytes=64) for h in range(2)]
+        w_d = [sb.tile([P, HALF * PACK], BF16, name="w_d0", align_bytes=64),
+               late.tile([P, HALF * PACK], BF16, name="w_d1", offset=64, align_bytes=64)]
         planes = sb.tile([P, PACK, SLOTS], BF16, name="planes", tag="planes")
         dots = bank(3, "dots")
 
         def gather_positives(t):
-            products = sb.tile([P, R], F32, name="products%d" % t)
+            if t == 2:
+                products = late.tile([P, R], F32, name="products2", offset=4 * T * 3, align_bytes=64)
+            else:
+                products = sb.tile([P, R], F32, name="products%d" % t)
             nc.vector.tensor_tensor(products[:], w[t][:].indirect(pos[:]), xT[:, t, :], MULT)
             for b in range(PACK):
                 nc.tensor.matmul(dots[:, b, :], lhsT=products[:, b * P:(b + 1) * P], rhs=ident[:], is_transpose=True,
@@ -140,7 +143,7 @@ def tile_attend_gspos_ns_w_kernel(tc, x, wT, us, ts, wt, offs, poffs, out):
             copy(w_d[h][:].rearrange("p (c i t) -> p c t i", i=PACK, t=PACK),
                  planes[:, :, halves[h]].rearrange("p t (c i) -> p c t i", i=PACK))
 
-        x_d = sb.tile([P, R * PACK], BF16, name="x_d", align_bytes=64)
+        x_d = late.tile([P, R * PACK], BF16, name="x_d", offset=4 * T * 3 - 4 * R, align_bytes=64)
         x_d_codes = sb.tile([P, R], U32, name="x_d_codes", align_bytes=64)
         x_d_scales = sb.tile([P, R], U8, name="x_d_scales", align_bytes=64)
 
@@ -150,9 +153,11 @@ def tile_attend_gspos_ns_w_kernel(tc, x, wT, us, ts, wt, offs, poffs, out):
         gather_negatives(1, everything)
         nc.vector.tensor_copy(x_d[:].rearrange("p (j s t) -> p s j t", j=PACK, t=PACK),
                               xT[:].rearrange("p t (s j) -> p s j t", j=PACK))
+        nc.vector.quantize_mx(out=x_d_codes[:].bitcast(E4M3X4), scales=x_d_scales[:], in_=x_d[:])
+        window[2] = late.tile([P, T], F32, name="window2", offset=4 * T * 2, align_bytes=64)
+        nc.gpsimd.memset(window[2][:].bitcast(I32), 0)
         gather_positives(2)
         gather_negatives(2, everything)
-        nc.vector.quantize_mx(out=x_d_codes[:].bitcast(E4M3X4), scales=x_d_scales[:], in_=x_d[:])
         gather_positives(last)
         for h in range(2):
             gather_negatives(last, halves[h])
@@ -167,8 +172,7 @@ def tile_attend_gspos_ns_w_kernel(tc, x, wT, us, ts, wt, offs, poffs, out):
         sig_first = sb.tile([P, PACK * HALF], F32, name="sig_first")
         sig = [tile[:, 0:PACK * HALF].rearrange("p (j i) -> p j i", j=PACK) for tile in (sig_first, sig_second)]
         gp_row = sig_second[:, PACK * HALF - HALF:PACK * HALF + HALF]
-        scaled = [sb.tile([P, PACK, HALF], F32, name="scaled%d" % h, tag="scaled%d" % h) for h in range(2)]
-        g = [late.tile([P, HALF * PACK], BF16, name="g%d" % h, offset=4 * T - PACK * HALF, align_bytes=64) for h in range(2)]
+        g = [late.tile([P, HALF * PACK], BF16, name="g%d" % h, offset=4 * T, align_bytes=64) for h in range(2)]
 
         def scores(h):
             nc.vector.quantize_mx(out=w_d_codes[:, halves[h]].bitcast(E4M3X4), scales=w_d_scales[:, halves[h]], in_=w_d[h][:])
@@ -181,11 +185,13 @@ def tile_attend_gspos_ns_w_kernel(tc, x, wT, us, ts, wt, offs, poffs, out):
                                     start=True, stop=True)
             return banks
 
-        def squash(h, k, scores_bank):
-            nc.vector.tensor_tensor(scaled[h][:, 2 * k:2 * k + 2, :], flat(scores_bank).rearrange("p (j i) -> p j i", j=2),
+        def squash(h, k, scores_bank, tag):
+            scaled = sb.tile([P, 2, HALF], F32, name="scaled%d_%d" % (h, k), tag="scaled%d" % tag)
+            nc.vector.tensor_tensor(scaled[:], flat(scores_bank).rearrange("p (j i) -> p j i", j=2),
                                     ts_all[:, halves[h]].unsqueeze(1).to_broadcast([P, 2, HALF]), MULT)
-            for j in (2 * k, 2 * k + 1):
-                nc.scalar.activation(sig[h][:, j, :], scaled[h][:, j, :], SIGMOID, scale=us_col[:, j:j + 1])
+            for e in range(2):
+                j = 2 * k + e
+                nc.scalar.activation(sig[h][:, j, :], scaled[:, e, :], SIGMOID, scale=us_col[:, j:j + 1])
 
         def weigh(h):
             nc.vector.tensor_tensor(g[h][:].rearrange("p (c i j) -> p c j i", i=PACK, j=PACK),
@@ -195,19 +201,19 @@ def tile_attend_gspos_ns_w_kernel(tc, x, wT, us, ts, wt, offs, poffs, out):
         def quantize_g(h):
             nc.vector.quantize_mx(out=g_codes[:, halves[h]].bitcast(E5M2X4), scales=g_scales[:, halves[h]], in_=g[h][:])
 
-        def product(t, h, n, tag, copy):
-            name = "%d_%d" % (t, h)
-            sums = flat(bank(n, "sums" + name))[:, first_half]
+        def product(t, slots, n, tag, copy):
+            name = "%d_%d" % (t, slots.start)
+            sums = flat(bank(n, "sums" + name))[:, 0:slots.stop - slots.start]
             cols = slice(t * P, (t + 1) * P)
             nc.tensor.matmul_mx(out=sums,
                                 lhsT=x_r_codes[:, cols].bitcast(E4M3X4), lhsT_scale=x_r_scales[:, cols],
-                                rhs=g_codes[:, halves[h]].bitcast(E5M2X4), rhs_scale=g_scales[:, halves[h]], start=True, stop=True)
-            dn = sb.tile([P, HALF], F32, name="dn" + name, tag="dn%d" % tag)
+                                rhs=g_codes[:, slots].bitcast(E5M2X4), rhs_scale=g_scales[:, slots], start=True, stop=True)
+            dn = sb.tile([P, slots.stop - slots.start], F32, name="dn" + name, tag="dn%d" % tag)
             copy(dn[:], sums)
             return dn
 
         def scatter_negatives(t, h, dn):
-            nc.scalar.activation(window[t][:].indirect(entries(neg, halves[h])), dn[:], COPY)
+            nc.scalar.activation(window[t][:].indirect(entries(neg, halves[h])), dn, COPY)
 
         def scatter_positives(t, rows):
             nc.vector.tensor_tensor(window[t][:].indirect(entries(pos, rows)), xT[:, t, rows], gp_row[:, rows], MULT)
@@ -218,16 +224,20 @@ def tile_attend_gspos_ns_w_kernel(tc, x, wT, us, ts, wt, offs, poffs, out):
             nc.sync.dma_start(out=out_planes[t], in_=window[t][:])
 
         first_scores = scores(0)
+        wu_first = late.tile([P, PACK], F32, name="wu_first", offset=0, align_bytes=64)
         wu = sb.tile([P, PACK], F32, name="wu")
         minus_us_ts = sb.tile([P, PACK], F32, name="minus_us_ts")
         minus_wu_ts = sb.tile([P, PACK], F32, name="minus_wu_ts")
-        nc.vector.tensor_tensor(wu[:], us_col[:], wt_col[:], MULT)
+        nc.vector.tensor_tensor(wu_first[:], us_col[:], wt_col[:], MULT)
         nc.vector.scalar_tensor_tensor(minus_us_ts[:], turned_pos[:, :, P - 1], -1.0, uw_list[:, 0, :], MULT, MULT)
         factors = [sb.tile([P, PACK, HALF], F32, name="factors0")]
         for j in range(PACK):
-            nc.vector.tensor_scalar(factors[0][:, j, :], ts_all[:, first_half], wu[:, j:j + 1], None, MULT)
+            nc.vector.tensor_scalar(factors[0][:, j, :], ts_all[:, first_half], wu_first[:, j:j + 1], None, MULT)
         nc.vector.tensor_tensor(minus_wu_ts[:], minus_us_ts[:], uw_list[:, 1, :], MULT)
+        nc.vector.tensor_tensor(wu[:], us_col[:], wt_col[:], MULT)
         second_scores = scores(1)
+        window[1] = late.tile([P, T], F32, name="window1", offset=0, align_bytes=64)
+        nc.gpsimd.memset(window[1][:].bitcast(I32), 0)
         terms = sb.tile([P, PACK, P], F32, name="terms", tag="planes")
         minus_sp = sb.tile([P, PACK], F32, name="minus_sp")
         sig_p = sb.tile([P, PACK], F32, name="sig_p")
@@ -241,33 +251,38 @@ def tile_attend_gspos_ns_w_kernel(tc, x, wT, us, ts, wt, offs, poffs, out):
             nc.tensor.transpose(spread_gp[b // 2][:, b % 2, :], gp[:, b:b + 1].to_broadcast([P, P]), ident[:])
         for h, banks in enumerate((first_scores, second_scores)):
             for k in range(2):
-                squash(h, k, banks[k])
+                squash(h, k, banks[k], 2 * h + k)
         weigh(0)
-        factors.append(sb.tile([P, PACK, HALF], F32, name="factors1", tag="scaled0"))
+        factors.append(sb.tile([P, PACK, HALF], F32, name="factors1", tag="scaled1"))
         for j in range(2):
             nc.scalar.activation(factors[1][:, j, :], ts_all[:, second_half], COPY, scale=wu[:, j:j + 1])
         for j in range(2, PACK):
             nc.vector.tensor_scalar(factors[1][:, j, :], ts_all[:, second_half], wu[:, j:j + 1], None, MULT)
         quantize_g(0)
-
         nc.scalar.copy(gp_row[:, second_half], flat(spread_gp[1])[:, 0:HALF])
-        scatter_negatives(0, 0, product(0, 0, 4, 0, nc.scalar.copy))
+        scatter_negatives(0, 0, product(0, first_half, 4, 0, nc.scalar.copy)[:])
         weigh(1)
         nc.vector.tensor_copy(gp_row[:, first_half], flat(spread_gp[0])[:, 0:HALF])
         quantize_g(1)
-        for t in (1, 2):
-            window[t] = late.tile([P, T], F32, name="window%d" % t, offset=4 * T * (t - 1), align_bytes=64)
-            nc.gpsimd.memset(window[t][:].bitcast(I32), 0)
-        scatter_positives(last, everything)
-        second = product(0, 1, 3, 1, nc.scalar.copy)
-        first = product(1, 0, 0, 2, nc.scalar.copy)
-        scatter_negatives(0, 1, second)
-        later = [product(t, 1, 4 + t, 2 + t, nc.vector.tensor_copy) for t in range(1, PACK)]
-        for t in range(1, PACK):
-            scatter_positives(t - 1, everything)
-            store(t - 1)
-            scatter_negatives(t, 0, first)
-            if t < last:
-                first = product(t + 1, 0, t % 2, 1, nc.scalar.copy)
-            scatter_negatives(t, 1, later[t - 1])
+        window[last] = late.tile([P, T], F32, name="window3", offset=4 * T, align_bytes=64)
+        nc.gpsimd.memset(window[last][:].bitcast(I32), 0)
+
+        def product_half(k):
+            return product(k // 2, halves[k % 2], (4, 3, 3, 0, 1, 5, 6, 7)[k], k % 3, nc.scalar.copy)[:]
+
+        scatter_positives(2, everything)
+        waiting = [product_half(1)]
+        for k in range(1, 2 * PACK):
+            if k + 1 < 2 * PACK:
+                waiting.append(product_half(k + 1))
+            if k == 2 * last:
+                scatter_positives(last, everything)
+                scatter_positives(1, everything)
+                store(1)
+            scatter_negatives(k // 2, k % 2, waiting[k - 1])
+            if k == 1:
+                scatter_positives(0, everything)
+                store(0)
+            if k == 5:
+                store(2)
         store(last)

@@ -87,12 +87,14 @@ def tile_attend_gspos_ns_w_kernel(tc, x, wT, us, ts, wt, offs, poffs, out):
         nc.scalar.activation(ts_neg_row[:], ts_row[:].indirect(neg[:]), COPY)
         nc.vector.tensor_copy(ts_pos_row[:], ts_row[:].indirect(pos[:]))
 
-        x_r = sb.tile([P, D * PACK], BF16, name="x_r", align_bytes=64)
+        x_r = late.tile([P, D * PACK], BF16, name="x_r", offset=0, align_bytes=64)
         nc.vector.tensor_copy(x_r[:].rearrange("p (t m j) -> p m j t", t=PACK, j=PACK),
                               x_sb[:].rearrange("p (j m t) -> p m j t", j=PACK, t=PACK))
         x_r_codes = sb.tile([P, D], U32, name="x_r_codes", align_bytes=64)
         x_r_scales = sb.tile([P, D], U8, name="x_r_scales", align_bytes=64)
         nc.vector.quantize_mx(out=x_r_codes[:].bitcast(E4M3X4), scales=x_r_scales[:], in_=x_r[:])
+        window[1] = late.tile([P, T], F32, name="window1", offset=0, align_bytes=64)
+        nc.gpsimd.memset(window[1][:].bitcast(I32), 0)
 
         x_planes = x_sb[:].rearrange("p (j m t) -> p j t m", j=PACK, t=PACK)
         xT = sb.tile([P, PACK, R], F32, name="xT")
@@ -121,8 +123,7 @@ def tile_attend_gspos_ns_w_kernel(tc, x, wT, us, ts, wt, offs, poffs, out):
         ts_all = sb.tile([P, SLOTS], F32, name="ts_all")
         nc.scalar.copy(ts_all[:], flat(spread_ts))
 
-        w_d = [sb.tile([P, HALF * PACK], BF16, name="w_d0", align_bytes=64),
-               late.tile([P, HALF * PACK], BF16, name="w_d1", offset=64, align_bytes=64)]
+        w_d = [sb.tile([P, HALF * PACK], BF16, name="w_d%d" % h, align_bytes=64) for h in range(2)]
         planes = sb.tile([P, PACK, SLOTS], BF16, name="planes", tag="planes")
         dots = bank(3, "dots")
 
@@ -172,7 +173,8 @@ def tile_attend_gspos_ns_w_kernel(tc, x, wT, us, ts, wt, offs, poffs, out):
         sig_first = sb.tile([P, PACK * HALF], F32, name="sig_first")
         sig = [tile[:, 0:PACK * HALF].rearrange("p (j i) -> p j i", j=PACK) for tile in (sig_first, sig_second)]
         gp_row = sig_second[:, PACK * HALF - HALF:PACK * HALF + HALF]
-        g = [late.tile([P, HALF * PACK], BF16, name="g%d" % h, offset=4 * T, align_bytes=64) for h in range(2)]
+        g_both = late.tile([P, 3 * P * PACK], BF16, name="g_both", offset=4 * T, align_bytes=64)
+        g = [g_both[:, P * PACK:3 * P * PACK], g_both[:, 0:2 * P * PACK]]
 
         def scores(h):
             nc.vector.quantize_mx(out=w_d_codes[:, halves[h]].bitcast(E4M3X4), scales=w_d_scales[:, halves[h]], in_=w_d[h][:])
@@ -193,13 +195,13 @@ def tile_attend_gspos_ns_w_kernel(tc, x, wT, us, ts, wt, offs, poffs, out):
                 j = 2 * k + e
                 nc.scalar.activation(sig[h][:, j, :], scaled[:, e, :], SIGMOID, scale=us_col[:, j:j + 1])
 
-        def weigh(h):
-            nc.vector.tensor_tensor(g[h][:].rearrange("p (c i j) -> p c j i", i=PACK, j=PACK),
-                                    sig[h].rearrange("p j (c i) -> p c j i", i=PACK),
-                                    factors[h][:].rearrange("p j (c i) -> p c j i", i=PACK), MULT)
+        def weigh(h, part):
+            nc.vector.tensor_tensor(g[h][:, PACK * part.start:PACK * part.stop].rearrange("p (c i j) -> p c j i", i=PACK, j=PACK),
+                                    sig[h][:, :, part].rearrange("p j (c i) -> p c j i", i=PACK),
+                                    factors[h][:, :, part].rearrange("p j (c i) -> p c j i", i=PACK), MULT)
 
         def quantize_g(h):
-            nc.vector.quantize_mx(out=g_codes[:, halves[h]].bitcast(E5M2X4), scales=g_scales[:, halves[h]], in_=g[h][:])
+            nc.vector.quantize_mx(out=g_codes[:, halves[h]].bitcast(E5M2X4), scales=g_scales[:, halves[h]], in_=g[h])
 
         def product(t, slots, n, tag, copy):
             name = "%d_%d" % (t, slots.start)
@@ -224,20 +226,16 @@ def tile_attend_gspos_ns_w_kernel(tc, x, wT, us, ts, wt, offs, poffs, out):
             nc.sync.dma_start(out=out_planes[t], in_=window[t][:])
 
         first_scores = scores(0)
-        wu_first = late.tile([P, PACK], F32, name="wu_first", offset=0, align_bytes=64)
         wu = sb.tile([P, PACK], F32, name="wu")
         minus_us_ts = sb.tile([P, PACK], F32, name="minus_us_ts")
         minus_wu_ts = sb.tile([P, PACK], F32, name="minus_wu_ts")
-        nc.vector.tensor_tensor(wu_first[:], us_col[:], wt_col[:], MULT)
+        nc.vector.tensor_tensor(wu[:], us_col[:], wt_col[:], MULT)
         nc.vector.scalar_tensor_tensor(minus_us_ts[:], turned_pos[:, :, P - 1], -1.0, uw_list[:, 0, :], MULT, MULT)
         factors = [sb.tile([P, PACK, HALF], F32, name="factors0")]
         for j in range(PACK):
-            nc.vector.tensor_scalar(factors[0][:, j, :], ts_all[:, first_half], wu_first[:, j:j + 1], None, MULT)
+            nc.vector.tensor_scalar(factors[0][:, j, :], ts_all[:, first_half], wu[:, j:j + 1], None, MULT)
         nc.vector.tensor_tensor(minus_wu_ts[:], minus_us_ts[:], uw_list[:, 1, :], MULT)
-        nc.vector.tensor_tensor(wu[:], us_col[:], wt_col[:], MULT)
         second_scores = scores(1)
-        window[1] = late.tile([P, T], F32, name="window1", offset=0, align_bytes=64)
-        nc.gpsimd.memset(window[1][:].bitcast(I32), 0)
         terms = sb.tile([P, PACK, P], F32, name="terms", tag="planes")
         minus_sp = sb.tile([P, PACK], F32, name="minus_sp")
         sig_p = sb.tile([P, PACK], F32, name="sig_p")
@@ -252,16 +250,17 @@ def tile_attend_gspos_ns_w_kernel(tc, x, wT, us, ts, wt, offs, poffs, out):
         for h, banks in enumerate((first_scores, second_scores)):
             for k in range(2):
                 squash(h, k, banks[k], 2 * h + k)
-        weigh(0)
+        weigh(0, first_half)
         factors.append(sb.tile([P, PACK, HALF], F32, name="factors1", tag="scaled1"))
         for j in range(2):
             nc.scalar.activation(factors[1][:, j, :], ts_all[:, second_half], COPY, scale=wu[:, j:j + 1])
         for j in range(2, PACK):
             nc.vector.tensor_scalar(factors[1][:, j, :], ts_all[:, second_half], wu[:, j:j + 1], None, MULT)
+        weigh(1, slice(0, P))
         quantize_g(0)
         nc.scalar.copy(gp_row[:, second_half], flat(spread_gp[1])[:, 0:HALF])
         scatter_negatives(0, 0, product(0, first_half, 4, 0, nc.scalar.copy)[:])
-        weigh(1)
+        weigh(1, slice(P, HALF))
         nc.vector.tensor_copy(gp_row[:, first_half], flat(spread_gp[0])[:, 0:HALF])
         quantize_g(1)
         window[last] = late.tile([P, T], F32, name="window3", offset=4 * T, align_bytes=64)
@@ -285,4 +284,4 @@ def tile_attend_gspos_ns_w_kernel(tc, x, wT, us, ts, wt, offs, poffs, out):
                 store(0)
             if k == 5:
                 store(2)
-        store(last)
+        nc.scalar.dma_start(out=out_planes[last], in_=window[last][:])

@@ -266,22 +266,25 @@ def tile_attend_gspos_ns_w_kernel(tc, x, wT, us, ts, wt, offs, poffs, out):
         window[last] = late.tile([P, T], F32, name="window3", offset=4 * T, align_bytes=64)
         nc.gpsimd.memset(window[last][:].bitcast(I32), 0)
 
+        order = (0, 2, 1, last)
+
         def product_half(k):
-            return product(k // 2, halves[k % 2], (4, 3, 3, 0, 1, 5, 6, 7)[k], k % 3, nc.scalar.copy)[:]
+            return product(order[k // 2], halves[k % 2], (4, 3, 3, 0, 1, 5, 6, 7)[k], k % 3, nc.scalar.copy)[:]
 
         scatter_positives(2, everything)
+        scatter_positives(1, first_half)
         waiting = [product_half(1)]
         for k in range(1, 2 * PACK):
             if k + 1 < 2 * PACK:
                 waiting.append(product_half(k + 1))
             if k == 2 * last:
                 scatter_positives(last, everything)
-                scatter_positives(1, everything)
+                scatter_positives(1, second_half)
                 store(1)
-            scatter_negatives(k // 2, k % 2, waiting[k - 1])
+            scatter_negatives(order[k // 2], k % 2, waiting[k - 1])
             if k == 1:
                 scatter_positives(0, everything)
-                store(0)
-            if k == 5:
+            if k == 3:
                 store(2)
+                store(0)
         nc.scalar.dma_start(out=out_planes[last], in_=window[last][:])

@@ -11,6 +11,7 @@ U8 = mybir.dt.uint8
 E4M3X4 = mybir.dt.float8_e4m3fn_x4
 E5M2X4 = mybir.dt.float8_e5m2_x4
 MULT = mybir.AluOpType.mult
+ADD = mybir.AluOpType.add
 COPY = mybir.ActivationFunctionType.Copy
 SIGMOID = mybir.ActivationFunctionType.Sigmoid
 
@@ -123,7 +124,7 @@ def tile_attend_gspos_ns_w_kernel(tc, x, wT, us, ts, wt, offs, poffs, out):
         ts_all = sb.tile([P, SLOTS], F32, name="ts_all")
         nc.scalar.copy(ts_all[:], flat(spread_ts))
 
-        w_d = [sb.tile([P, HALF * PACK], BF16, name="w_d%d" % h, align_bytes=64) for h in range(2)]
+        w_d = [sb.tile([P, HALF * PACK], BF16, name="w_d%d" % h, tag="w_d%d" % h, align_bytes=64) for h in range(2)]
         planes = sb.tile([P, PACK, SLOTS], BF16, name="planes", tag="planes")
         dots = bank(3, "dots")
 
@@ -236,6 +237,9 @@ def tile_attend_gspos_ns_w_kernel(tc, x, wT, us, ts, wt, offs, poffs, out):
             nc.vector.tensor_scalar(factors[0][:, j, :], ts_all[:, first_half], wu[:, j:j + 1], None, MULT)
         nc.vector.tensor_tensor(minus_wu_ts[:], minus_us_ts[:], uw_list[:, 1, :], MULT)
         second_scores = scores(1)
+        factors.append(sb.tile([P, PACK, HALF], F32, name="factors1", tag="w_d1", align_bytes=64))
+        for j in range(PACK):
+            nc.gpsimd.tensor_scalar(factors[1][:, j, :], ts_all[:, second_half], wu[:, j:j + 1], 0.0, MULT, ADD)
         terms = sb.tile([P, PACK, P], F32, name="terms", tag="planes")
         minus_sp = sb.tile([P, PACK], F32, name="minus_sp")
         sig_p = sb.tile([P, PACK], F32, name="sig_p")
@@ -251,11 +255,6 @@ def tile_attend_gspos_ns_w_kernel(tc, x, wT, us, ts, wt, offs, poffs, out):
             for k in range(2):
                 squash(h, k, banks[k], 2 * h + k)
         weigh(0, first_half)
-        factors.append(sb.tile([P, PACK, HALF], F32, name="factors1", tag="scaled1"))
-        for j in range(2):
-            nc.scalar.activation(factors[1][:, j, :], ts_all[:, second_half], COPY, scale=wu[:, j:j + 1])
-        for j in range(2, PACK):
-            nc.vector.tensor_scalar(factors[1][:, j, :], ts_all[:, second_half], wu[:, j:j + 1], None, MULT)
         weigh(1, slice(0, P))
         quantize_g(0)
         nc.scalar.copy(gp_row[:, second_half], flat(spread_gp[1])[:, 0:HALF])

@@ -22,6 +22,7 @@ R = 512
 SLOTS = 512
 T = 2048
 HALF = SLOTS // 2
+EARLY = 64
 
 FLOPS = 2 * R * D * SLOTS + 2 * D * R * SLOTS
 
@@ -126,7 +127,7 @@ def tile_attend_gspos_ns_w_kernel(tc, x, wT, us, ts, wt, offs, poffs, out):
 
         w_d = [sb.tile([P, HALF * PACK], BF16, name="w_d%d" % h, tag="w_d%d" % h, align_bytes=64) for h in range(2)]
         planes = sb.tile([P, PACK, SLOTS], BF16, name="planes", tag="planes")
-        dots = bank(3, "dots")
+        dots = bank(5, "dots")
 
         def gather_positives(t):
             if t == 2:
@@ -174,8 +175,8 @@ def tile_attend_gspos_ns_w_kernel(tc, x, wT, us, ts, wt, offs, poffs, out):
         sig_first = sb.tile([P, PACK * HALF], F32, name="sig_first")
         sig = [tile[:, 0:PACK * HALF].rearrange("p (j i) -> p j i", j=PACK) for tile in (sig_first, sig_second)]
         gp_row = sig_second[:, PACK * HALF - HALF:PACK * HALF + HALF]
-        g_both = late.tile([P, 3 * P * PACK], BF16, name="g_both", offset=4 * T, align_bytes=64)
-        g = [g_both[:, P * PACK:3 * P * PACK], g_both[:, 0:2 * P * PACK]]
+        g_both = late.tile([P, (EARLY + HALF) * PACK], BF16, name="g_both", offset=4 * T, align_bytes=64)
+        g = [g_both[:, EARLY * PACK:], g_both[:, 0:HALF * PACK]]
 
         def scores(h):
             nc.vector.quantize_mx(out=w_d_codes[:, halves[h]].bitcast(E4M3X4), scales=w_d_scales[:, halves[h]], in_=w_d[h][:])
@@ -255,11 +256,11 @@ def tile_attend_gspos_ns_w_kernel(tc, x, wT, us, ts, wt, offs, poffs, out):
             for k in range(2):
                 squash(h, k, banks[k], 2 * h + k)
         weigh(0, first_half)
-        weigh(1, slice(0, P))
+        weigh(1, slice(0, EARLY))
         quantize_g(0)
         nc.scalar.copy(gp_row[:, second_half], flat(spread_gp[1])[:, 0:HALF])
         scatter_negatives(0, 0, product(0, first_half, 4, 0, nc.scalar.copy)[:])
-        weigh(1, slice(P, HALF))
+        weigh(1, slice(EARLY, HALF))
         nc.vector.tensor_copy(gp_row[:, first_half], flat(spread_gp[0])[:, 0:HALF])
         quantize_g(1)
         window[last] = late.tile([P, T], F32, name="window3", offset=4 * T, align_bytes=64)

@@ -122,7 +122,7 @@ def tile_attend_gspos_ns_w_kernel(tc, x, wT, us, ts, wt, offs, poffs, out):
         turned_pos = bank(4, "turned_pos")
         for b in range(PACK):
             nc.tensor.transpose(turned_pos[:, b, :], ts_pos_row[:, b * P:(b + 1) * P], ident[:])
-        ts_all = sb.tile([P, SLOTS], F32, name="ts_all")
+        ts_all = late.tile([P, SLOTS], F32, name="ts_all", offset=4 * T * 4, align_bytes=64)
         nc.scalar.copy(ts_all[:], flat(spread_ts))
 
         w_d = [sb.tile([P, HALF * PACK], BF16, name="w_d%d" % h, tag="w_d%d" % h, align_bytes=64) for h in range(2)]
@@ -255,36 +255,38 @@ def tile_attend_gspos_ns_w_kernel(tc, x, wT, us, ts, wt, offs, poffs, out):
         for h, banks in enumerate((first_scores, second_scores)):
             for k in range(2):
                 squash(h, k, banks[k], 2 * h + k)
+        opening = late.tile([P, HALF], F32, name="opening", offset=4 * T * 4 + 4 * HALF, align_bytes=64)
+        nc.vector.tensor_tensor(opening[:], flat(spread_gp[0])[:, 0:HALF], xT[:, 0, first_half], MULT)
+        nc.scalar.activation(window[0][:].indirect(entries(pos, first_half)), opening[:], COPY)
         weigh(0, first_half)
         weigh(1, slice(0, EARLY))
         quantize_g(0)
+        first_dn = product(0, first_half, 4, 0, nc.scalar.copy)
         nc.scalar.copy(gp_row[:, second_half], flat(spread_gp[1])[:, 0:HALF])
-        scatter_negatives(0, 0, product(0, first_half, 4, 0, nc.scalar.copy)[:])
+        scatter_negatives(0, 0, first_dn[:])
         weigh(1, slice(EARLY, HALF))
         nc.vector.tensor_copy(gp_row[:, first_half], flat(spread_gp[0])[:, 0:HALF])
         quantize_g(1)
         window[last] = late.tile([P, T], F32, name="window3", offset=4 * T, align_bytes=64)
         nc.gpsimd.memset(window[last][:].bitcast(I32), 0)
 
-        order = (0, 2, 1, last)
-
-        def product_half(k):
-            return product(order[k // 2], halves[k % 2], (4, 3, 3, 0, 1, 5, 6, 7)[k], k % 3, nc.scalar.copy)[:]
-
         scatter_positives(2, everything)
+        second_dn = product(0, second_half, 3, 1, nc.scalar.copy)
+        dn = {2: product(2, everything, 0, 2, nc.scalar.copy)}
+        scatter_negatives(0, 1, second_dn[:])
+        dn[1] = product(1, everything, 1, 3, nc.vector.tensor_copy)
         scatter_positives(1, first_half)
-        waiting = [product_half(1)]
-        for k in range(1, 2 * PACK):
-            if k + 1 < 2 * PACK:
-                waiting.append(product_half(k + 1))
-            if k == 2 * last:
-                scatter_positives(last, everything)
-                scatter_positives(1, second_half)
-                store(1)
-            scatter_negatives(order[k // 2], k % 2, waiting[k - 1])
-            if k == 1:
-                scatter_positives(0, everything)
-            if k == 3:
-                store(2)
-                store(0)
+        scatter_positives(0, second_half)
+        for h in range(2):
+            scatter_negatives(2, h, dn[2][:, halves[h]])
+        store(2)
+        store(0)
+        dn[last] = product(last, everything, 6, 2, nc.scalar.copy)
+        scatter_positives(last, everything)
+        for h in range(2):
+            scatter_negatives(1, h, dn[1][:, halves[h]])
+        scatter_positives(1, second_half)
+        store(1)
+        for h in range(2):
+            scatter_negatives(last, h, dn[last][:, halves[h]])
         nc.scalar.dma_start(out=out_planes[last], in_=window[last][:])

@@ -23,6 +23,7 @@ SLOTS = 512
 T = 2048
 HALF = SLOTS // 2
 EARLY = 64
+MID = P // 2
 
 FLOPS = 2 * R * D * SLOTS + 2 * D * R * SLOTS
 
@@ -63,7 +64,8 @@ def tile_attend_gspos_ns_w_kernel(tc, x, wT, us, ts, wt, offs, poffs, out):
         uw_rows = sb.tile([P, R], F32, name="uw_rows")
         nc.vector.memset(ones[:], 1.0)
         nc.vector.memset(ts_row[0:P - 1, :].bitcast(I32), 0)
-        nc.vector.memset(uw_rows[0:P - 2, :].bitcast(I32), 0)
+        nc.vector.memset(uw_rows[0:MID - 2, :].bitcast(I32), 0)
+        nc.vector.memset(uw_rows[MID:P, :].bitcast(I32), 0)
         ident = sb.tile([P, P], F32, name="ident")
         nc.gpsimd.affine_select(out=ident[:], in_=ones[:], compare_op=mybir.AluOpType.is_equal, fill=0.0, base=0,
                                 pattern=[[-1, P]], channel_multiplier=1)
@@ -75,8 +77,8 @@ def tile_attend_gspos_ns_w_kernel(tc, x, wT, us, ts, wt, offs, poffs, out):
         w_planes = wT.rearrange("(p t) c -> t p c", t=PACK)
         w = [sb.tile([P, T], F32, name="w%d" % t) for t in range(PACK)]
         nc.sync.dma_start(out=w[0][:], in_=w_planes[0])
-        nc.sync.dma_start(out=uw_rows[P - 2:P - 1, :], in_=us.rearrange("r o -> o r"))
-        nc.sync.dma_start(out=uw_rows[P - 1:P, :], in_=wt.rearrange("r o -> o r"))
+        nc.sync.dma_start(out=uw_rows[MID - 2:MID - 1, :], in_=us.rearrange("r o -> o r"))
+        nc.sync.dma_start(out=uw_rows[MID - 1:MID, :], in_=wt.rearrange("r o -> o r"))
         for t in range(1, PACK):
             nc.sync.dma_start(out=w[t][:], in_=w_planes[t])
         us_col = sb.tile([P, PACK], F32, name="us_col")
@@ -115,7 +117,7 @@ def tile_attend_gspos_ns_w_kernel(tc, x, wT, us, ts, wt, offs, poffs, out):
         for b in range(PACK):
             nc.tensor.transpose(turned_uw[:, b, :], uw_rows[:, b * P:(b + 1) * P], ident[:])
         uw_list = sb.tile([P, 2, PACK], F32, name="uw_list")
-        nc.scalar.copy(uw_list[:], turned_uw[:, :, P - 2:P].rearrange("p b v -> p v b"))
+        nc.scalar.copy(uw_list[:], turned_uw[:, :, MID - 2:MID].rearrange("p b v -> p v b"))
         spread_ts = bank(3, "spread_ts")
         for b in range(PACK):
             nc.tensor.transpose(spread_ts[:, b, :], ts_neg[:, b:b + 1].to_broadcast([P, P]), ident[:])
@@ -249,8 +251,8 @@ def tile_attend_gspos_ns_w_kernel(tc, x, wT, us, ts, wt, offs, poffs, out):
         for b in range(PACK):
             nc.scalar.activation(terms[:, b, :], dots[:, b, :], COPY, scale=minus_us_ts[:, b:b + 1], accum_out=minus_sp[:, b:b + 1])
         nc.scalar.activation(sig_p[:], minus_sp[:], SIGMOID)
+        nc.vector.tensor_tensor(gp[:], sig_p[:], minus_wu_ts[:], MULT)
         for b in range(PACK):
-            nc.scalar.activation(gp[:, b:b + 1], sig_p[:, b:b + 1], COPY, scale=minus_wu_ts[:, b:b + 1])
             nc.tensor.transpose(spread_gp[b // 2][:, b % 2, :], gp[:, b:b + 1].to_broadcast([P, P]), ident[:])
         for h, banks in enumerate((first_scores, second_scores)):
             for k in range(2):

@@ -22,7 +22,7 @@ R = 512
 SLOTS = 512
 T = 2048
 HALF = SLOTS // 2
-EARLY = 64
+HELD = 32
 MID = P // 2
 
 FLOPS = 2 * R * D * SLOTS + 2 * D * R * SLOTS
@@ -133,12 +133,12 @@ def tile_attend_gspos_ns_w_kernel(tc, x, wT, us, ts, wt, offs, poffs, out):
 
         def gather_positives(t):
             if t == 2:
-                products = late.tile([P, R], F32, name="products2", offset=4 * T * 3, align_bytes=64)
+                prods = late.tile([P, R], F32, name="products2", offset=4 * T * 3, align_bytes=64)
             else:
-                products = sb.tile([P, R], F32, name="products%d" % t)
-            nc.vector.tensor_tensor(products[:], w[t][:].indirect(pos[:]), xT[:, t, :], MULT)
+                prods = sb.tile([P, R], F32, name="products%d" % t)
+            nc.vector.tensor_tensor(prods[:], w[t][:].indirect(pos[:]), xT[:, t, :], MULT)
             for b in range(PACK):
-                nc.tensor.matmul(dots[:, b, :], lhsT=products[:, b * P:(b + 1) * P], rhs=ident[:], is_transpose=True,
+                nc.tensor.matmul(dots[:, b, :], lhsT=prods[:, b * P:(b + 1) * P], rhs=ident[:], is_transpose=True,
                                  start=(t == 0 and b == 0), stop=(t == last and b == last))
 
         def gather_negatives(t, slots):
@@ -159,8 +159,8 @@ def tile_attend_gspos_ns_w_kernel(tc, x, wT, us, ts, wt, offs, poffs, out):
         nc.vector.tensor_copy(x_d[:].rearrange("p (j s t) -> p s j t", j=PACK, t=PACK),
                               xT[:].rearrange("p t (s j) -> p s j t", j=PACK))
         nc.vector.quantize_mx(out=x_d_codes[:].bitcast(E4M3X4), scales=x_d_scales[:], in_=x_d[:])
-        window[2] = late.tile([P, T], F32, name="window2", offset=4 * T * 2, align_bytes=64)
-        nc.gpsimd.memset(window[2][:].bitcast(I32), 0)
+        window[last] = late.tile([P, T], F32, name="window3", offset=4 * T * 2, align_bytes=64)
+        nc.gpsimd.memset(window[last][:].bitcast(I32), 0)
         gather_positives(2)
         gather_negatives(2, everything)
         gather_positives(last)
@@ -173,12 +173,11 @@ def tile_attend_gspos_ns_w_kernel(tc, x, wT, us, ts, wt, offs, poffs, out):
         w_d_scales = sb.tile([P, SLOTS], U8, name="w_d_scales", align_bytes=64)
         g_codes = sb.tile([P, SLOTS], U32, name="g_codes", align_bytes=64)
         g_scales = sb.tile([P, SLOTS], U8, name="g_scales", align_bytes=64)
-        sig_second = sb.tile([P, PACK * HALF + HALF], F32, name="sig_second")
-        sig_first = sb.tile([P, PACK * HALF], F32, name="sig_first")
-        sig = [tile[:, 0:PACK * HALF].rearrange("p (j i) -> p j i", j=PACK) for tile in (sig_first, sig_second)]
-        gp_row = sig_second[:, PACK * HALF - HALF:PACK * HALF + HALF]
-        g_both = late.tile([P, (EARLY + HALF) * PACK], BF16, name="g_both", offset=4 * T, align_bytes=64)
-        g = [g_both[:, EARLY * PACK:], g_both[:, 0:HALF * PACK]]
+        sig_second = sb.tile([P, R - HELD + PACK * HALF], F32, name="sig_second")
+        sig_first = sb.tile([P, PACK * HALF], F32, name="sig_first", tag="sig_first")
+        sig = [part.rearrange("p (j i) -> p j i", j=PACK) for part in (sig_first[:], sig_second[:, R - HELD:])]
+        gp_row = sig_second[:, 0:R]
+        g = [late.tile([P, HALF * PACK], BF16, name="g%d" % h, offset=4 * T * 5, align_bytes=64)[:] for h in range(2)]
 
         def scores(h):
             nc.vector.quantize_mx(out=w_d_codes[:, halves[h]].bitcast(E4M3X4), scales=w_d_scales[:, halves[h]], in_=w_d[h][:])
@@ -199,27 +198,30 @@ def tile_attend_gspos_ns_w_kernel(tc, x, wT, us, ts, wt, offs, poffs, out):
                 j = 2 * k + e
                 nc.scalar.activation(sig[h][:, j, :], scaled[:, e, :], SIGMOID, scale=us_col[:, j:j + 1])
 
-        def weigh(h, part):
-            nc.vector.tensor_tensor(g[h][:, PACK * part.start:PACK * part.stop].rearrange("p (c i j) -> p c j i", i=PACK, j=PACK),
-                                    sig[h][:, :, part].rearrange("p j (c i) -> p c j i", i=PACK),
-                                    factors[h][:, :, part].rearrange("p j (c i) -> p c j i", i=PACK), MULT)
+        def weigh(h, engine):
+            engine.tensor_tensor(g[h].rearrange("p (c i j) -> p c j i", i=PACK, j=PACK),
+                                 sig[h].rearrange("p j (c i) -> p c j i", i=PACK),
+                                 factors[h][:].rearrange("p j (c i) -> p c j i", i=PACK), MULT)
 
         def quantize_g(h):
             nc.vector.quantize_mx(out=g_codes[:, halves[h]].bitcast(E5M2X4), scales=g_scales[:, halves[h]], in_=g[h])
 
-        def product(t, slots, n, tag, copy):
-            name = "%d_%d" % (t, slots.start)
-            sums = flat(bank(n, "sums" + name))[:, 0:slots.stop - slots.start]
+        def product(t, h, n, copy):
+            name = "%d_%d" % (t, h)
+            sums = flat(bank(n, "sums" + name))[:, first_half]
             cols = slice(t * P, (t + 1) * P)
             nc.tensor.matmul_mx(out=sums,
                                 lhsT=x_r_codes[:, cols].bitcast(E4M3X4), lhsT_scale=x_r_scales[:, cols],
-                                rhs=g_codes[:, slots].bitcast(E5M2X4), rhs_scale=g_scales[:, slots], start=True, stop=True)
-            dn = sb.tile([P, slots.stop - slots.start], F32, name="dn" + name, tag="dn%d" % tag)
-            copy(dn[:], sums)
-            return dn
+                                rhs=g_codes[:, halves[h]].bitcast(E5M2X4), rhs_scale=g_scales[:, halves[h]],
+                                start=True, stop=True)
+            held = sb.tile([P, HALF], F32, name="dn" + name)
+            copy(held[:], sums)
+            dn[t, h] = held[:]
 
-        def scatter_negatives(t, h, dn):
-            nc.scalar.activation(window[t][:].indirect(entries(neg, halves[h])), dn, COPY)
+        dn = {}
+
+        def scatter_negatives(t, h):
+            nc.scalar.activation(window[t][:].indirect(entries(neg, halves[h])), dn[t, h], COPY)
 
         def scatter_positives(t, rows):
             nc.vector.tensor_tensor(window[t][:].indirect(entries(pos, rows)), xT[:, t, rows], gp_row[:, rows], MULT)
@@ -230,65 +232,72 @@ def tile_attend_gspos_ns_w_kernel(tc, x, wT, us, ts, wt, offs, poffs, out):
             nc.sync.dma_start(out=out_planes[t], in_=window[t][:])
 
         first_scores = scores(0)
-        wu = sb.tile([P, PACK], F32, name="wu")
+        wu = late.tile([P, PACK], F32, name="wu", offset=4 * T, align_bytes=64)
         minus_us_ts = sb.tile([P, PACK], F32, name="minus_us_ts")
         minus_wu_ts = sb.tile([P, PACK], F32, name="minus_wu_ts")
         nc.vector.tensor_tensor(wu[:], us_col[:], wt_col[:], MULT)
         nc.vector.scalar_tensor_tensor(minus_us_ts[:], turned_pos[:, :, P - 1], -1.0, uw_list[:, 0, :], MULT, MULT)
         factors = [sb.tile([P, PACK, HALF], F32, name="factors0")]
-        for j in range(PACK):
+        for j in range(last):
             nc.vector.tensor_scalar(factors[0][:, j, :], ts_all[:, first_half], wu[:, j:j + 1], None, MULT)
         nc.vector.tensor_tensor(minus_wu_ts[:], minus_us_ts[:], uw_list[:, 1, :], MULT)
         second_scores = scores(1)
         factors.append(sb.tile([P, PACK, HALF], F32, name="factors1", tag="w_d1", align_bytes=64))
-        for j in range(PACK):
+        for j in range(last):
             nc.gpsimd.tensor_scalar(factors[1][:, j, :], ts_all[:, second_half], wu[:, j:j + 1], 0.0, MULT, ADD)
         terms = sb.tile([P, PACK, P], F32, name="terms", tag="planes")
         minus_sp = sb.tile([P, PACK], F32, name="minus_sp")
         sig_p = sb.tile([P, PACK], F32, name="sig_p")
         gp = sb.tile([P, PACK], F32, name="gp")
-        spread_gp = [bank((2, 5)[h], "spread_gp%d" % h) for h in range(2)]
+        spread_gp = bank(2, "spread_gp")
         for b in range(PACK):
             nc.scalar.activation(terms[:, b, :], dots[:, b, :], COPY, scale=minus_us_ts[:, b:b + 1], accum_out=minus_sp[:, b:b + 1])
         nc.scalar.activation(sig_p[:], minus_sp[:], SIGMOID)
+        for h in range(2):
+            nc.scalar.activation(factors[h][:, last, :], ts_all[:, halves[h]], COPY, scale=wu[:, last:PACK])
+        window[2] = late.tile([P, T], F32, name="window2", offset=4 * T, align_bytes=64)
+        nc.gpsimd.memset(window[2][:].bitcast(I32), 0)
         nc.vector.tensor_tensor(gp[:], sig_p[:], minus_wu_ts[:], MULT)
         for b in range(PACK):
-            nc.tensor.transpose(spread_gp[b // 2][:, b % 2, :], gp[:, b:b + 1].to_broadcast([P, P]), ident[:])
+            nc.tensor.transpose(spread_gp[:, b, :], gp[:, b:b + 1].to_broadcast([P, P]), ident[:])
         for h, banks in enumerate((first_scores, second_scores)):
             for k in range(2):
                 squash(h, k, banks[k], 2 * h + k)
         opening = late.tile([P, HALF], F32, name="opening", offset=4 * T * 4 + 4 * HALF, align_bytes=64)
-        nc.vector.tensor_tensor(opening[:], flat(spread_gp[0])[:, 0:HALF], xT[:, 0, first_half], MULT)
+        nc.vector.tensor_tensor(opening[:], flat(spread_gp)[:, first_half], xT[:, 0, first_half], MULT)
         nc.scalar.activation(window[0][:].indirect(entries(pos, first_half)), opening[:], COPY)
-        weigh(0, first_half)
-        weigh(1, slice(0, EARLY))
+        weigh(0, nc.vector)
+        own = sb.tile([P, HALF], F32, name="own", tag="sig_first")
+        nc.vector.tensor_tensor(own[:], flat(spread_gp)[:, first_half], xT[:, 2, first_half], MULT)
         quantize_g(0)
-        first_dn = product(0, first_half, 4, 0, nc.scalar.copy)
-        nc.scalar.copy(gp_row[:, second_half], flat(spread_gp[1])[:, 0:HALF])
-        scatter_negatives(0, 0, first_dn[:])
-        weigh(1, slice(EARLY, HALF))
-        nc.vector.tensor_copy(gp_row[:, first_half], flat(spread_gp[0])[:, 0:HALF])
+        weigh(1, nc.gpsimd)
+        nc.vector.tensor_copy(window[2][:].indirect(entries(pos, first_half)), own[:])
+        product(0, 0, 4, nc.scalar.copy)
+        product(2, 0, 3, nc.scalar.copy)
+        nc.vector.tensor_copy(gp_row[:, 0:R - HELD], flat(spread_gp)[:, 0:R - HELD])
+        product(1, 0, 0, nc.vector.tensor_copy)
+        product(last, 0, 1, nc.vector.tensor_copy)
+        scatter_negatives(0, 0)
+        scatter_negatives(2, 0)
+        nc.vector.tensor_copy(gp_row[:, R - HELD:R], flat(spread_gp)[:, R - HELD:R])
         quantize_g(1)
-        window[last] = late.tile([P, T], F32, name="window3", offset=4 * T, align_bytes=64)
-        nc.gpsimd.memset(window[last][:].bitcast(I32), 0)
 
-        scatter_positives(2, everything)
-        second_dn = product(0, second_half, 3, 1, nc.scalar.copy)
-        dn = {2: product(2, everything, 0, 2, nc.scalar.copy)}
-        scatter_negatives(0, 1, second_dn[:])
-        dn[1] = product(1, everything, 1, 3, nc.vector.tensor_copy)
-        scatter_positives(1, first_half)
         scatter_positives(0, second_half)
-        for h in range(2):
-            scatter_negatives(2, h, dn[2][:, halves[h]])
-        store(2)
+        product(0, 1, 4, nc.scalar.copy)
+        scatter_positives(2, second_half)
+        product(2, 1, 3, nc.scalar.copy)
+        product(1, 1, 0, nc.vector.tensor_copy)
+        product(last, 1, 1, nc.vector.tensor_copy)
+        scatter_positives(1, second_half)
+        scatter_negatives(0, 1)
         store(0)
-        dn[last] = product(last, everything, 6, 2, nc.scalar.copy)
+        scatter_negatives(2, 1)
+        store(2)
         scatter_positives(last, everything)
         for h in range(2):
-            scatter_negatives(1, h, dn[1][:, halves[h]])
-        scatter_positives(1, second_half)
+            scatter_negatives(1, h)
+        scatter_positives(1, first_half)
         store(1)
         for h in range(2):
-            scatter_negatives(last, h, dn[last][:, halves[h]])
+            scatter_negatives(last, h)
         nc.scalar.dma_start(out=out_planes[last], in_=window[last][:])

@@ -206,7 +206,7 @@ def tile_attend_gspos_ns_w_kernel(tc, x, wT, us, ts, wt, offs, poffs, out):
         def quantize_g(h):
             nc.vector.quantize_mx(out=g_codes[:, halves[h]].bitcast(E5M2X4), scales=g_scales[:, halves[h]], in_=g[h])
 
-        def product(t, h, n, copy):
+        def product(t, h, n, copy, buffer):
             name = "%d_%d" % (t, h)
             sums = flat(bank(n, "sums" + name))[:, first_half]
             cols = slice(t * P, (t + 1) * P)
@@ -214,7 +214,7 @@ def tile_attend_gspos_ns_w_kernel(tc, x, wT, us, ts, wt, offs, poffs, out):
                                 lhsT=x_r_codes[:, cols].bitcast(E4M3X4), lhsT_scale=x_r_scales[:, cols],
                                 rhs=g_codes[:, halves[h]].bitcast(E5M2X4), rhs_scale=g_scales[:, halves[h]],
                                 start=True, stop=True)
-            held = sb.tile([P, HALF], F32, name="dn" + name)
+            held = sb.tile([P, HALF], F32, name="dn" + name, tag="dn%d" % buffer)
             copy(held[:], sums)
             dn[t, h] = held[:]
 
@@ -272,30 +272,30 @@ def tile_attend_gspos_ns_w_kernel(tc, x, wT, us, ts, wt, offs, poffs, out):
         quantize_g(0)
         weigh(1, nc.gpsimd)
         nc.vector.tensor_copy(window[2][:].indirect(entries(pos, first_half)), own[:])
-        product(0, 0, 4, nc.scalar.copy)
-        product(2, 0, 3, nc.scalar.copy)
+        product(0, 0, 4, nc.scalar.copy, 0)
+        product(2, 0, 3, nc.scalar.copy, 1)
         nc.vector.tensor_copy(gp_row[:, 0:R - HELD], flat(spread_gp)[:, 0:R - HELD])
-        product(1, 0, 0, nc.vector.tensor_copy)
-        product(last, 0, 1, nc.vector.tensor_copy)
+        product(1, 0, 0, nc.vector.tensor_copy, 2)
+        product(last, 0, 1, nc.vector.tensor_copy, 3)
         scatter_negatives(0, 0)
         scatter_negatives(2, 0)
+        scatter_negatives(1, 0)
         nc.vector.tensor_copy(gp_row[:, R - HELD:R], flat(spread_gp)[:, R - HELD:R])
         quantize_g(1)
 
         scatter_positives(0, second_half)
-        product(0, 1, 4, nc.scalar.copy)
+        product(0, 1, 4, nc.scalar.copy, 4)
+        product(2, 1, 3, nc.vector.tensor_copy, 5)
         scatter_positives(2, second_half)
-        product(2, 1, 3, nc.scalar.copy)
-        product(1, 1, 0, nc.vector.tensor_copy)
-        product(last, 1, 1, nc.vector.tensor_copy)
+        product(1, 1, 0, nc.vector.tensor_copy, 6)
         scatter_positives(1, second_half)
         scatter_negatives(0, 1)
         store(0)
         scatter_negatives(2, 1)
         store(2)
         scatter_positives(last, everything)
-        for h in range(2):
-            scatter_negatives(1, h)
+        scatter_negatives(1, 1)
+        product(last, 1, 1, nc.scalar.copy, 6)
         scatter_positives(1, first_half)
         store(1)
         for h in range(2):

from contextlib import ExitStack

import concourse.mybir as mybir

F32 = mybir.dt.float32
BF16 = mybir.dt.bfloat16
I32 = mybir.dt.int32
U32 = mybir.dt.uint32
U16 = mybir.dt.uint16
U8 = mybir.dt.uint8
E4M3X4 = mybir.dt.float8_e4m3fn_x4
E5M2X4 = mybir.dt.float8_e5m2_x4
MULT = mybir.AluOpType.mult
ADD = mybir.AluOpType.add
COPY = mybir.ActivationFunctionType.Copy
SIGMOID = mybir.ActivationFunctionType.Sigmoid

P = 128
PACK = 4
D = 512
R = 512
SLOTS = 512
T = 2048
HALF = SLOTS // 2
HELD = 32
MID = P // 2

FLOPS = 2 * R * D * SLOTS + 2 * D * R * SLOTS


def tile_attend_gspos_ns_w_kernel(tc, x, wT, us, ts, wt, offs, poffs, out):
    nc = tc.nc
    with ExitStack() as ctx:
        lists = ctx.enter_context(tc.tile_pool(name="lists", bufs=1))
        sb = ctx.enter_context(tc.tile_pool(name="sb", bufs=1))
        late = ctx.enter_context(tc.tile_pool(name="late", bufs=1))
        psum = ctx.enter_context(tc.psum_pool(name="psum", bufs=1))

        def bank(n, name):
            return psum.tile([P, PACK, P], F32, name=name, tag="bank%d" % n)

        def flat(tile):
            return tile[:].rearrange("p a b -> p (a b)")

        def entries(listed, part):
            return listed[:, part.start // 16:part.stop // 16]

        first_half, second_half, everything = slice(0, HALF), slice(HALF, R), slice(0, R)
        halves = (first_half, second_half)
        last = PACK - 1

        neg = lists.tile([P, SLOTS // 16], U16, name="neg")
        pos = lists.tile([P, R // 16], U16, name="pos")
        ts_row = sb.tile([P, T], F32, name="ts_row")
        x_sb = sb.tile([P, PACK * D], F32, name="x_sb")
        x_rows = x.rearrange("(s j) d -> s (j d)", j=PACK)
        nc.sync.dma_start(out=x_sb[:, 0:2 * D], in_=x_rows[:, 0:2 * D])
        nc.sync.dma_start(neg[:], offs)
        nc.sync.dma_start(pos[:], poffs)
        nc.sync.dma_start(out=ts_row[P - 1:P, :], in_=ts[0:1, :])
        nc.sync.dma_start(out=x_sb[:, 2 * D:PACK * D], in_=x_rows[:, 2 * D:PACK * D])

        ones = sb.tile([P, P], F32, name="ones", tag="ones")
        uw_rows = sb.tile([P, R], F32, name="uw_rows")
        nc.vector.memset(ones[:], 1.0)
        nc.vector.memset(ts_row[0:P - 1, :].bitcast(I32), 0)
        nc.vector.memset(uw_rows[0:MID - 2, :].bitcast(I32), 0)
        nc.vector.memset(uw_rows[MID:P, :].bitcast(I32), 0)
        ident = sb.tile([P, P], F32, name="ident")
        nc.gpsimd.affine_select(out=ident[:], in_=ones[:], compare_op=mybir.AluOpType.is_equal, fill=0.0, base=0,
                                pattern=[[-1, P]], channel_multiplier=1)
        table_warm_up = sb.tile([P, 1], F32, name="table_warm_up")
        nc.scalar.activation(table_warm_up[0:P // 2, :], ones[0:P // 2, 0:1], SIGMOID)
        window = {0: sb.tile([P, T], F32, name="window0", tag="ones")}
        nc.gpsimd.memset(window[0][:].bitcast(I32), 0)

        w_planes = wT.rearrange("(p t) c -> t p c", t=PACK)
        w = [sb.tile([P, T], F32, name="w%d" % t) for t in range(PACK)]
        nc.sync.dma_start(out=w[0][:], in_=w_planes[0])
        nc.sync.dma_start(out=uw_rows[MID - 2:MID - 1, :], in_=us.rearrange("r o -> o r"))
        nc.sync.dma_start(out=uw_rows[MID - 1:MID, :], in_=wt.rearrange("r o -> o r"))
        for t in range(1, PACK):
            nc.sync.dma_start(out=w[t][:], in_=w_planes[t])
        us_col = sb.tile([P, PACK], F32, name="us_col")
        wt_col = sb.tile([P, PACK], F32, name="wt_col")
        nc.sync.dma_start(out=us_col[:], in_=us.rearrange("(s j) o -> s (j o)", j=PACK))
        nc.sync.dma_start(out=wt_col[:], in_=wt.rearrange("(s j) o -> s (j o)", j=PACK))

        ts_neg_row = sb.tile([P, SLOTS], F32, name="ts_neg_row")
        ts_pos_row = sb.tile([P, R], F32, name="ts_pos_row")
        nc.scalar.activation(ts_neg_row[:], ts_row[:].indirect(neg[:]), COPY)
        nc.vector.tensor_copy(ts_pos_row[:], ts_row[:].indirect(pos[:]))

        x_r = late.tile([P, D * PACK], BF16, name="x_r", offset=0, align_bytes=64)
        nc.vector.tensor_copy(x_r[:].rearrange("p (t m j) -> p m j t", t=PACK, j=PACK),
                              x_sb[:].rearrange("p (j m t) -> p m j t", j=PACK, t=PACK))
        x_r_codes = sb.tile([P, D], U32, name="x_r_codes", align_bytes=64)
        x_r_scales = sb.tile([P, D], U8, name="x_r_scales", align_bytes=64)
        nc.vector.quantize_mx(out=x_r_codes[:].bitcast(E4M3X4), scales=x_r_scales[:], in_=x_r[:])
        window[1] = late.tile([P, T], F32, name="window1", offset=0, align_bytes=64)
        nc.gpsimd.memset(window[1][:].bitcast(I32), 0)

        x_planes = x_sb[:].rearrange("p (j m t) -> p j t m", j=PACK, t=PACK)
        xT = sb.tile([P, PACK, R], F32, name="xT")
        for t in range(PACK):
            turned_x = bank(4 + t % 2, "turned_x%d" % t)
            for j in range(PACK):
                nc.tensor.transpose(turned_x[:, j, :], x_planes[:, j, t, :], ident[:])
            nc.scalar.copy(xT[:, t, :].rearrange("p (s j) -> p s j", j=PACK), turned_x[:].rearrange("p j s -> p s j"))

        turned_neg = bank(4, "turned_neg")
        for b in range(PACK):
            nc.tensor.transpose(turned_neg[:, b, :], ts_neg_row[:, b * P:(b + 1) * P], ident[:])
        ts_neg = sb.tile([P, PACK], F32, name="ts_neg")
        nc.scalar.copy(ts_neg[:], turned_neg[:, :, P - 1])
        turned_uw = bank(5, "turned_uw")
        for b in range(PACK):
            nc.tensor.transpose(turned_uw[:, b, :], uw_rows[:, b * P:(b + 1) * P], ident[:])
        uw_list = sb.tile([P, 2, PACK], F32, name="uw_list")
        nc.scalar.copy(uw_list[:], turned_uw[:, :, MID - 2:MID].rearrange("p b v -> p v b"))
        spread_ts = bank(3, "spread_ts")
        for b in range(PACK):
            nc.tensor.transpose(spread_ts[:, b, :], ts_neg[:, b:b + 1].to_broadcast([P, P]), ident[:])
        turned_pos = bank(4, "turned_pos")
        for b in range(PACK):
            nc.tensor.transpose(turned_pos[:, b, :], ts_pos_row[:, b * P:(b + 1) * P], ident[:])
        ts_all = late.tile([P, SLOTS], F32, name="ts_all", offset=4 * T * 4, align_bytes=64)
        nc.scalar.copy(ts_all[:], flat(spread_ts))

        w_d = [sb.tile([P, HALF * PACK], BF16, name="w_d%d" % h, tag="w_d%d" % h, align_bytes=64) for h in range(2)]
        planes = sb.tile([P, PACK, SLOTS], BF16, name="planes", tag="planes")
        dots = bank(5, "dots")

        def gather_positives(t):
            if t == 2:
                prods = late.tile([P, R], F32, name="products2", offset=4 * T * 3, align_bytes=64)
            else:
                prods = sb.tile([P, R], F32, name="products%d" % t)
            nc.vector.tensor_tensor(prods[:], w[t][:].indirect(pos[:]), xT[:, t, :], MULT)
            for b in range(PACK):
                nc.tensor.matmul(dots[:, b, :], lhsT=prods[:, b * P:(b + 1) * P], rhs=ident[:], is_transpose=True,
                                 start=(t == 0 and b == 0), stop=(t == last and b == last))

        def gather_negatives(t, slots):
            nc.scalar.activation(planes[:, t, slots], w[t][:].indirect(entries(neg, slots)), COPY)

        def interleave(h, copy):
            copy(w_d[h][:].rearrange("p (c i t) -> p c t i", i=PACK, t=PACK),
                 planes[:, :, halves[h]].rearrange("p t (c i) -> p c t i", i=PACK))

        x_d = late.tile([P, R * PACK], BF16, name="x_d", offset=4 * T * 3 - 4 * R, align_bytes=64)
        x_d_codes = sb.tile([P, R], U32, name="x_d_codes", align_bytes=64)
        x_d_scales = sb.tile([P, R], U8, name="x_d_scales", align_bytes=64)

        gather_positives(0)
        gather_negatives(0, everything)
        gather_positives(1)
        gather_negatives(1, everything)
        nc.vector.tensor_copy(x_d[:].rearrange("p (j s t) -> p s j t", j=PACK, t=PACK),
                              xT[:].rearrange("p t (s j) -> p s j t", j=PACK))
        nc.vector.quantize_mx(out=x_d_codes[:].bitcast(E4M3X4), scales=x_d_scales[:], in_=x_d[:])
        window[last] = late.tile([P, T], F32, name="window3", offset=4 * T * 2, align_bytes=64)
        nc.gpsimd.memset(window[last][:].bitcast(I32), 0)
        gather_positives(2)
        gather_negatives(2, everything)
        gather_positives(last)
        for h in range(2):
            gather_negatives(last, halves[h])
        interleave(0, nc.vector.tensor_copy)
        interleave(1, nc.scalar.copy)

        w_d_codes = sb.tile([P, SLOTS], U32, name="w_d_codes", align_bytes=64)
        w_d_scales = sb.tile([P, SLOTS], U8, name="w_d_scales", align_bytes=64)
        g_codes = sb.tile([P, SLOTS], U32, name="g_codes", align_bytes=64)
        g_scales = sb.tile([P, SLOTS], U8, name="g_scales", align_bytes=64)
        sig_second = sb.tile([P, R - HELD + PACK * HALF], F32, name="sig_second")
        sig_first = sb.tile([P, PACK * HALF], F32, name="sig_first", tag="sig_first")
        sig = [part.rearrange("p (j i) -> p j i", j=PACK) for part in (sig_first[:], sig_second[:, R - HELD:])]
        gp_row = sig_second[:, 0:R]
        g = [late.tile([P, HALF * PACK], BF16, name="g%d" % h, offset=4 * T * 5, align_bytes=64)[:] for h in range(2)]

        def scores(h):
            nc.vector.quantize_mx(out=w_d_codes[:, halves[h]].bitcast(E4M3X4), scales=w_d_scales[:, halves[h]], in_=w_d[h][:])
            banks = [bank((0, 6)[h] + k, "scores%d_%d" % (h, k)) for k in range(2)]
            for j in range(PACK):
                rows = slice(j * P, (j + 1) * P)
                nc.tensor.matmul_mx(out=flat(banks[j // 2])[:, halves[j % 2]],
                                    lhsT=x_d_codes[:, rows].bitcast(E4M3X4), lhsT_scale=x_d_scales[:, rows],
                                    rhs=w_d_codes[:, halves[h]].bitcast(E4M3X4), rhs_scale=w_d_scales[:, halves[h]],
                                    start=True, stop=True)
            return banks

        def squash(h, k, scores_bank, tag):
            scaled = sb.tile([P, 2, HALF], F32, name="scaled%d_%d" % (h, k), tag="scaled%d" % tag)
            nc.vector.tensor_tensor(scaled[:], flat(scores_bank).rearrange("p (j i) -> p j i", j=2),
                                    ts_all[:, halves[h]].unsqueeze(1).to_broadcast([P, 2, HALF]), MULT)
            for e in range(2):
                j = 2 * k + e
                nc.scalar.activation(sig[h][:, j, :], scaled[:, e, :], SIGMOID, scale=us_col[:, j:j + 1])

        def weigh(h, engine):
            engine.tensor_tensor(g[h].rearrange("p (c i j) -> p c j i", i=PACK, j=PACK),
                                 sig[h].rearrange("p j (c i) -> p c j i", i=PACK),
                                 factors[h][:].rearrange("p j (c i) -> p c j i", i=PACK), MULT)

        def quantize_g(h):
            nc.vector.quantize_mx(out=g_codes[:, halves[h]].bitcast(E5M2X4), scales=g_scales[:, halves[h]], in_=g[h])

        def product(t, h, n, copy, buffer):
            name = "%d_%d" % (t, h)
            sums = flat(bank(n, "sums" + name))[:, first_half]
            cols = slice(t * P, (t + 1) * P)
            nc.tensor.matmul_mx(out=sums,
                                lhsT=x_r_codes[:, cols].bitcast(E4M3X4), lhsT_scale=x_r_scales[:, cols],
                                rhs=g_codes[:, halves[h]].bitcast(E5M2X4), rhs_scale=g_scales[:, halves[h]],
                                start=True, stop=True)
            held = sb.tile([P, HALF], F32, name="dn" + name, tag="dn%d" % buffer)
            copy(held[:], sums)
            dn[t, h] = held[:]

        dn = {}

        def scatter_negatives(t, h):
            nc.scalar.activation(window[t][:].indirect(entries(neg, halves[h])), dn[t, h], COPY)

        def scatter_positives(t, rows):
            nc.vector.tensor_tensor(window[t][:].indirect(entries(pos, rows)), xT[:, t, rows], gp_row[:, rows], MULT)

        out_planes = out.rearrange("(p t) c -> t p c", t=PACK)

        def store(t):
            nc.sync.dma_start(out=out_planes[t], in_=window[t][:])

        first_scores = scores(0)
        wu = late.tile([P, PACK], F32, name="wu", offset=4 * T, align_bytes=64)
        minus_us_ts = sb.tile([P, PACK], F32, name="minus_us_ts")
        minus_wu_ts = sb.tile([P, PACK], F32, name="minus_wu_ts")
        nc.vector.tensor_tensor(wu[:], us_col[:], wt_col[:], MULT)
        nc.vector.scalar_tensor_tensor(minus_us_ts[:], turned_pos[:, :, P - 1], -1.0, uw_list[:, 0, :], MULT, MULT)
        factors = [sb.tile([P, PACK, HALF], F32, name="factors0")]
        for j in range(last):
            nc.vector.tensor_scalar(factors[0][:, j, :], ts_all[:, first_half], wu[:, j:j + 1], None, MULT)
        nc.vector.tensor_tensor(minus_wu_ts[:], minus_us_ts[:], uw_list[:, 1, :], MULT)
        second_scores = scores(1)
        factors.append(sb.tile([P, PACK, HALF], F32, name="factors1", tag="w_d1", align_bytes=64))
        for j in range(last):
            nc.gpsimd.tensor_scalar(factors[1][:, j, :], ts_all[:, second_half], wu[:, j:j + 1], 0.0, MULT, ADD)
        terms = sb.tile([P, PACK, P], F32, name="terms", tag="planes")
        minus_sp = sb.tile([P, PACK], F32, name="minus_sp")
        sig_p = sb.tile([P, PACK], F32, name="sig_p")
        gp = sb.tile([P, PACK], F32, name="gp")
        spread_gp = bank(2, "spread_gp")
        for b in range(PACK):
            nc.scalar.activation(terms[:, b, :], dots[:, b, :], COPY, scale=minus_us_ts[:, b:b + 1], accum_out=minus_sp[:, b:b + 1])
        nc.scalar.activation(sig_p[:], minus_sp[:], SIGMOID)
        for h in range(2):
            nc.scalar.activation(factors[h][:, last, :], ts_all[:, halves[h]], COPY, scale=wu[:, last:PACK])
        window[2] = late.tile([P, T], F32, name="window2", offset=4 * T, align_bytes=64)
        nc.gpsimd.memset(window[2][:].bitcast(I32), 0)
        nc.vector.tensor_tensor(gp[:], sig_p[:], minus_wu_ts[:], MULT)
        for b in range(PACK):
            nc.tensor.transpose(spread_gp[:, b, :], gp[:, b:b + 1].to_broadcast([P, P]), ident[:])
        for h, banks in enumerate((first_scores, second_scores)):
            for k in range(2):
                squash(h, k, banks[k], 2 * h + k)
        opening = late.tile([P, HALF], F32, name="opening", offset=4 * T * 4 + 4 * HALF, align_bytes=64)
        nc.vector.tensor_tensor(opening[:], flat(spread_gp)[:, first_half], xT[:, 0, first_half], MULT)
        nc.scalar.activation(window[0][:].indirect(entries(pos, first_half)), opening[:], COPY)
        weigh(0, nc.vector)
        own = sb.tile([P, HALF], F32, name="own", tag="sig_first")
        nc.vector.tensor_tensor(own[:], flat(spread_gp)[:, first_half], xT[:, 2, first_half], MULT)
        quantize_g(0)
        weigh(1, nc.gpsimd)
        nc.vector.tensor_copy(window[2][:].indirect(entries(pos, first_half)), own[:])
        product(0, 0, 4, nc.scalar.copy, 0)
        product(2, 0, 3, nc.scalar.copy, 1)
        nc.vector.tensor_copy(gp_row[:, 0:R - HELD], flat(spread_gp)[:, 0:R - HELD])
        product(1, 0, 0, nc.vector.tensor_copy, 2)
        product(last, 0, 1, nc.vector.tensor_copy, 3)
        scatter_negatives(0, 0)
        scatter_negatives(2, 0)
        scatter_negatives(1, 0)
        nc.vector.tensor_copy(gp_row[:, R - HELD:R], flat(spread_gp)[:, R - HELD:R])
        quantize_g(1)

        scatter_positives(0, second_half)
        product(0, 1, 4, nc.scalar.copy, 4)
        product(2, 1, 3, nc.vector.tensor_copy, 5)
        scatter_positives(2, second_half)
        product(1, 1, 0, nc.vector.tensor_copy, 6)
        scatter_positives(1, second_half)
        scatter_negatives(0, 1)
        store(0)
        scatter_negatives(2, 1)
        store(2)
        scatter_positives(last, everything)
        scatter_negatives(1, 1)
        product(last, 1, 1, nc.scalar.copy, 6)
        scatter_positives(1, first_half)
        store(1)
        for h in range(2):
            scatter_negatives(last, h)
        nc.scalar.dma_start(out=out_planes[last], in_=window[last][:])
